import numpy as np
import ml_dtypes


def mxq(x, axis, fmt="e4m3"):
    dtype, down = {"e4m3": (ml_dtypes.float8_e4m3fn, 7), "e5m2": (ml_dtypes.float8_e5m2, 14)}[fmt]
    v = np.moveaxis(np.asarray(x, np.float32).astype(ml_dtypes.bfloat16).astype(np.float64), axis, -1)
    blocks = v.reshape(v.shape[:-1] + (-1, 32))
    amax = np.abs(blocks).max(-1, keepdims=True)
    byte = np.maximum(np.where(amax > 0, np.frexp(amax)[1] - 1 + 127, 0) - down, 1)
    scale = np.exp2(byte - 127.0)
    codes = (blocks / scale).astype(np.float32).astype(dtype).astype(np.float64)
    return np.moveaxis((codes * scale).reshape(v.shape), -1, axis)


WIDE = False


def mx_kscale(k):
    if not WIDE:
        return np.ones(k)
    levels = np.array([10, -10, 5, -5, 0])
    if k % 512:
        return np.exp2(np.random.permutation(np.resize(levels, k // 32))).repeat(32)
    a = np.empty((k // 512, 16))
    for p in range(k // 512):
        a[p, :8] = np.random.permutation(np.resize(levels, 8))
        for g in range(8):
            far = levels[np.abs(levels - a[p, g]) >= 10]
            a[p, g + 8] = far[np.random.randint(len(far))]
    return np.exp2(a.ravel()).repeat(32)


def f64(x):
    return np.asarray(x).astype(np.float64)


def striped(idx):
    return np.tile(idx.reshape(-1, 16).T, (8, 1)).astype(np.uint16)


def unstriped(offs):
    return offs[:16].T.reshape(-1).astype(np.int64)


def pack_weight(w):
    k, n = w.shape
    w = f64(np.asarray(w, np.float32).astype(ml_dtypes.bfloat16)).reshape(k // 32, 32, n)
    amax = np.abs(w).max(1)
    byte = np.clip(np.where(amax > 0, np.frexp(amax)[1] - 1 + 127 - 7, 1), 1, 254)
    scaled = (w * np.exp2(127.0 - byte)[:, None, :]).reshape(k, n).astype(np.float32)
    words = np.ascontiguousarray(scaled.reshape(k // 512, 128, 4, n).transpose(0, 1, 3, 2)).astype(ml_dtypes.float8_e4m3fn).view(np.uint8)
    return words, np.ascontiguousarray(byte.astype(np.uint8).reshape(k // 512, 16, n))


def unpack_weight(words, scales):
    g, p, n, _ = words.shape
    vals = np.ascontiguousarray(words).view(ml_dtypes.float8_e4m3fn).astype(np.float64) * np.repeat(np.exp2(scales.astype(np.float64) - 127.0), 8, axis=1)[..., None]
    return vals.transpose(0, 1, 3, 2).reshape(g * 512, n)


def planes(y):
    n, m = y.shape
    v = y.astype(np.float32).astype(ml_dtypes.bfloat16).astype(np.float64).reshape(n // 32, 32, m)
    top = np.abs(v).max(1)
    byte = np.clip(np.where(top > 0, np.frexp(top)[1] - 1 + 127 - 7, 1), 1, 254)
    codes = (v * np.exp2(127.0 - byte)[:, None, :]).reshape(n, m).astype(np.float32).astype(ml_dtypes.float8_e4m3fn).view(np.uint8)
    words = codes.reshape(n // 512, 128, 4, m).transpose(0, 1, 3, 2)
    return np.ascontiguousarray(words), np.ascontiguousarray(byte.astype(np.uint8).reshape(n // 512, 16, m))


K, T, S, N, V, W = 512, 4096, 1024, 512, 512, 1024


def setup_inputs():
    n = np.random.standard_normal
    s = mx_kscale(K)[:, None]
    c = mx_kscale(S)
    packed_xT = pack_weight(n((K, T)) * s)
    packed_eT = pack_weight(n((K, W)) / np.sqrt(K) / s)
    return {
        "x_words": packed_xT[0],
        "x_scales": packed_xT[1],
        "e_words": packed_eT[0],
        "e_scales": packed_eT[1],
        "mask": (np.random.uniform(0.3, 1.0, (S, 1)) * c[:, None]).astype(np.float32),
        "wv": (n((K, N)) / np.sqrt(K) / s).astype(np.float32),
        "inv": (np.random.uniform(0.6, 1.4, (S, 1)) / c[:, None]).astype(np.float32),
        "offs": striped(np.random.permutation(T)[:S]),
        "slot": striped(np.random.permutation(W)[:V]),
    }


def reference(x_words, x_scales, e_words, e_scales, mask, wv, inv, offs, slot):
    xq = unpack_weight(x_words, x_scales)[:, unstriped(offs)]
    wvq = mxq(f64(wv), 0, "e4m3")
    h = f64(inv) * (xq.T @ wvq)
    e_slot = unpack_weight(e_words, e_scales)[:, unstriped(slot)]
    y = xq.T @ e_slot
    ex = np.exp(y - y.max(axis=1, keepdims=True))
    p = ex / ex.sum(axis=1, keepdims=True)
    a = f64(mask) * p
    out_0 = mxq(h, 0, "e4m3").T @ mxq(a, 0, "e4m3")
    return (out_0,) + planes(out_0)

@@ -1,0 +1,239 @@
+from contextlib import ExitStack
+
+import concourse.mybir as mybir
+
+K, T, S, N, V, W = 512, 4096, 1024, 512, 512, 1024
+FLOPS = 2 * (S * K * N + S * K * V + S * N * V)
+
+F32 = mybir.dt.float32
+BF16 = mybir.dt.bfloat16
+I32 = mybir.dt.int32
+U32 = mybir.dt.uint32
+U16 = mybir.dt.uint16
+U8 = mybir.dt.uint8
+FP8X4 = mybir.dt.float8_e4m3fn_x4
+ACT = mybir.ActivationFunctionType
+ALU = mybir.AluOpType
+AX = mybir.AxisListType
+
+P = 128
+PACK = 4
+PASS = P * PACK
+PASSES = S // PASS
+QUADS = 4
+CHUNK = 128
+CHUNKS = V // CHUNK
+ROW0, ROW_STEP = 4, 8
+
+
+def weave_out(tile_ap):
+    return tile_ap.rearrange("p (c i j) -> p c j i", i=2, j=PACK)
+
+
+def weave_in(planes_ap):
+    return planes_ap.rearrange("p j (c i) -> p c j i", i=2)
+
+
+def spread(factor_ap, columns):
+    return factor_ap.unsqueeze(1).unsqueeze(3).to_broadcast([P, columns // 2, PACK, 2])
+
+
+def tile_picked_yslot_soft_po_kernel(tc, x_words, x_scales, e_words, e_scales, mask, wv, inv, offs, slot, out_0, out_1, out_2):
+    nc = tc.nc
+    with ExitStack() as ctx:
+        lists = ctx.enter_context(tc.tile_pool(name="lists", bufs=1))
+        sb = ctx.enter_context(tc.tile_pool(name="sb", bufs=1))
+        psum = ctx.enter_context(tc.psum_pool(name="psum", bufs=1))
+
+        def tile(name, shape, dtype, tag=None):
+            return sb.tile(shape, dtype, name=name, tag=tag or name, align_bytes=64)
+
+        def bank(b, shape, name):
+            return psum.tile(shape, F32, name=name, tag=f"bank{b}")
+
+        offs_t = lists.tile([P, S // 16], U16, name="offs_t")
+        slot_t = lists.tile([P, V // 16], U16, name="slot_t")
+        xw = tile("xw", [P, T], I32)
+        ew = tile("ew", [P, W], I32)
+        xs = tile("xs", [P, T], U8)
+        es = tile("es", [P, W], U8)
+        placed = [tile("placed0", [P, PASS + V], U8), tile("placed1", [P, PASS], U8)]
+        wv_raw = tile("wv_raw", [P, PACK, N], F32, "wide")
+        inv_t = tile("inv_t", [P, PASSES, PACK], F32)
+        mask_t = tile("mask_t", [P, PASSES, PACK], F32)
+
+        nc.gpsimd.memset(xs[:, : T // 2].bitcast(I32), 0)
+        nc.vector.memset(xs[:, T // 2 :].bitcast(I32), 0)
+        nc.gpsimd.memset(es[:].bitcast(I32), 0)
+        for g in range(PASSES):
+            nc.vector.memset(placed[g][:].bitcast(I32), 0)
+        nc.sync.dma_start(ew[:], e_words[0].rearrange("p n t -> p (n t)").bitcast(I32))
+        nc.sync.dma_start(offs_t[:], offs)
+        nc.sync.dma_start(xs[ROW0:P:ROW_STEP, :].bitcast(I32), x_scales[0].bitcast(I32))
+        nc.sync.dma_start(slot_t[:], slot)
+        nc.sync.dma_start(es[ROW0:P:ROW_STEP, :].bitcast(I32), e_scales[0].bitcast(I32))
+        nc.sync.dma_start(mask_t[:], mask.rearrange("(g p j) o -> p g (j o)", p=P, j=PACK))
+        nc.sync.dma_start(inv_t[:], inv.rearrange("(g p j) o -> p g (j o)", p=P, j=PACK))
+        nc.sync.dma_start(xw[:], x_words[0].rearrange("p n t -> p (n t)").bitcast(I32))
+        nc.sync.dma_start(wv_raw[:], wv.rearrange("(p k) m -> p k m", k=PACK))
+
+        e_picked = tile("e_picked", [P, V], U8, "slots")
+        x_picked = [tile(f"x_picked{g}", [P, PASS], U8) for g in range(PASSES)]
+        staged = [tile("staged0", [P, PASS + V], U8), tile("staged1", [P, PASS], U8)]
+        x_bytes = [placed[g][:, :PASS].rearrange("p (j n) -> p j n", j=PACK) for g in range(PASSES)]
+        e_bytes = placed[0][:, PASS:]
+        x_codes = [tile(f"x_codes{g}", [P, PACK, P], U32) for g in range(PASSES)]
+
+        def entries(g):
+            return offs_t[:, g * PASS // 16 : (g + 1) * PASS // 16]
+
+        def deal_bytes(g):
+            nc.vector.tensor_copy(
+                staged[g][:, :PASS].rearrange("p (j n) -> p j n", j=PACK),
+                x_picked[g][:].rearrange("p (n j) -> p j n", j=PACK),
+            )
+
+        def place_bytes(g, queue):
+            for q in range(QUADS):
+                queue.dma_start(
+                    placed[g][32 * q : 32 * q + 4, :].bitcast(I32),
+                    staged[g][32 * q + ROW0 : 32 * (q + 1) : ROW_STEP, :].bitcast(I32),
+                )
+
+        nc.vector.tensor_copy(x_picked[0][:], xs[:].indirect(entries(0)))
+        nc.vector.tensor_copy(e_picked[:], es[:].indirect(slot_t[:]))
+        deal_bytes(0)
+        nc.vector.tensor_copy(staged[0][:, PASS:].bitcast(I32), e_picked[:].bitcast(I32))
+        place_bytes(0, nc.scalar)
+        e_codes = tile("e_codes", [P, V], U32, "slots")
+        nc.vector.tensor_copy(e_codes[:], ew[:].bitcast(U32).indirect(slot_t[:]))
+        nc.vector.tensor_copy(x_picked[1][:], xs[:].indirect(entries(1)))
+
+        neg_max = tile("neg_max", [P, PASSES, PACK], F32)
+        total = tile("total", [P, PASSES, PACK], F32)
+        share = tile("share", [P, PASSES, PACK], F32)
+        weight = tile("weight", [P, PASSES, PACK], F32)
+
+        def scores(g):
+            for j in range(PACK):
+                y = bank(PACK * g + j, [P, V], f"y{g}{j}")
+                nc.tensor.matmul_mx(
+                    out=y[:], lhsT=x_codes[g][:, j, :].bitcast(FP8X4), lhsT_scale=x_bytes[g][:, j, :],
+                    rhs=e_codes[:].bitcast(FP8X4), rhs_scale=e_bytes, start=True, stop=True,
+                )
+                nc.vector.tensor_reduce(neg_max[:, g, j : j + 1], y[:], AX.X, ALU.max, negate=True)
+                nc.scalar.activation(
+                    ex[g][:, j, :], y[:], ACT.Exp, bias=neg_max[:, g, j : j + 1], accum_out=total[:, g, j : j + 1]
+                )
+
+        def pick_words(g):
+            nc.vector.tensor_copy(x_codes[g][:].rearrange("p j n -> p n j"), xw[:].bitcast(U32).indirect(entries(g)))
+
+        def weights(g):
+            nc.vector.reciprocal(share[:, g, :], total[:, g, :])
+            nc.vector.tensor_tensor(weight[:, g, :], share[:, g, :], mask_t[:, g, :], ALU.mult)
+
+        wv_bf = tile("wv_bf", [P, N * PACK], BF16)
+        wv_codes = tile("wv_codes", [P, N], U32)
+        wv_bytes = tile("wv_bytes", [P, N], U8)
+        a_bf = [tile(f"a_bf{g}", [P, V * PACK], BF16) for g in range(PASSES)]
+        a_codes = [tile(f"a_codes{g}", [P, V], U32) for g in range(PASSES)]
+        a_bytes = [tile(f"a_bytes{g}", [P, V], U8) for g in range(PASSES)]
+        h_bf = [tile(f"h_bf{g}", [P, N * PACK], BF16) for g in range(PASSES)]
+        h_codes = [tile(f"h_codes{g}", [P, N], U32) for g in range(PASSES)]
+        h_bytes = [tile(f"h_bytes{g}", [P, N], U8) for g in range(PASSES)]
+        h_planes = tile("h_planes", [P, PACK, N], BF16)
+
+        nc.scalar.copy(
+            wv_bf[:].rearrange("p (j m k) -> p m k j", j=PACK, k=PACK),
+            wv_raw[:].rearrange("p k (m j) -> p m k j", j=PACK),
+        )
+        ex = [tile("ex0", [P, PACK, V], F32, "wide"), tile("ex1", [P, PACK, V], F32)]
+        pick_words(0)
+        deal_bytes(1)
+        place_bytes(1, nc.sync)
+        pick_words(1)
+        scores(0)
+        nc.vector.quantize_mx(wv_codes[:].bitcast(FP8X4), wv_bytes[:], wv_bf[:])
+        scores(1)
+        weights(0)
+        nc.vector.tensor_tensor(weave_out(a_bf[0][:]), weave_in(ex[0][:]), spread(weight[:, 0, :], V), ALU.mult)
+
+        h0 = [bank(c, [P, PACK, CHUNK], f"h0{c}") for c in range(CHUNKS)]
+        for c in range(CHUNKS):
+            cols = slice(c * CHUNK, (c + 1) * CHUNK)
+            for j in range(PACK):
+                nc.tensor.matmul_mx(
+                    out=h0[c][:, j, :], lhsT=x_codes[0][:, j, :].bitcast(FP8X4), lhsT_scale=x_bytes[0][:, j, :],
+                    rhs=wv_codes[:, cols].bitcast(FP8X4), rhs_scale=wv_bytes[:, cols], start=True, stop=True,
+                )
+        for j in range(PACK):
+            h1 = bank(PACK + j, [P, N], f"h1{j}")
+            nc.tensor.matmul_mx(
+                out=h1[:], lhsT=x_codes[1][:, j, :].bitcast(FP8X4), lhsT_scale=x_bytes[1][:, j, :],
+                rhs=wv_codes[:].bitcast(FP8X4), rhs_scale=wv_bytes[:], start=True, stop=True,
+            )
+            nc.scalar.activation(h_planes[:, j, :], h1[:], ACT.Copy, scale=inv_t[:, 1, j : j + 1])
+        nc.scalar.copy(weave_out(h_bf[1][:]), weave_in(h_planes[:]))
+
+        for c in range(CHUNKS):
+            wide = slice(c * CHUNK * PACK, (c + 1) * CHUNK * PACK)
+            nc.vector.tensor_tensor(weave_out(h_bf[0][:, wide]), weave_in(h0[c][:]), spread(inv_t[:, 0, :], CHUNK), ALU.mult)
+            if c == 0:
+                nc.vector.quantize_mx(a_codes[0][:].bitcast(FP8X4), a_bytes[0][:], a_bf[0][:])
+                weights(1)
+
+        out_codes = tile("out_codes", [P, V], U32)
+        out_bytes = tile("out_bytes", [P, V], U8)
+        out_bf = [tile(f"out_bf{c}", [P, CHUNK * PACK], BF16) for c in range(CHUNKS)]
+        out_f = [tile(f"out_f{c}", [P, PACK, CHUNK], F32) for c in range(CHUNKS)]
+
+        def weigh(c):
+            cols = slice(c * CHUNK, (c + 1) * CHUNK)
+            wide = slice(c * CHUNK * PACK, (c + 1) * CHUNK * PACK)
+            nc.vector.tensor_tensor(weave_out(a_bf[1][:, wide]), weave_in(ex[1][:, :, cols]), spread(weight[:, 1, :], CHUNK), ALU.mult)
+
+        def quant_a(c):
+            cols = slice(c * CHUNK, (c + 1) * CHUNK)
+            wide = slice(c * CHUNK * PACK, (c + 1) * CHUNK * PACK)
+            nc.vector.quantize_mx(a_codes[1][:, cols].bitcast(FP8X4), a_bytes[1][:, cols], a_bf[1][:, wide])
+
+        def product(c):
+            cols = slice(c * CHUNK, (c + 1) * CHUNK)
+            acc = bank(c, [P, PACK, CHUNK], f"acc{c}")
+            for j in range(PACK):
+                rows = slice(j * P, (j + 1) * P)
+                for g in range(PASSES):
+                    nc.tensor.matmul_mx(
+                        out=acc[:, j, :], lhsT=h_codes[g][:, rows].bitcast(FP8X4), lhsT_scale=h_bytes[g][:, rows],
+                        rhs=a_codes[g][:, cols].bitcast(FP8X4), rhs_scale=a_bytes[g][:, cols],
+                        start=(g == 0), stop=(g == PASSES - 1),
+                    )
+            nc.scalar.copy(out_f[c][:], acc[:])
+            nc.sync.dma_start(out_0.rearrange("(p j) v -> p j v", j=PACK)[:, :, cols], out_f[c][:])
+
+        def planes(c):
+            cols = slice(c * CHUNK, (c + 1) * CHUNK)
+            nc.vector.tensor_copy(weave_out(out_bf[c][:]), weave_in(out_f[c][:]))
+            nc.vector.quantize_mx(out_codes[:, cols].bitcast(FP8X4), out_bytes[:, cols], out_bf[c][:])
+            nc.sync.dma_start(out_1[0].rearrange("p n t -> p (n t)").bitcast(I32)[:, cols], out_codes[:, cols].bitcast(I32))
+
+        weigh(0)
+        nc.vector.quantize_mx(h_codes[0][:].bitcast(FP8X4), h_bytes[0][:], h_bf[0][:])
+        weigh(1)
+        nc.vector.quantize_mx(h_codes[1][:].bitcast(FP8X4), h_bytes[1][:], h_bf[1][:])
+        quant_a(0)
+        product(0)
+        weigh(2)
+        quant_a(1)
+        product(1)
+        weigh(3)
+        quant_a(2)
+        product(2)
+        quant_a(3)
+        product(3)
+        for c in range(CHUNKS):
+            planes(c)
+        for q in range(QUADS):
+            queue = nc.sync if q % 2 == 0 else nc.scalar
+            queue.dma_start(out_2[0, 4 * q : 4 * q + 4, :].bitcast(I32), out_bytes[32 * q : 32 * q + 4, :].bitcast(I32))

@@ -54,31 +54,34 @@ def tile_picked_yslot_soft_po_kernel(tc, x_words, x_scales, e_words, e_scales, m
         offs_t = lists.tile([P, S // 16], U16, name="offs_t")
         slot_t = lists.tile([P, V // 16], U16, name="slot_t")
         xw = tile("xw", [P, T], I32)
-        ew = tile("ew", [P, W], I32)
+        ew = tile("ew", [P, W], I32, "wide1")
         xs = tile("xs", [P, T], U8)
         es = tile("es", [P, W], U8)
         placed = [tile("placed0", [P, PASS + V], U8), tile("placed1", [P, PASS], U8)]
-        wv_raw = tile("wv_raw", [P, PACK, N], F32, "wide")
         inv_t = tile("inv_t", [P, PASSES, PACK], F32)
         mask_t = tile("mask_t", [P, PASSES, PACK], F32)
 
-        nc.gpsimd.memset(xs[:, : T // 2].bitcast(I32), 0)
-        nc.vector.memset(xs[:, T // 2 :].bitcast(I32), 0)
         nc.gpsimd.memset(es[:].bitcast(I32), 0)
+        nc.gpsimd.memset(xs[:, : T // 4].bitcast(I32), 0)
+        nc.vector.memset(xs[:, T // 4 :].bitcast(I32), 0)
         for g in range(PASSES):
-            nc.vector.memset(placed[g][:].bitcast(I32), 0)
-        nc.sync.dma_start(ew[:], e_words[0].rearrange("p n t -> p (n t)").bitcast(I32))
-        nc.sync.dma_start(offs_t[:], offs)
-        nc.sync.dma_start(xs[ROW0:P:ROW_STEP, :].bitcast(I32), x_scales[0].bitcast(I32))
+            nc.gpsimd.memset(placed[g][:].bitcast(I32), 0)
         nc.sync.dma_start(slot_t[:], slot)
         nc.sync.dma_start(es[ROW0:P:ROW_STEP, :].bitcast(I32), e_scales[0].bitcast(I32))
-        nc.sync.dma_start(mask_t[:], mask.rearrange("(g p j) o -> p g (j o)", p=P, j=PACK))
-        nc.sync.dma_start(inv_t[:], inv.rearrange("(g p j) o -> p g (j o)", p=P, j=PACK))
+        nc.sync.dma_start(offs_t[:], offs)
+        nc.sync.dma_start(xs[ROW0:P:ROW_STEP, :].bitcast(I32), x_scales[0].bitcast(I32))
+        nc.sync.dma_start(ew[:], e_words[0].rearrange("p n t -> p (n t)").bitcast(I32))
+        nc.gpsimd.dma_start(mask_t[:], mask.rearrange("(g p j) o -> p g (j o)", p=P, j=PACK))
+        nc.gpsimd.dma_start(inv_t[:], inv.rearrange("(g p j) o -> p g (j o)", p=P, j=PACK))
         nc.sync.dma_start(xw[:], x_words[0].rearrange("p n t -> p (n t)").bitcast(I32))
-        nc.sync.dma_start(wv_raw[:], wv.rearrange("(p k) m -> p k m", k=PACK))
+
+        def load_wv(half):
+            raw = tile(f"wv_raw{half}", [P, PACK, N // 2], F32, f"wide{half}")
+            nc.sync.dma_start(raw[:], wv.rearrange("(p k) m -> p k m", k=PACK)[:, :, half * N // 2 : (half + 1) * N // 2])
+            return raw
+
 
         e_picked = tile("e_picked", [P, V], U8, "slots")
-        x_picked = [tile(f"x_picked{g}", [P, PASS], U8) for g in range(PASSES)]
         staged = [tile("staged0", [P, PASS + V], U8), tile("staged1", [P, PASS], U8)]
         x_bytes = [placed[g][:, :PASS].rearrange("p (j n) -> p j n", j=PACK) for g in range(PASSES)]
         e_bytes = placed[0][:, PASS:]
@@ -93,21 +96,27 @@ def tile_picked_yslot_soft_po_kernel(tc, x_words, x_scales, e_words, e_scales, m
                 x_picked[g][:].rearrange("p (n j) -> p j n", j=PACK),
             )
 
-        def place_bytes(g, queue):
+        def place_bytes(g):
             for q in range(QUADS):
-                queue.dma_start(
+                nc.sync.dma_start(
                     placed[g][32 * q : 32 * q + 4, :].bitcast(I32),
                     staged[g][32 * q + ROW0 : 32 * (q + 1) : ROW_STEP, :].bitcast(I32),
                 )
 
-        nc.vector.tensor_copy(x_picked[0][:], xs[:].indirect(entries(0)))
+        x_picked = [tile("x_picked0", [P, PASS], U8, "wide0")]
         nc.vector.tensor_copy(e_picked[:], es[:].indirect(slot_t[:]))
+        nc.vector.tensor_copy(x_picked[0][:], xs[:].indirect(entries(0)))
         deal_bytes(0)
         nc.vector.tensor_copy(staged[0][:, PASS:].bitcast(I32), e_picked[:].bitcast(I32))
-        place_bytes(0, nc.scalar)
+        place_bytes(0)
+        wv_raw = [load_wv(0)]
         e_codes = tile("e_codes", [P, V], U32, "slots")
         nc.vector.tensor_copy(e_codes[:], ew[:].bitcast(U32).indirect(slot_t[:]))
+        x_picked.append(tile("x_picked1", [P, PASS], U8, "wide1"))
         nc.vector.tensor_copy(x_picked[1][:], xs[:].indirect(entries(1)))
+        deal_bytes(1)
+        wv_raw.append(load_wv(1))
+        place_bytes(1)
 
         neg_max = tile("neg_max", [P, PASSES, PACK], F32)
         total = tile("total", [P, PASSES, PACK], F32)
@@ -136,28 +145,27 @@ def tile_picked_yslot_soft_po_kernel(tc, x_words, x_scales, e_words, e_scales, m
         wv_bf = tile("wv_bf", [P, N * PACK], BF16)
         wv_codes = tile("wv_codes", [P, N], U32)
         wv_bytes = tile("wv_bytes", [P, N], U8)
-        a_bf = [tile(f"a_bf{g}", [P, V * PACK], BF16) for g in range(PASSES)]
-        a_codes = [tile(f"a_codes{g}", [P, V], U32) for g in range(PASSES)]
-        a_bytes = [tile(f"a_bytes{g}", [P, V], U8) for g in range(PASSES)]
+        a_bf = [tile(f"a_bf{c}", [P, PASSES, CHUNK * PACK], BF16) for c in range(CHUNKS)]
+        a_codes = [tile(f"a_codes{c}", [P, PASSES, CHUNK], U32) for c in range(CHUNKS)]
+        a_bytes = [tile(f"a_bytes{c}", [P, PASSES, CHUNK], U8) for c in range(CHUNKS)]
+        a_planes = tile("a_planes", [P, PACK, V // 2], BF16)
         h_bf = [tile(f"h_bf{g}", [P, N * PACK], BF16) for g in range(PASSES)]
         h_codes = [tile(f"h_codes{g}", [P, N], U32) for g in range(PASSES)]
         h_bytes = [tile(f"h_bytes{g}", [P, N], U8) for g in range(PASSES)]
         h_planes = tile("h_planes", [P, PACK, N], BF16)
 
-        nc.scalar.copy(
-            wv_bf[:].rearrange("p (j m k) -> p m k j", j=PACK, k=PACK),
-            wv_raw[:].rearrange("p k (m j) -> p m k j", j=PACK),
-        )
-        ex = [tile("ex0", [P, PACK, V], F32, "wide"), tile("ex1", [P, PACK, V], F32)]
+        for half in range(2):
+            nc.scalar.copy(
+                wv_bf[:].rearrange("p (j m k) -> p m k j", j=PACK, k=PACK)[:, half * P // 2 : (half + 1) * P // 2],
+                wv_raw[half][:].rearrange("p k (m j) -> p m k j", j=PACK),
+            )
+        ex = [tile(f"ex{g}", [P, PACK, V], F32, f"wide{g}") for g in range(PASSES)]
         pick_words(0)
-        deal_bytes(1)
-        place_bytes(1, nc.sync)
         pick_words(1)
         scores(0)
         nc.vector.quantize_mx(wv_codes[:].bitcast(FP8X4), wv_bytes[:], wv_bf[:])
-        scores(1)
         weights(0)
-        nc.vector.tensor_tensor(weave_out(a_bf[0][:]), weave_in(ex[0][:]), spread(weight[:, 0, :], V), ALU.mult)
+        scores(1)
 
         h0 = [bank(c, [P, PACK, CHUNK], f"h0{c}") for c in range(CHUNKS)]
         for c in range(CHUNKS):
@@ -175,41 +183,53 @@ def tile_picked_yslot_soft_po_kernel(tc, x_words, x_scales, e_words, e_scales, m
             )
             nc.scalar.activation(h_planes[:, j, :], h1[:], ACT.Copy, scale=inv_t[:, 1, j : j + 1])
         nc.scalar.copy(weave_out(h_bf[1][:]), weave_in(h_planes[:]))
+        for j in range(PACK):
+            nc.scalar.activation(a_planes[:, j, :], ex[0][:, j, V // 2 :], ACT.Copy, scale=weight[:, 0, j : j + 1])
+        for c in range(CHUNKS // 2, CHUNKS):
+            first = c * CHUNK - V // 2
+            nc.scalar.copy(weave_out(a_bf[c][:, 0, :]), weave_in(a_planes[:, :, first : first + CHUNK]))
 
         for c in range(CHUNKS):
             wide = slice(c * CHUNK * PACK, (c + 1) * CHUNK * PACK)
             nc.vector.tensor_tensor(weave_out(h_bf[0][:, wide]), weave_in(h0[c][:]), spread(inv_t[:, 0, :], CHUNK), ALU.mult)
-            if c == 0:
-                nc.vector.quantize_mx(a_codes[0][:].bitcast(FP8X4), a_bytes[0][:], a_bf[0][:])
-                weights(1)
+        weights(1)
 
         out_codes = tile("out_codes", [P, V], U32)
         out_bytes = tile("out_bytes", [P, V], U8)
         out_bf = [tile(f"out_bf{c}", [P, CHUNK * PACK], BF16) for c in range(CHUNKS)]
         out_f = [tile(f"out_f{c}", [P, PACK, CHUNK], F32) for c in range(CHUNKS)]
 
-        def weigh(c):
+        def weigh(g, c):
             cols = slice(c * CHUNK, (c + 1) * CHUNK)
-            wide = slice(c * CHUNK * PACK, (c + 1) * CHUNK * PACK)
-            nc.vector.tensor_tensor(weave_out(a_bf[1][:, wide]), weave_in(ex[1][:, :, cols]), spread(weight[:, 1, :], CHUNK), ALU.mult)
+            nc.vector.tensor_tensor(weave_out(a_bf[c][:, g, :]), weave_in(ex[g][:, :, cols]), spread(weight[:, g, :], CHUNK), ALU.mult)
 
         def quant_a(c):
-            cols = slice(c * CHUNK, (c + 1) * CHUNK)
-            wide = slice(c * CHUNK * PACK, (c + 1) * CHUNK * PACK)
-            nc.vector.quantize_mx(a_codes[1][:, cols].bitcast(FP8X4), a_bytes[1][:, cols], a_bf[1][:, wide])
+            nc.vector.quantize_mx(
+                a_codes[c][:].rearrange("p g n -> p (g n)").bitcast(FP8X4),
+                a_bytes[c][:].rearrange("p g n -> p (g n)"),
+                a_bf[c][:].rearrange("p g n -> p (g n)"),
+            )
 
         def product(c):
             cols = slice(c * CHUNK, (c + 1) * CHUNK)
-            acc = bank(c, [P, PACK, CHUNK], f"acc{c}")
+            last = c == CHUNKS - 1
+            banks = [bank(c, [P, PACK, CHUNK], f"acc{c}")]
+            if last:
+                banks.append(bank(PACK, [P, PACK, CHUNK], "acc_last"))
             for j in range(PACK):
+                acc = banks[-1] if j >= PACK // 2 else banks[0]
                 rows = slice(j * P, (j + 1) * P)
                 for g in range(PASSES):
                     nc.tensor.matmul_mx(
                         out=acc[:, j, :], lhsT=h_codes[g][:, rows].bitcast(FP8X4), lhsT_scale=h_bytes[g][:, rows],
-                        rhs=a_codes[g][:, cols].bitcast(FP8X4), rhs_scale=a_bytes[g][:, cols],
+                        rhs=a_codes[c][:, g, :].bitcast(FP8X4), rhs_scale=a_bytes[c][:, g, :],
                         start=(g == 0), stop=(g == PASSES - 1),
                     )
-            nc.scalar.copy(out_f[c][:], acc[:])
+            if last:
+                nc.scalar.copy(out_f[c][:, : PACK // 2, :], banks[0][:, : PACK // 2, :])
+                nc.vector.tensor_copy(out_f[c][:, PACK // 2 :, :], banks[1][:, PACK // 2 :, :])
+            else:
+                nc.scalar.copy(out_f[c][:], banks[0][:])
             nc.sync.dma_start(out_0.rearrange("(p j) v -> p j v", j=PACK)[:, :, cols], out_f[c][:])
 
         def planes(c):
@@ -218,21 +238,25 @@ def tile_picked_yslot_soft_po_kernel(tc, x_words, x_scales, e_words, e_scales, m
             nc.vector.quantize_mx(out_codes[:, cols].bitcast(FP8X4), out_bytes[:, cols], out_bf[c][:])
             nc.sync.dma_start(out_1[0].rearrange("p n t -> p (n t)").bitcast(I32)[:, cols], out_codes[:, cols].bitcast(I32))
 
-        weigh(0)
+        weigh(0, 0)
         nc.vector.quantize_mx(h_codes[0][:].bitcast(FP8X4), h_bytes[0][:], h_bf[0][:])
-        weigh(1)
-        nc.vector.quantize_mx(h_codes[1][:].bitcast(FP8X4), h_bytes[1][:], h_bf[1][:])
+        weigh(1, 0)
+        weigh(0, 1)
         quant_a(0)
+        nc.vector.quantize_mx(h_codes[1][:].bitcast(FP8X4), h_bytes[1][:], h_bf[1][:])
         product(0)
-        weigh(2)
+        weigh(1, 1)
+        weigh(1, 2)
         quant_a(1)
         product(1)
-        weigh(3)
+        weigh(1, 3)
         quant_a(2)
         product(2)
         quant_a(3)
+        for c in range(CHUNKS - 2):
+            planes(c)
         product(3)
-        for c in range(CHUNKS):
+        for c in range(CHUNKS - 2, CHUNKS):
             planes(c)
         for q in range(QUADS):
             queue = nc.sync if q % 2 == 0 else nc.scalar

@@ -23,7 +23,7 @@ PASSES = S // PASS
 QUADS = 4
 CHUNK = 128
 CHUNKS = V // CHUNK
-ROW0, ROW_STEP = 4, 8
+ROW0 = P - 16
 
 
 def weave_out(tile_ap):
@@ -61,15 +61,14 @@ def tile_picked_yslot_soft_po_kernel(tc, x_words, x_scales, e_words, e_scales, m
         inv_t = tile("inv_t", [P, PASSES, PACK], F32)
         mask_t = tile("mask_t", [P, PASSES, PACK], F32)
 
-        nc.gpsimd.memset(es[:].bitcast(I32), 0)
-        nc.gpsimd.memset(xs[:, : T // 4].bitcast(I32), 0)
-        nc.vector.memset(xs[:, T // 4 :].bitcast(I32), 0)
+        nc.vector.memset(es[:ROW0, :].bitcast(I32), 0)
+        nc.vector.memset(xs[:ROW0, :].bitcast(I32), 0)
         for g in range(PASSES):
-            nc.gpsimd.memset(placed[g][:].bitcast(I32), 0)
+            nc.vector.memset(placed[g][:].bitcast(I32), 0)
         nc.sync.dma_start(slot_t[:], slot)
-        nc.sync.dma_start(es[ROW0:P:ROW_STEP, :].bitcast(I32), e_scales[0].bitcast(I32))
+        nc.sync.dma_start(es[ROW0:, :].bitcast(I32), e_scales[0].bitcast(I32))
         nc.sync.dma_start(offs_t[:], offs)
-        nc.sync.dma_start(xs[ROW0:P:ROW_STEP, :].bitcast(I32), x_scales[0].bitcast(I32))
+        nc.sync.dma_start(xs[ROW0:, :].bitcast(I32), x_scales[0].bitcast(I32))
         nc.sync.dma_start(ew[:], e_words[0].rearrange("p n t -> p (n t)").bitcast(I32))
         nc.gpsimd.dma_start(mask_t[:], mask.rearrange("(g p j) o -> p g (j o)", p=P, j=PACK))
         nc.gpsimd.dma_start(inv_t[:], inv.rearrange("(g p j) o -> p g (j o)", p=P, j=PACK))
@@ -100,7 +99,7 @@ def tile_picked_yslot_soft_po_kernel(tc, x_words, x_scales, e_words, e_scales, m
             for q in range(QUADS):
                 nc.sync.dma_start(
                     placed[g][32 * q : 32 * q + 4, :].bitcast(I32),
-                    staged[g][32 * q + ROW0 : 32 * (q + 1) : ROW_STEP, :].bitcast(I32),
+                    staged[g][ROW0 + 4 * q : ROW0 + 4 * q + 4, :].bitcast(I32),
                 )
 
         x_picked = [tile("x_picked0", [P, PASS], U8, "wide0")]
@@ -196,7 +195,7 @@ def tile_picked_yslot_soft_po_kernel(tc, x_words, x_scales, e_words, e_scales, m
 
         out_codes = tile("out_codes", [P, V], U32)
         out_bytes = tile("out_bytes", [P, V], U8)
-        out_bf = [tile(f"out_bf{c}", [P, CHUNK * PACK], BF16) for c in range(CHUNKS)]
+        out_wide = tile("out_wide", [P, V * PACK], BF16)
         out_f = [tile(f"out_f{c}", [P, PACK, CHUNK], F32) for c in range(CHUNKS)]
 
         def weigh(g, c):
@@ -232,10 +231,12 @@ def tile_picked_yslot_soft_po_kernel(tc, x_words, x_scales, e_words, e_scales, m
                 nc.scalar.copy(out_f[c][:], banks[0][:])
             nc.sync.dma_start(out_0.rearrange("(p j) v -> p j v", j=PACK)[:, :, cols], out_f[c][:])
 
-        def planes(c):
-            cols = slice(c * CHUNK, (c + 1) * CHUNK)
-            nc.vector.tensor_copy(weave_out(out_bf[c][:]), weave_in(out_f[c][:]))
-            nc.vector.quantize_mx(out_codes[:, cols].bitcast(FP8X4), out_bytes[:, cols], out_bf[c][:])
+        def weave(c):
+            nc.vector.tensor_copy(weave_out(out_wide[:, c * CHUNK * PACK : (c + 1) * CHUNK * PACK]), weave_in(out_f[c][:]))
+
+        def planes(first, last):
+            cols = slice(first * CHUNK, last * CHUNK)
+            nc.vector.quantize_mx(out_codes[:, cols].bitcast(FP8X4), out_bytes[:, cols], out_wide[:, first * CHUNK * PACK : last * CHUNK * PACK])
             nc.sync.dma_start(out_1[0].rearrange("p n t -> p (n t)").bitcast(I32)[:, cols], out_codes[:, cols].bitcast(I32))
 
         weigh(0, 0)
@@ -253,11 +254,13 @@ def tile_picked_yslot_soft_po_kernel(tc, x_words, x_scales, e_words, e_scales, m
         quant_a(2)
         product(2)
         quant_a(3)
-        for c in range(CHUNKS - 2):
-            planes(c)
         product(3)
-        for c in range(CHUNKS - 2, CHUNKS):
-            planes(c)
+        weave(0)
+        weave(1)
+        weave(2)
+        planes(0, 2)
+        weave(3)
+        planes(2, 4)
         for q in range(QUADS):
             queue = nc.sync if q % 2 == 0 else nc.scalar
             queue.dma_start(out_2[0, 4 * q : 4 * q + 4, :].bitcast(I32), out_bytes[32 * q : 32 * q + 4, :].bitcast(I32))

@@ -79,7 +79,6 @@ def tile_picked_yslot_soft_po_kernel(tc, x_words, x_scales, e_words, e_scales, m
             nc.sync.dma_start(raw[:], wv.rearrange("(p k) m -> p k m", k=PACK)[:, :, half * N // 2 : (half + 1) * N // 2])
             return raw
 
-
         e_picked = tile("e_picked", [P, V], U8, "slots")
         staged = [tile("staged0", [P, PASS + V], U8), tile("staged1", [P, PASS], U8)]
         x_bytes = [placed[g][:, :PASS].rearrange("p (j n) -> p j n", j=PACK) for g in range(PASSES)]
@@ -155,8 +154,8 @@ def tile_picked_yslot_soft_po_kernel(tc, x_words, x_scales, e_words, e_scales, m
 
         for half in range(2):
             nc.scalar.copy(
-                wv_bf[:].rearrange("p (j m k) -> p m k j", j=PACK, k=PACK)[:, half * P // 2 : (half + 1) * P // 2],
-                wv_raw[half][:].rearrange("p k (m j) -> p m k j", j=PACK),
+                wv_bf[:].rearrange("p (j m k) -> p m j k", j=PACK, k=PACK)[:, half * P // 2 : (half + 1) * P // 2],
+                wv_raw[half][:].rearrange("p k (m j) -> p m j k", j=PACK),
             )
         ex = [tile(f"ex{g}", [P, PACK, V], F32, f"wide{g}") for g in range(PASSES)]
         pick_words(0)
@@ -181,7 +180,8 @@ def tile_picked_yslot_soft_po_kernel(tc, x_words, x_scales, e_words, e_scales, m
                 rhs=wv_codes[:].bitcast(FP8X4), rhs_scale=wv_bytes[:], start=True, stop=True,
             )
             nc.scalar.activation(h_planes[:, j, :], h1[:], ACT.Copy, scale=inv_t[:, 1, j : j + 1])
-        nc.scalar.copy(weave_out(h_bf[1][:]), weave_in(h_planes[:]))
+        split = N - CHUNK
+        nc.scalar.copy(weave_out(h_bf[1][:, : split * PACK]), weave_in(h_planes[:, :, :split]))
         for j in range(PACK):
             nc.scalar.activation(a_planes[:, j, :], ex[0][:, j, V // 2 :], ACT.Copy, scale=weight[:, 0, j : j + 1])
         for c in range(CHUNKS // 2, CHUNKS):
@@ -231,10 +231,10 @@ def tile_picked_yslot_soft_po_kernel(tc, x_words, x_scales, e_words, e_scales, m
                 nc.scalar.copy(out_f[c][:], banks[0][:])
             nc.sync.dma_start(out_0.rearrange("(p j) v -> p j v", j=PACK)[:, :, cols], out_f[c][:])
 
-        def weave(c):
-            nc.vector.tensor_copy(weave_out(out_wide[:, c * CHUNK * PACK : (c + 1) * CHUNK * PACK]), weave_in(out_f[c][:]))
+        def weave(c, copy):
+            copy(weave_out(out_wide[:, c * CHUNK * PACK : (c + 1) * CHUNK * PACK]), weave_in(out_f[c][:]))
 
-        def planes(first, last):
+        def hand_on(first, last):
             cols = slice(first * CHUNK, last * CHUNK)
             nc.vector.quantize_mx(out_codes[:, cols].bitcast(FP8X4), out_bytes[:, cols], out_wide[:, first * CHUNK * PACK : last * CHUNK * PACK])
             nc.sync.dma_start(out_1[0].rearrange("p n t -> p (n t)").bitcast(I32)[:, cols], out_codes[:, cols].bitcast(I32))
@@ -242,6 +242,7 @@ def tile_picked_yslot_soft_po_kernel(tc, x_words, x_scales, e_words, e_scales, m
         weigh(0, 0)
         nc.vector.quantize_mx(h_codes[0][:].bitcast(FP8X4), h_bytes[0][:], h_bf[0][:])
         weigh(1, 0)
+        nc.vector.tensor_copy(weave_out(h_bf[1][:, split * PACK :]), weave_in(h_planes[:, :, split:]))
         weigh(0, 1)
         quant_a(0)
         nc.vector.quantize_mx(h_codes[1][:].bitcast(FP8X4), h_bytes[1][:], h_bf[1][:])
@@ -255,12 +256,12 @@ def tile_picked_yslot_soft_po_kernel(tc, x_words, x_scales, e_words, e_scales, m
         product(2)
         quant_a(3)
         product(3)
-        weave(0)
-        weave(1)
-        weave(2)
-        planes(0, 2)
-        weave(3)
-        planes(2, 4)
+        weave(0, nc.vector.tensor_copy)
+        weave(1, nc.vector.tensor_copy)
+        weave(2, nc.scalar.copy)
+        hand_on(0, CHUNKS // 2)
+        weave(3, nc.vector.tensor_copy)
+        hand_on(CHUNKS // 2, CHUNKS)
         for q in range(QUADS):
             queue = nc.sync if q % 2 == 0 else nc.scalar
             queue.dma_start(out_2[0, 4 * q : 4 * q + 4, :].bitcast(I32), out_bytes[32 * q : 32 * q + 4, :].bitcast(I32))

@@ -54,7 +54,7 @@ def tile_picked_yslot_soft_po_kernel(tc, x_words, x_scales, e_words, e_scales, m
         offs_t = lists.tile([P, S // 16], U16, name="offs_t")
         slot_t = lists.tile([P, V // 16], U16, name="slot_t")
         xw = tile("xw", [P, T], I32)
-        ew = tile("ew", [P, W], I32, "wide1")
+        ew = tile("ew", [P, W], I32, "slot_words")
         xs = tile("xs", [P, T], U8)
         es = tile("es", [P, W], U8)
         placed = [tile("placed0", [P, PASS + V], U8), tile("placed1", [P, PASS], U8)]
@@ -69,10 +69,10 @@ def tile_picked_yslot_soft_po_kernel(tc, x_words, x_scales, e_words, e_scales, m
         nc.sync.dma_start(es[ROW0:, :].bitcast(I32), e_scales[0].bitcast(I32))
         nc.sync.dma_start(offs_t[:], offs)
         nc.sync.dma_start(xs[ROW0:, :].bitcast(I32), x_scales[0].bitcast(I32))
-        nc.sync.dma_start(ew[:], e_words[0].rearrange("p n t -> p (n t)").bitcast(I32))
+        nc.sync.dma_start(xw[:], x_words[0].rearrange("p n t -> p (n t)").bitcast(I32))
         nc.gpsimd.dma_start(mask_t[:], mask.rearrange("(g p j) o -> p g (j o)", p=P, j=PACK))
         nc.gpsimd.dma_start(inv_t[:], inv.rearrange("(g p j) o -> p g (j o)", p=P, j=PACK))
-        nc.sync.dma_start(xw[:], x_words[0].rearrange("p n t -> p (n t)").bitcast(I32))
+        nc.sync.dma_start(ew[:], e_words[0].rearrange("p n t -> p (n t)").bitcast(I32))
 
         def load_wv(half):
             raw = tile(f"wv_raw{half}", [P, PACK, N // 2], F32, f"wide{half}")
@@ -83,7 +83,6 @@ def tile_picked_yslot_soft_po_kernel(tc, x_words, x_scales, e_words, e_scales, m
         staged = [tile("staged0", [P, PASS + V], U8), tile("staged1", [P, PASS], U8)]
         x_bytes = [placed[g][:, :PASS].rearrange("p (j n) -> p j n", j=PACK) for g in range(PASSES)]
         e_bytes = placed[0][:, PASS:]
-        x_codes = [tile(f"x_codes{g}", [P, PACK, P], U32) for g in range(PASSES)]
 
         def entries(g):
             return offs_t[:, g * PASS // 16 : (g + 1) * PASS // 16]
@@ -104,12 +103,10 @@ def tile_picked_yslot_soft_po_kernel(tc, x_words, x_scales, e_words, e_scales, m
         x_picked = [tile("x_picked0", [P, PASS], U8, "wide0")]
         nc.vector.tensor_copy(e_picked[:], es[:].indirect(slot_t[:]))
         nc.vector.tensor_copy(x_picked[0][:], xs[:].indirect(entries(0)))
-        deal_bytes(0)
         nc.vector.tensor_copy(staged[0][:, PASS:].bitcast(I32), e_picked[:].bitcast(I32))
+        deal_bytes(0)
         place_bytes(0)
         wv_raw = [load_wv(0)]
-        e_codes = tile("e_codes", [P, V], U32, "slots")
-        nc.vector.tensor_copy(e_codes[:], ew[:].bitcast(U32).indirect(slot_t[:]))
         x_picked.append(tile("x_picked1", [P, PASS], U8, "wide1"))
         nc.vector.tensor_copy(x_picked[1][:], xs[:].indirect(entries(1)))
         deal_bytes(1)
@@ -158,7 +155,11 @@ def tile_picked_yslot_soft_po_kernel(tc, x_words, x_scales, e_words, e_scales, m
                 wv_raw[half][:].rearrange("p k (m j) -> p m j k", j=PACK),
             )
         ex = [tile(f"ex{g}", [P, PACK, V], F32, f"wide{g}") for g in range(PASSES)]
+        x_codes = [tile("x_codes0", [P, PACK, P], U32)]
         pick_words(0)
+        e_codes = tile("e_codes", [P, V], U32, "slots")
+        nc.vector.tensor_copy(e_codes[:], ew[:].bitcast(U32).indirect(slot_t[:]))
+        x_codes.append(tile("x_codes1", [P, PACK, P], U32, "slot_words"))
         pick_words(1)
         scores(0)
         nc.vector.quantize_mx(wv_codes[:].bitcast(FP8X4), wv_bytes[:], wv_bf[:])

@@ -70,8 +70,8 @@ def tile_picked_yslot_soft_po_kernel(tc, x_words, x_scales, e_words, e_scales, m
         nc.sync.dma_start(offs_t[:], offs)
         nc.sync.dma_start(xs[ROW0:, :].bitcast(I32), x_scales[0].bitcast(I32))
         nc.sync.dma_start(xw[:], x_words[0].rearrange("p n t -> p (n t)").bitcast(I32))
-        nc.gpsimd.dma_start(mask_t[:], mask.rearrange("(g p j) o -> p g (j o)", p=P, j=PACK))
-        nc.gpsimd.dma_start(inv_t[:], inv.rearrange("(g p j) o -> p g (j o)", p=P, j=PACK))
+        nc.scalar.dma_start(mask_t[:], mask.rearrange("(g p j) o -> p g (j o)", p=P, j=PACK))
+        nc.scalar.dma_start(inv_t[:], inv.rearrange("(g p j) o -> p g (j o)", p=P, j=PACK))
         nc.sync.dma_start(ew[:], e_words[0].rearrange("p n t -> p (n t)").bitcast(I32))
 
         def load_wv(half):
@@ -113,156 +113,194 @@ def tile_picked_yslot_soft_po_kernel(tc, x_words, x_scales, e_words, e_scales, m
         wv_raw.append(load_wv(1))
         place_bytes(1)
 
-        neg_max = tile("neg_max", [P, PASSES, PACK], F32)
-        total = tile("total", [P, PASSES, PACK], F32)
-        share = tile("share", [P, PASSES, PACK], F32)
+        total = [tile(f"total{g}", [P, PACK], F32) for g in range(PASSES)]
+        factors = tile("factors", [P, PASSES, PACK, 2], F32)
         weight = tile("weight", [P, PASSES, PACK], F32)
+        nc.scalar.copy(factors[:, :, :, 1], mask_t[:])
 
-        def scores(g):
-            for j in range(PACK):
+        def scores(g, hands, tag):
+            neg_max = tile(f"neg_max{g}{hands[0]}", [P, PACK], F32, tag)
+            for j in hands:
                 y = bank(PACK * g + j, [P, V], f"y{g}{j}")
                 nc.tensor.matmul_mx(
                     out=y[:], lhsT=x_codes[g][:, j, :].bitcast(FP8X4), lhsT_scale=x_bytes[g][:, j, :],
                     rhs=e_codes[:].bitcast(FP8X4), rhs_scale=e_bytes, start=True, stop=True,
                 )
-                nc.vector.tensor_reduce(neg_max[:, g, j : j + 1], y[:], AX.X, ALU.max, negate=True)
+                nc.vector.tensor_reduce(neg_max[:, j : j + 1], y[:], AX.X, ALU.max, negate=True)
                 nc.scalar.activation(
-                    ex[g][:, j, :], y[:], ACT.Exp, bias=neg_max[:, g, j : j + 1], accum_out=total[:, g, j : j + 1]
+                    ex[g][:, j, :], y[:], ACT.Exp, bias=neg_max[:, j : j + 1], accum_out=total[g][:, j : j + 1]
                 )
 
         def pick_words(g):
             nc.vector.tensor_copy(x_codes[g][:].rearrange("p j n -> p n j"), xw[:].bitcast(U32).indirect(entries(g)))
 
         def weights(g):
-            nc.vector.reciprocal(share[:, g, :], total[:, g, :])
-            nc.vector.tensor_tensor(weight[:, g, :], share[:, g, :], mask_t[:, g, :], ALU.mult)
+            nc.vector.reciprocal(factors[:, g, :, 0], total[g][:])
+            nc.vector.tensor_reduce(weight[:, g, :], factors[:, g, :, :], AX.X, ALU.mult)
 
-        wv_bf = tile("wv_bf", [P, N * PACK], BF16)
-        wv_codes = tile("wv_codes", [P, N], U32)
-        wv_bytes = tile("wv_bytes", [P, N], U8)
-        a_bf = [tile(f"a_bf{c}", [P, PASSES, CHUNK * PACK], BF16) for c in range(CHUNKS)]
-        a_codes = [tile(f"a_codes{c}", [P, PASSES, CHUNK], U32) for c in range(CHUNKS)]
-        a_bytes = [tile(f"a_bytes{c}", [P, PASSES, CHUNK], U8) for c in range(CHUNKS)]
-        a_planes = tile("a_planes", [P, PACK, V // 2], BF16)
+        HALF = V // 2
+        LEFT, RIGHT = 0, 1
+        wv_bf = [tile(f"wv_bf{s}", [P, HALF * PACK], BF16) for s in range(2)]
+        wv_codes = [tile(f"wv_codes{s}", [P, HALF], U32) for s in range(2)]
+        wv_bytes = [tile(f"wv_bytes{s}", [P, HALF], U8) for s in range(2)]
         h_bf = [tile(f"h_bf{g}", [P, N * PACK], BF16) for g in range(PASSES)]
-        h_codes = [tile(f"h_codes{g}", [P, N], U32) for g in range(PASSES)]
         h_bytes = [tile(f"h_bytes{g}", [P, N], U8) for g in range(PASSES)]
-        h_planes = tile("h_planes", [P, PACK, N], BF16)
+        right_codes = [tile(f"right_codes{g}", [P, HALF], U32) for g in range(PASSES)]
+        right_bytes = [tile(f"right_bytes{g}", [P, HALF], U8) for g in range(PASSES)]
+        left_codes = [tile(f"left_codes{c}", [P, PASSES * CHUNK], U32) for c in range(2)]
+        left_bytes = [tile(f"left_bytes{c}", [P, PASSES * CHUNK], U8) for c in range(2)]
 
-        for half in range(2):
+        def round_wv(s):
             nc.scalar.copy(
-                wv_bf[:].rearrange("p (j m k) -> p m j k", j=PACK, k=PACK)[:, half * P // 2 : (half + 1) * P // 2],
-                wv_raw[half][:].rearrange("p k (m j) -> p m j k", j=PACK),
+                wv_bf[s][:].rearrange("p (j m k) -> p m j k", j=PACK, k=PACK),
+                wv_raw[s][:].rearrange("p k (m j) -> p m j k", j=PACK),
             )
-        ex = [tile(f"ex{g}", [P, PACK, V], F32, f"wide{g}") for g in range(PASSES)]
+
+        def quant(codes, scales, values):
+            nc.vector.quantize_mx(codes[:].bitcast(FP8X4), scales[:], values[:])
+
+        def h_product(out, g, t, s, cols):
+            nc.tensor.matmul_mx(
+                out=out, lhsT=x_codes[g][:, t, :].bitcast(FP8X4), lhsT_scale=x_bytes[g][:, t, :],
+                rhs=wv_codes[s][:, cols].bitcast(FP8X4), rhs_scale=wv_bytes[s][:, cols], start=True, stop=True,
+            )
+
+        def h_on_vector(g, s, first_bank):
+            for u in range(2):
+                hb = bank(first_bank + u, [P, PACK, CHUNK], f"h{g}{s}{u}")
+                for t in range(PACK):
+                    h_product(hb[:, t, :], g, t, s, slice(u * CHUNK, (u + 1) * CHUNK))
+                nc.vector.tensor_tensor(
+                    h_bf[g][:].rearrange("p (j s m t) -> p s j m t", j=PACK, s=2, t=PACK)[:, s, 2 * u : 2 * u + 2],
+                    hb[:].rearrange("p t (j m) -> p j m t", j=2),
+                    inv_t[:, g, :].unsqueeze(1).unsqueeze(1).to_broadcast([P, 2, P // 2, PACK]),
+                    ALU.mult,
+                )
+
+        def h_on_scalar(g, s, first_bank):
+            h_planes = tile("h_planes", [P, PACK, HALF], BF16, "last_max")
+            for u in range(2):
+                hb = bank(first_bank + u, [P, 2, HALF], f"h{g}{s}{u}")
+                for t in range(2):
+                    h_product(hb[:, t, :], g, 2 * u + t, s, slice(0, HALF))
+                for t in range(2):
+                    nc.scalar.activation(h_planes[:, 2 * u + t, :], hb[:, t, :], ACT.Copy, scale=inv_t[:, g, 2 * u + t : 2 * u + t + 1])
+            nc.scalar.copy(
+                h_bf[g][:].rearrange("p (j s c i t) -> p s j c t i", j=PACK, s=2, i=2, t=PACK)[:, s],
+                h_planes[:].rearrange("p t (j c i) -> p j c t i", j=PACK, i=2),
+            )
+
+        def a_piece(g, c):
+            if c < 2:
+                return left_bf[c][:, g * CHUNK * PACK : (g + 1) * CHUNK * PACK]
+            return right_bf[g][:, (c - 2) * CHUNK * PACK : (c - 1) * CHUNK * PACK]
+
+        def a_on_scalar(g):
+            planes = tile("a_planes", [P, PACK, V - CHUNK], BF16)
+            for j in range(PACK):
+                nc.scalar.activation(planes[:, j, :], ex[g][:, j, CHUNK:], ACT.Copy, scale=weight[:, g, j : j + 1])
+            nc.scalar.copy(weave_out(right_bf[g][:]), weave_in(planes[:, :, CHUNK:]))
+            nc.scalar.copy(weave_out(a_piece(g, 1)), weave_in(planes[:, :, :CHUNK]))
+
+        def a_on_vector(g, c):
+            weigh(nc.vector, g, c)
+
+        def weigh(engine, g, c):
+            cols = slice(c * CHUNK, (c + 1) * CHUNK)
+            engine.tensor_tensor(weave_out(a_piece(g, c)), weave_in(ex[g][:, :, cols]), spread(weight[:, g, :], CHUNK), ALU.mult)
+
+        round_wv(0)
         x_codes = [tile("x_codes0", [P, PACK, P], U32)]
         pick_words(0)
         e_codes = tile("e_codes", [P, V], U32, "slots")
         nc.vector.tensor_copy(e_codes[:], ew[:].bitcast(U32).indirect(slot_t[:]))
         x_codes.append(tile("x_codes1", [P, PACK, P], U32, "slot_words"))
         pick_words(1)
-        scores(0)
-        nc.vector.quantize_mx(wv_codes[:].bitcast(FP8X4), wv_bytes[:], wv_bf[:])
+        ex = [tile("ex0", [P, PACK, V], F32, "wide0")]
+        scores(0, (0, 1, 2, 3), None)
+        quant(wv_codes[0], wv_bytes[0], wv_bf[0])
+        round_wv(1)
+        quant(wv_codes[1], wv_bytes[1], wv_bf[1])
         weights(0)
-        scores(1)
-
-        h0 = [bank(c, [P, PACK, CHUNK], f"h0{c}") for c in range(CHUNKS)]
-        for c in range(CHUNKS):
-            cols = slice(c * CHUNK, (c + 1) * CHUNK)
-            for j in range(PACK):
-                nc.tensor.matmul_mx(
-                    out=h0[c][:, j, :], lhsT=x_codes[0][:, j, :].bitcast(FP8X4), lhsT_scale=x_bytes[0][:, j, :],
-                    rhs=wv_codes[:, cols].bitcast(FP8X4), rhs_scale=wv_bytes[:, cols], start=True, stop=True,
-                )
-        for j in range(PACK):
-            h1 = bank(PACK + j, [P, N], f"h1{j}")
-            nc.tensor.matmul_mx(
-                out=h1[:], lhsT=x_codes[1][:, j, :].bitcast(FP8X4), lhsT_scale=x_bytes[1][:, j, :],
-                rhs=wv_codes[:].bitcast(FP8X4), rhs_scale=wv_bytes[:], start=True, stop=True,
-            )
-            nc.scalar.activation(h_planes[:, j, :], h1[:], ACT.Copy, scale=inv_t[:, 1, j : j + 1])
-        split = N - CHUNK
-        nc.scalar.copy(weave_out(h_bf[1][:, : split * PACK]), weave_in(h_planes[:, :, :split]))
-        for j in range(PACK):
-            nc.scalar.activation(a_planes[:, j, :], ex[0][:, j, V // 2 :], ACT.Copy, scale=weight[:, 0, j : j + 1])
-        for c in range(CHUNKS // 2, CHUNKS):
-            first = c * CHUNK - V // 2
-            nc.scalar.copy(weave_out(a_bf[c][:, 0, :]), weave_in(a_planes[:, :, first : first + CHUNK]))
-
-        for c in range(CHUNKS):
-            wide = slice(c * CHUNK * PACK, (c + 1) * CHUNK * PACK)
-            nc.vector.tensor_tensor(weave_out(h_bf[0][:, wide]), weave_in(h0[c][:]), spread(inv_t[:, 0, :], CHUNK), ALU.mult)
+        ex.append(tile("ex1", [P, PACK, V], F32, "wide1"))
+        scores(1, (0, 1, 2, 3), "last_max")
         weights(1)
+        right_bf = [tile("right_bf0", [P, HALF * PACK], BF16, "wv_bf1"), tile("right_bf1", [P, HALF * PACK], BF16)]
+        for c in (2, 3):
+            nc.gpsimd.tensor_tensor(
+                a_piece(0, c).rearrange("p (n j) -> p n j", j=PACK),
+                ex[0][:, :, c * CHUNK : (c + 1) * CHUNK].rearrange("p j n -> p n j"),
+                weight[:, 0, :].unsqueeze(1).to_broadcast([P, CHUNK, PACK]),
+                ALU.mult,
+            )
+        h_on_vector(0, 0, 0)
+        h_on_scalar(1, 0, 2)
+        h_on_vector(0, 1, 4)
+        h_on_vector(1, 1, 6)
+        h_codes = [tile("h_codes0", [P, N], U32, "wv_codes1"), tile("h_codes1", [P, N], U32)]
+        left_bf = [tile(f"left_bf{c}", [P, PASSES * CHUNK * PACK], BF16, tag) for c, tag in enumerate(("wv_bytes1", "slot_words"))]
+        a_on_scalar(1)
+
+        def multiply(out, g, j, codes, scales):
+            rows = slice(j * P, (j + 1) * P)
+            nc.tensor.matmul_mx(
+                out=out, lhsT=h_codes[g][:, rows].bitcast(FP8X4), lhsT_scale=h_bytes[g][:, rows],
+                rhs=codes.bitcast(FP8X4), rhs_scale=scales, start=(g == 0), stop=(g == PASSES - 1),
+            )
 
         out_codes = tile("out_codes", [P, V], U32)
         out_bytes = tile("out_bytes", [P, V], U8)
         out_wide = tile("out_wide", [P, V * PACK], BF16)
-        out_f = [tile(f"out_f{c}", [P, PACK, CHUNK], F32) for c in range(CHUNKS)]
+        right_f = tile("right_f", [P, PACK, HALF], F32)
+        left_f = [tile(f"left_f{c}", [P, PACK, CHUNK], F32) for c in range(2)]
+        out_rows = out_0.rearrange("(p j) v -> p j v", j=PACK)
+        right_acc = [bank(j, [P, HALF], f"right_acc{j}") for j in range(PACK)]
 
-        def weigh(g, c):
-            cols = slice(c * CHUNK, (c + 1) * CHUNK)
-            nc.vector.tensor_tensor(weave_out(a_bf[c][:, g, :]), weave_in(ex[g][:, :, cols]), spread(weight[:, g, :], CHUNK), ALU.mult)
-
-        def quant_a(c):
-            nc.vector.quantize_mx(
-                a_codes[c][:].rearrange("p g n -> p (g n)").bitcast(FP8X4),
-                a_bytes[c][:].rearrange("p g n -> p (g n)"),
-                a_bf[c][:].rearrange("p g n -> p (g n)"),
-            )
-
-        def product(c):
-            cols = slice(c * CHUNK, (c + 1) * CHUNK)
-            last = c == CHUNKS - 1
-            banks = [bank(c, [P, PACK, CHUNK], f"acc{c}")]
-            if last:
-                banks.append(bank(PACK, [P, PACK, CHUNK], "acc_last"))
+        def right_pass(g):
+            quant(right_codes[g], right_bytes[g], right_bf[g])
             for j in range(PACK):
-                acc = banks[-1] if j >= PACK // 2 else banks[0]
-                rows = slice(j * P, (j + 1) * P)
+                multiply(right_acc[j][:], g, j, right_codes[g][:], right_bytes[g][:])
+
+        def left_product(c, banks):
+            quant(left_codes[c], left_bytes[c], left_bf[c])
+            accs = [bank(b, [P, PACK, CHUNK], f"left_acc{b}") for b in banks]
+            share = PACK // len(accs)
+            for j in range(PACK):
                 for g in range(PASSES):
-                    nc.tensor.matmul_mx(
-                        out=acc[:, j, :], lhsT=h_codes[g][:, rows].bitcast(FP8X4), lhsT_scale=h_bytes[g][:, rows],
-                        rhs=a_codes[c][:, g, :].bitcast(FP8X4), rhs_scale=a_bytes[c][:, g, :],
-                        start=(g == 0), stop=(g == PASSES - 1),
-                    )
-            if last:
-                nc.scalar.copy(out_f[c][:, : PACK // 2, :], banks[0][:, : PACK // 2, :])
-                nc.vector.tensor_copy(out_f[c][:, PACK // 2 :, :], banks[1][:, PACK // 2 :, :])
-            else:
-                nc.scalar.copy(out_f[c][:], banks[0][:])
-            nc.sync.dma_start(out_0.rearrange("(p j) v -> p j v", j=PACK)[:, :, cols], out_f[c][:])
+                    cols = slice(g * CHUNK, (g + 1) * CHUNK)
+                    multiply(accs[j // share][:, j, :], g, j, left_codes[c][:, cols], left_bytes[c][:, cols])
+            for acc, copy, first in zip(accs, (nc.scalar.copy, nc.vector.tensor_copy), (0, share)):
+                copy(left_f[c][:, first : first + share, :], acc[:, first : first + share, :])
+            nc.sync.dma_start(out_rows[:, :, c * CHUNK : (c + 1) * CHUNK], left_f[c][:])
 
         def weave(c, copy):
-            copy(weave_out(out_wide[:, c * CHUNK * PACK : (c + 1) * CHUNK * PACK]), weave_in(out_f[c][:]))
+            planes = left_f[c][:] if c < 2 else right_f[:, :, (c - 2) * CHUNK : (c - 1) * CHUNK]
+            copy(weave_out(out_wide[:, c * CHUNK * PACK : (c + 1) * CHUNK * PACK]), weave_in(planes))
 
-        def hand_on(first, last):
-            cols = slice(first * CHUNK, last * CHUNK)
-            nc.vector.quantize_mx(out_codes[:, cols].bitcast(FP8X4), out_bytes[:, cols], out_wide[:, first * CHUNK * PACK : last * CHUNK * PACK])
+        def hand_on(s):
+            cols = slice(s * HALF, (s + 1) * HALF)
+            nc.vector.quantize_mx(out_codes[:, cols].bitcast(FP8X4), out_bytes[:, cols], out_wide[:, s * HALF * PACK : (s + 1) * HALF * PACK])
             nc.sync.dma_start(out_1[0].rearrange("p n t -> p (n t)").bitcast(I32)[:, cols], out_codes[:, cols].bitcast(I32))
 
-        weigh(0, 0)
-        nc.vector.quantize_mx(h_codes[0][:].bitcast(FP8X4), h_bytes[0][:], h_bf[0][:])
-        weigh(1, 0)
-        nc.vector.tensor_copy(weave_out(h_bf[1][:, split * PACK :]), weave_in(h_planes[:, :, split:]))
-        weigh(0, 1)
-        quant_a(0)
-        nc.vector.quantize_mx(h_codes[1][:].bitcast(FP8X4), h_bytes[1][:], h_bf[1][:])
-        product(0)
-        weigh(1, 1)
-        weigh(1, 2)
-        quant_a(1)
-        product(1)
-        weigh(1, 3)
-        quant_a(2)
-        product(2)
-        quant_a(3)
-        product(3)
+        quant(h_codes[0], h_bytes[0], h_bf[0])
+        a_on_vector(0, 0)
+        a_on_vector(1, 0)
+        right_pass(0)
+        quant(h_codes[1], h_bytes[1], h_bf[1])
+        left_product(0, (4,))
+        right_pass(1)
+        for j in range(PACK):
+            nc.scalar.copy(right_f[:, j, :], right_acc[j][:])
+            if j % 2 == 1:
+                nc.sync.dma_start(out_rows[:, j - 1 : j + 1, HALF:], right_f[:, j - 1 : j + 1, :])
+        a_on_vector(0, 1)
+        left_product(1, (5, 6))
         weave(0, nc.vector.tensor_copy)
+        weave(2, nc.vector.tensor_copy)
+        weave(3, nc.scalar.copy)
         weave(1, nc.vector.tensor_copy)
-        weave(2, nc.scalar.copy)
-        hand_on(0, CHUNKS // 2)
-        weave(3, nc.vector.tensor_copy)
-        hand_on(CHUNKS // 2, CHUNKS)
+        hand_on(RIGHT)
+        hand_on(LEFT)
         for q in range(QUADS):
             queue = nc.sync if q % 2 == 0 else nc.scalar
             queue.dma_start(out_2[0, 4 * q : 4 * q + 4, :].bitcast(I32), out_bytes[32 * q : 32 * q + 4, :].bitcast(I32))

@@ -151,10 +151,7 @@ def tile_picked_yslot_soft_po_kernel(tc, x_words, x_scales, e_words, e_scales, m
         left_bytes = [tile(f"left_bytes{c}", [P, PASSES * CHUNK], U8) for c in range(2)]
 
         def round_wv(s):
-            nc.scalar.copy(
-                wv_bf[s][:].rearrange("p (j m k) -> p m j k", j=PACK, k=PACK),
-                wv_raw[s][:].rearrange("p k (m j) -> p m j k", j=PACK),
-            )
+            nc.scalar.copy(weave_out(wv_bf[s][:]), weave_in(wv_raw[s][:]))
 
         def quant(codes, scales, values):
             nc.vector.quantize_mx(codes[:].bitcast(FP8X4), scales[:], values[:])
@@ -171,9 +168,9 @@ def tile_picked_yslot_soft_po_kernel(tc, x_words, x_scales, e_words, e_scales, m
                 for t in range(PACK):
                     h_product(hb[:, t, :], g, t, s, slice(u * CHUNK, (u + 1) * CHUNK))
                 nc.vector.tensor_tensor(
-                    h_bf[g][:].rearrange("p (j s m t) -> p s j m t", j=PACK, s=2, t=PACK)[:, s, 2 * u : 2 * u + 2],
-                    hb[:].rearrange("p t (j m) -> p j m t", j=2),
-                    inv_t[:, g, :].unsqueeze(1).unsqueeze(1).to_broadcast([P, 2, P // 2, PACK]),
+                    h_bf[g][:].rearrange("p (j c m t) -> p c j m t", j=PACK, c=CHUNKS, t=PACK)[:, 2 * s + u],
+                    hb[:].rearrange("p t (m j) -> p j m t", j=PACK),
+                    inv_t[:, g, :].unsqueeze(1).unsqueeze(1).to_broadcast([P, PACK, CHUNK // PACK, PACK]),
                     ALU.mult,
                 )
 
@@ -184,7 +181,7 @@ def tile_picked_yslot_soft_po_kernel(tc, x_words, x_scales, e_words, e_scales, m
                 for t in range(2):
                     h_product(hb[:, t, :], g, 2 * u + t, s, slice(0, HALF))
                 for t in range(2):
-                    nc.scalar.activation(h_planes[:, 2 * u + t, :], hb[:, t, :], ACT.Copy, scale=inv_t[:, g, 2 * u + t : 2 * u + t + 1])
+                    nc.scalar.activation(h_planes[:, 2 * u + t, :].rearrange("p (j m) -> p j m", j=PACK), hb[:, t, :].rearrange("p (m j) -> p j m", j=PACK), ACT.Copy, scale=inv_t[:, g, 2 * u + t : 2 * u + t + 1])
             nc.scalar.copy(
                 h_bf[g][:].rearrange("p (j s c i t) -> p s j c t i", j=PACK, s=2, i=2, t=PACK)[:, s],
                 h_planes[:].rearrange("p t (j c i) -> p j c t i", j=PACK, i=2),

@@ -43,6 +43,7 @@ def tile_picked_yslot_soft_po_kernel(tc, x_words, x_scales, e_words, e_scales, m
     with ExitStack() as ctx:
         lists = ctx.enter_context(tc.tile_pool(name="lists", bufs=1))
         sb = ctx.enter_context(tc.tile_pool(name="sb", bufs=1))
+        front = ctx.enter_context(tc.tile_pool(name="front", bufs=1))
         psum = ctx.enter_context(tc.psum_pool(name="psum", bufs=1))
 
         def tile(name, shape, dtype, tag=None):
@@ -57,14 +58,13 @@ def tile_picked_yslot_soft_po_kernel(tc, x_words, x_scales, e_words, e_scales, m
         ew = tile("ew", [P, W], I32, "slot_words")
         xs = tile("xs", [P, T], U8)
         es = tile("es", [P, W], U8)
-        placed = [tile("placed0", [P, PASS + V], U8), tile("placed1", [P, PASS], U8)]
+        placed = tile("placed", [P, S + V], U8)
         inv_t = tile("inv_t", [P, PASSES, PACK], F32)
         mask_t = tile("mask_t", [P, PASSES, PACK], F32)
 
         nc.vector.memset(es[:ROW0, :].bitcast(I32), 0)
         nc.vector.memset(xs[:ROW0, :].bitcast(I32), 0)
-        for g in range(PASSES):
-            nc.vector.memset(placed[g][:].bitcast(I32), 0)
+        nc.vector.memset(placed[:].bitcast(I32), 0)
         nc.sync.dma_start(slot_t[:], slot)
         nc.sync.dma_start(es[ROW0:, :].bitcast(I32), e_scales[0].bitcast(I32))
         nc.sync.dma_start(offs_t[:], offs)
@@ -74,49 +74,44 @@ def tile_picked_yslot_soft_po_kernel(tc, x_words, x_scales, e_words, e_scales, m
         nc.scalar.dma_start(inv_t[:], inv.rearrange("(g p j) o -> p g (j o)", p=P, j=PACK))
         nc.sync.dma_start(ew[:], e_words[0].rearrange("p n t -> p (n t)").bitcast(I32))
 
+        RAW = PACK * (N // 2) * 4
+
         def load_wv(half):
-            raw = tile(f"wv_raw{half}", [P, PACK, N // 2], F32, f"wide{half}")
+            raw = front.tile([P, PACK, N // 2], F32, name=f"wv_raw{half}", offset=(1 + half) * RAW, align_bytes=64)
             nc.sync.dma_start(raw[:], wv.rearrange("(p k) m -> p k m", k=PACK)[:, :, half * N // 2 : (half + 1) * N // 2])
             return raw
 
         e_picked = tile("e_picked", [P, V], U8, "slots")
-        staged = [tile("staged0", [P, PASS + V], U8), tile("staged1", [P, PASS], U8)]
-        x_bytes = [placed[g][:, :PASS].rearrange("p (j n) -> p j n", j=PACK) for g in range(PASSES)]
-        e_bytes = placed[0][:, PASS:]
+        staged = tile("staged", [P, S + V], U8)
+        x_bytes = [placed[:, g * PASS : (g + 1) * PASS].rearrange("p (j n) -> p j n", j=PACK) for g in range(PASSES)]
+        e_bytes = placed[:, S:]
 
         def entries(g):
             return offs_t[:, g * PASS // 16 : (g + 1) * PASS // 16]
 
-        def deal_bytes(g):
-            nc.vector.tensor_copy(
-                staged[g][:, :PASS].rearrange("p (j n) -> p j n", j=PACK),
-                x_picked[g][:].rearrange("p (n j) -> p j n", j=PACK),
-            )
-
-        def place_bytes(g):
-            for q in range(QUADS):
-                nc.sync.dma_start(
-                    placed[g][32 * q : 32 * q + 4, :].bitcast(I32),
-                    staged[g][ROW0 + 4 * q : ROW0 + 4 * q + 4, :].bitcast(I32),
-                )
-
-        x_picked = [tile("x_picked0", [P, PASS], U8, "wide0")]
+        x_picked = front.tile([P, S], U8, name="x_picked", offset=2 * RAW - PASS, align_bytes=64)
         nc.vector.tensor_copy(e_picked[:], es[:].indirect(slot_t[:]))
-        nc.vector.tensor_copy(x_picked[0][:], xs[:].indirect(entries(0)))
-        nc.vector.tensor_copy(staged[0][:, PASS:].bitcast(I32), e_picked[:].bitcast(I32))
-        deal_bytes(0)
-        place_bytes(0)
-        wv_raw = [load_wv(0)]
-        x_picked.append(tile("x_picked1", [P, PASS], U8, "wide1"))
-        nc.vector.tensor_copy(x_picked[1][:], xs[:].indirect(entries(1)))
-        deal_bytes(1)
-        wv_raw.append(load_wv(1))
-        place_bytes(1)
+        nc.vector.tensor_copy(x_picked[:], xs[:].indirect(offs_t[:]))
+        nc.vector.tensor_copy(staged[:, S:].bitcast(I32), e_picked[:].bitcast(I32))
+        nc.vector.tensor_copy(
+            staged[:, :S].rearrange("p (g j n) -> p g j n", g=PASSES, j=PACK),
+            x_picked[:].rearrange("p (g n j) -> p g j n", g=PASSES, j=PACK),
+        )
+        for q in range(QUADS):
+            nc.sync.dma_start(
+                placed[32 * q : 32 * q + 4, :].bitcast(I32),
+                staged[ROW0 + 4 * q : ROW0 + 4 * q + 4, :].bitcast(I32),
+            )
+        wv_raw = [load_wv(0), load_wv(1)]
 
         total = [tile(f"total{g}", [P, PACK], F32) for g in range(PASSES)]
-        factors = tile("factors", [P, PASSES, PACK, 2], F32)
+        factors = [
+            front.tile([P, PACK, 2], F32, name="factors0", offset=5 * RAW, align_bytes=64),
+            tile("factors1", [P, PACK, 2], F32),
+        ]
         weight = tile("weight", [P, PASSES, PACK], F32)
-        nc.scalar.copy(factors[:, :, :, 1], mask_t[:])
+        for g in range(PASSES):
+            nc.scalar.copy(factors[g][:, :, 1], mask_t[:, g, :])
 
         def scores(g, hands, tag):
             neg_max = tile(f"neg_max{g}{hands[0]}", [P, PACK], F32, tag)
@@ -135,15 +130,18 @@ def tile_picked_yslot_soft_po_kernel(tc, x_words, x_scales, e_words, e_scales, m
             nc.vector.tensor_copy(x_codes[g][:].rearrange("p j n -> p n j"), xw[:].bitcast(U32).indirect(entries(g)))
 
         def weights(g):
-            nc.vector.reciprocal(factors[:, g, :, 0], total[g][:])
-            nc.vector.tensor_reduce(weight[:, g, :], factors[:, g, :, :], AX.X, ALU.mult)
+            nc.vector.reciprocal(factors[g][:, :, 0], total[g][:])
+            nc.vector.tensor_reduce(weight[:, g, :], factors[g][:], AX.X, ALU.mult)
 
         HALF = V // 2
         LEFT, RIGHT = 0, 1
-        wv_bf = [tile(f"wv_bf{s}", [P, HALF * PACK], BF16) for s in range(2)]
+        ROUNDED = HALF * PACK * 2
+        wv_bf = [
+            tile("wv_bf0", [P, HALF * PACK], BF16, "last_max"),
+            front.tile([P, HALF * PACK], BF16, name="wv_bf1", offset=4 * RAW + ROUNDED // 2, align_bytes=64),
+        ]
         wv_codes = [tile(f"wv_codes{s}", [P, HALF], U32) for s in range(2)]
         wv_bytes = [tile(f"wv_bytes{s}", [P, HALF], U8) for s in range(2)]
-        h_bf = [tile(f"h_bf{g}", [P, N * PACK], BF16) for g in range(PASSES)]
         h_bytes = [tile(f"h_bytes{g}", [P, N], U8) for g in range(PASSES)]
         right_codes = [tile(f"right_codes{g}", [P, HALF], U32) for g in range(PASSES)]
         right_bytes = [tile(f"right_bytes{g}", [P, HALF], U8) for g in range(PASSES)]
@@ -193,7 +191,7 @@ def tile_picked_yslot_soft_po_kernel(tc, x_words, x_scales, e_words, e_scales, m
             return right_bf[g][:, (c - 2) * CHUNK * PACK : (c - 1) * CHUNK * PACK]
 
         def a_on_scalar(g):
-            planes = tile("a_planes", [P, PACK, V - CHUNK], BF16)
+            planes = tile("a_planes", [P, PACK, V - CHUNK], BF16, "last_max")
             for j in range(PACK):
                 nc.scalar.activation(planes[:, j, :], ex[g][:, j, CHUNK:], ACT.Copy, scale=weight[:, g, j : j + 1])
             nc.scalar.copy(weave_out(right_bf[g][:]), weave_in(planes[:, :, CHUNK:]))
@@ -213,16 +211,23 @@ def tile_picked_yslot_soft_po_kernel(tc, x_words, x_scales, e_words, e_scales, m
         nc.vector.tensor_copy(e_codes[:], ew[:].bitcast(U32).indirect(slot_t[:]))
         x_codes.append(tile("x_codes1", [P, PACK, P], U32, "slot_words"))
         pick_words(1)
-        ex = [tile("ex0", [P, PACK, V], F32, "wide0")]
+        ex = [front.tile([P, PACK, V], F32, name="ex0", offset=0, align_bytes=64)]
         scores(0, (0, 1, 2, 3), None)
         quant(wv_codes[0], wv_bytes[0], wv_bf[0])
         round_wv(1)
         quant(wv_codes[1], wv_bytes[1], wv_bf[1])
         weights(0)
-        ex.append(tile("ex1", [P, PACK, V], F32, "wide1"))
+        ex.append(front.tile([P, PACK, V], F32, name="ex1", offset=2 * RAW, align_bytes=64))
         scores(1, (0, 1, 2, 3), "last_max")
         weights(1)
-        right_bf = [tile("right_bf0", [P, HALF * PACK], BF16, "wv_bf1"), tile("right_bf1", [P, HALF * PACK], BF16)]
+        right_bf = [
+            front.tile([P, HALF * PACK], BF16, name="right_bf0", offset=4 * RAW, align_bytes=64),
+            tile("right_bf1", [P, HALF * PACK], BF16),
+        ]
+        h_bf = [
+            front.tile([P, N * PACK], BF16, name="h_bf0", offset=4 * RAW + ROUNDED, align_bytes=64),
+            tile("h_bf1", [P, N * PACK], BF16),
+        ]
         for c in (2, 3):
             nc.gpsimd.tensor_tensor(
                 a_piece(0, c).rearrange("p (n j) -> p n j", j=PACK),
@@ -280,17 +285,23 @@ def tile_picked_yslot_soft_po_kernel(tc, x_words, x_scales, e_words, e_scales, m
             nc.sync.dma_start(out_1[0].rearrange("p n t -> p (n t)").bitcast(I32)[:, cols], out_codes[:, cols].bitcast(I32))
 
         quant(h_codes[0], h_bytes[0], h_bf[0])
+        spare = bank(7, [P, N], "spare")
+        for u in range(2):
+            nc.tensor.matmul_mx(
+                out=spare[:], lhsT=h_codes[0][:, :P].bitcast(FP8X4), lhsT_scale=h_bytes[0][:, :P],
+                rhs=h_codes[0][:].bitcast(FP8X4), rhs_scale=h_bytes[0][:], start=True, stop=True,
+            )
         a_on_vector(0, 0)
         a_on_vector(1, 0)
         right_pass(0)
         quant(h_codes[1], h_bytes[1], h_bf[1])
         left_product(0, (4,))
+        a_on_vector(0, 1)
         right_pass(1)
         for j in range(PACK):
             nc.scalar.copy(right_f[:, j, :], right_acc[j][:])
             if j % 2 == 1:
                 nc.sync.dma_start(out_rows[:, j - 1 : j + 1, HALF:], right_f[:, j - 1 : j + 1, :])
-        a_on_vector(0, 1)
         left_product(1, (5, 6))
         weave(0, nc.vector.tensor_copy)
         weave(2, nc.vector.tensor_copy)

@@ -59,8 +59,8 @@ def tile_picked_yslot_soft_po_kernel(tc, x_words, x_scales, e_words, e_scales, m
         xs = tile("xs", [P, T], U8)
         es = tile("es", [P, W], U8)
         placed = tile("placed", [P, S + V], U8)
-        inv_t = tile("inv_t", [P, PASSES, PACK], F32)
-        mask_t = tile("mask_t", [P, PASSES, PACK], F32)
+        inv_t = tile("inv_t", [P, PASSES, 2 * PACK], F32)
+        mask_t = tile("mask_t", [P, PASSES, 2 * PACK], F32)
 
         nc.vector.memset(es[:ROW0, :].bitcast(I32), 0)
         nc.vector.memset(xs[:ROW0, :].bitcast(I32), 0)
@@ -70,8 +70,8 @@ def tile_picked_yslot_soft_po_kernel(tc, x_words, x_scales, e_words, e_scales, m
         nc.sync.dma_start(offs_t[:], offs)
         nc.sync.dma_start(xs[ROW0:, :].bitcast(I32), x_scales[0].bitcast(I32))
         nc.sync.dma_start(xw[:], x_words[0].rearrange("p n t -> p (n t)").bitcast(I32))
-        nc.scalar.dma_start(mask_t[:], mask.rearrange("(g p j) o -> p g (j o)", p=P, j=PACK))
-        nc.scalar.dma_start(inv_t[:], inv.rearrange("(g p j) o -> p g (j o)", p=P, j=PACK))
+        nc.scalar.dma_start(mask_t[:, :, :PACK], mask.rearrange("(g p j) o -> p g (j o)", p=P, j=PACK))
+        nc.scalar.dma_start(inv_t[:, :, :PACK], inv.rearrange("(g p j) o -> p g (j o)", p=P, j=PACK))
         nc.sync.dma_start(ew[:], e_words[0].rearrange("p n t -> p (n t)").bitcast(I32))
 
         RAW = PACK * (N // 2) * 4
@@ -97,7 +97,7 @@ def tile_picked_yslot_soft_po_kernel(tc, x_words, x_scales, e_words, e_scales, m
             staged[:, :S].rearrange("p (g j n) -> p g j n", g=PASSES, j=PACK),
             x_picked[:].rearrange("p (g n j) -> p g j n", g=PASSES, j=PACK),
         )
-        for q in range(QUADS):
+        for q in (0, 2, 1, 3):
             nc.sync.dma_start(
                 placed[32 * q : 32 * q + 4, :].bitcast(I32),
                 staged[ROW0 + 4 * q : ROW0 + 4 * q + 4, :].bitcast(I32),
@@ -111,7 +111,7 @@ def tile_picked_yslot_soft_po_kernel(tc, x_words, x_scales, e_words, e_scales, m
         ]
         weight = tile("weight", [P, PASSES, PACK], F32)
         for g in range(PASSES):
-            nc.scalar.copy(factors[g][:, :, 1], mask_t[:, g, :])
+            nc.scalar.copy(factors[g][:, :, 1], mask_t[:, g, :PACK])
 
         def scores(g, hands, tag):
             neg_max = tile(f"neg_max{g}{hands[0]}", [P, PACK], F32, tag)
@@ -168,7 +168,7 @@ def tile_picked_yslot_soft_po_kernel(tc, x_words, x_scales, e_words, e_scales, m
                 nc.vector.tensor_tensor(
                     h_bf[g][:].rearrange("p (j c m t) -> p c j m t", j=PACK, c=CHUNKS, t=PACK)[:, 2 * s + u],
                     hb[:].rearrange("p t (m j) -> p j m t", j=PACK),
-                    inv_t[:, g, :].unsqueeze(1).unsqueeze(1).to_broadcast([P, PACK, CHUNK // PACK, PACK]),
+                    inv_t[:, g, :PACK].unsqueeze(1).unsqueeze(1).to_broadcast([P, PACK, CHUNK // PACK, PACK]),
                     ALU.mult,
                 )
 
@@ -310,5 +310,4 @@ def tile_picked_yslot_soft_po_kernel(tc, x_words, x_scales, e_words, e_scales, m
         hand_on(RIGHT)
         hand_on(LEFT)
         for q in range(QUADS):
-            queue = nc.sync if q % 2 == 0 else nc.scalar
-            queue.dma_start(out_2[0, 4 * q : 4 * q + 4, :].bitcast(I32), out_bytes[32 * q : 32 * q + 4, :].bitcast(I32))
+            nc.scalar.dma_start(out_2[0, 4 * q : 4 * q + 4, :].bitcast(I32), out_bytes[32 * q : 32 * q + 4, :].bitcast(I32))

@@ -34,10 +34,6 @@ def weave_in(planes_ap):
     return planes_ap.rearrange("p j (c i) -> p c j i", i=2)
 
 
-def spread(factor_ap, columns):
-    return factor_ap.unsqueeze(1).unsqueeze(3).to_broadcast([P, columns // 2, PACK, 2])
-
-
 def tile_picked_yslot_soft_po_kernel(tc, x_words, x_scales, e_words, e_scales, mask, wv, inv, offs, slot, out_0, out_1, out_2):
     nc = tc.nc
     with ExitStack() as ctx:
@@ -52,14 +48,26 @@ def tile_picked_yslot_soft_po_kernel(tc, x_words, x_scales, e_words, e_scales, m
         def bank(b, shape, name):
             return psum.tile(shape, F32, name=name, tag=f"bank{b}")
 
+        def quant(codes, scales, values):
+            nc.vector.quantize_mx(codes.bitcast(FP8X4), scales, values)
+
+        def product(out, left, left_bytes, right, right_bytes, start=True, stop=True):
+            nc.tensor.matmul_mx(
+                out=out, lhsT=left.bitcast(FP8X4), lhsT_scale=left_bytes,
+                rhs=right.bitcast(FP8X4), rhs_scale=right_bytes, start=start, stop=stop,
+            )
+
+        HALF = V // 2
         offs_t = lists.tile([P, S // 16], U16, name="offs_t")
         slot_t = lists.tile([P, V // 16], U16, name="slot_t")
         xw = tile("xw", [P, T], I32)
-        ew = tile("ew", [P, W], I32, "slot_words")
+        ew = tile("ew", [P, W], I32)
         xs = tile("xs", [P, T], U8)
         es = tile("es", [P, W], U8)
         placed = tile("placed", [P, S + V], U8)
-        inv_t = tile("inv_t", [P, PASSES, 2 * PACK], F32)
+        RAW = PACK * HALF * 4
+        CODES_AT = 10 * RAW
+        inv_t = front.tile([P, PASSES, 2 * PACK], F32, name="inv_t", offset=CODES_AT - 32)
         mask_t = tile("mask_t", [P, PASSES, 2 * PACK], F32)
 
         nc.vector.memset(es[:ROW0, :].bitcast(I32), 0)
@@ -74,22 +82,16 @@ def tile_picked_yslot_soft_po_kernel(tc, x_words, x_scales, e_words, e_scales, m
         nc.scalar.dma_start(inv_t[:, :, :PACK], inv.rearrange("(g p j) o -> p g (j o)", p=P, j=PACK))
         nc.sync.dma_start(ew[:], e_words[0].rearrange("p n t -> p (n t)").bitcast(I32))
 
-        RAW = PACK * (N // 2) * 4
-
-        def load_wv(half):
-            raw = front.tile([P, PACK, N // 2], F32, name=f"wv_raw{half}", offset=(1 + half) * RAW, align_bytes=64)
-            nc.sync.dma_start(raw[:], wv.rearrange("(p k) m -> p k m", k=PACK)[:, :, half * N // 2 : (half + 1) * N // 2])
-            return raw
+        WOVEN = N * PACK * 2
+        H_AT = [7 * RAW + g * (WOVEN + 192) for g in range(PASSES)]
+        total = [tile("total0", [P, PACK], F32), front.tile([P, PACK], F32, name="total1", offset=H_AT[1])]
+        factors = [front.tile([P, PACK, 6], F32, name=f"factors{g}", offset=H_AT[g] - 64 - 64 * g) for g in range(PASSES)]
+        for g in range(PASSES):
+            nc.scalar.copy(factors[g][:, :, 1], mask_t[:, g, :PACK])
 
         e_picked = tile("e_picked", [P, V], U8, "slots")
-        staged = tile("staged", [P, S + V], U8)
-        x_bytes = [placed[:, g * PASS : (g + 1) * PASS].rearrange("p (j n) -> p j n", j=PACK) for g in range(PASSES)]
-        e_bytes = placed[:, S:]
-
-        def entries(g):
-            return offs_t[:, g * PASS // 16 : (g + 1) * PASS // 16]
-
-        x_picked = front.tile([P, S], U8, name="x_picked", offset=2 * RAW - PASS, align_bytes=64)
+        x_picked = front.tile([P, S], U8, name="x_picked", offset=RAW - PASS, align_bytes=64)
+        staged = tile("staged", [P, S + V], U8, "tokens")
         nc.vector.tensor_copy(e_picked[:], es[:].indirect(slot_t[:]))
         nc.vector.tensor_copy(x_picked[:], xs[:].indirect(offs_t[:]))
         nc.vector.tensor_copy(staged[:, S:].bitcast(I32), e_picked[:].bitcast(I32))
@@ -102,212 +104,183 @@ def tile_picked_yslot_soft_po_kernel(tc, x_words, x_scales, e_words, e_scales, m
                 placed[32 * q : 32 * q + 4, :].bitcast(I32),
                 staged[ROW0 + 4 * q : ROW0 + 4 * q + 4, :].bitcast(I32),
             )
-        wv_raw = [load_wv(0), load_wv(1)]
+        wv_raw = [front.tile([P, PACK, HALF], F32, name=f"wv_raw{s}", offset=s * RAW, align_bytes=64) for s in range(2)]
+        for s in range(2):
+            nc.sync.dma_start(wv_raw[s][:], wv.rearrange("(p k) m -> p k m", k=PACK)[:, :, s * HALF : (s + 1) * HALF])
+        x_bytes = [placed[:, g * PASS : (g + 1) * PASS].rearrange("p (j n) -> p j n", j=PACK) for g in range(PASSES)]
+        e_bytes = placed[:, S:]
 
-        total = [tile(f"total{g}", [P, PACK], F32) for g in range(PASSES)]
-        factors = [
-            front.tile([P, PACK, 2], F32, name="factors0", offset=5 * RAW, align_bytes=64),
-            tile("factors1", [P, PACK, 2], F32),
-        ]
-        weight = tile("weight", [P, PASSES, PACK], F32)
-        for g in range(PASSES):
-            nc.scalar.copy(factors[g][:, :, 1], mask_t[:, g, :PACK])
+        def pick_words(g, tag=None):
+            codes = tile(f"x_codes{g}", [P, PACK, P], U32, tag)
+            entries = offs_t[:, g * PASS // 16 : (g + 1) * PASS // 16]
+            nc.vector.tensor_copy(codes[:].rearrange("p j n -> p n j"), xw[:].bitcast(U32).indirect(entries))
+            return codes
 
-        def scores(g, hands, tag):
-            neg_max = tile(f"neg_max{g}{hands[0]}", [P, PACK], F32, tag)
-            for j in hands:
-                y = bank(PACK * g + j, [P, V], f"y{g}{j}")
-                nc.tensor.matmul_mx(
-                    out=y[:], lhsT=x_codes[g][:, j, :].bitcast(FP8X4), lhsT_scale=x_bytes[g][:, j, :],
-                    rhs=e_codes[:].bitcast(FP8X4), rhs_scale=e_bytes, start=True, stop=True,
-                )
-                nc.vector.tensor_reduce(neg_max[:, j : j + 1], y[:], AX.X, ALU.max, negate=True)
-                nc.scalar.activation(
-                    ex[g][:, j, :], y[:], ACT.Exp, bias=neg_max[:, j : j + 1], accum_out=total[g][:, j : j + 1]
-                )
-
-        def pick_words(g):
-            nc.vector.tensor_copy(x_codes[g][:].rearrange("p j n -> p n j"), xw[:].bitcast(U32).indirect(entries(g)))
-
-        def weights(g):
-            nc.vector.reciprocal(factors[g][:, :, 0], total[g][:])
-            nc.vector.tensor_reduce(weight[:, g, :], factors[g][:], AX.X, ALU.mult)
-
-        HALF = V // 2
-        LEFT, RIGHT = 0, 1
-        ROUNDED = HALF * PACK * 2
-        wv_bf = [
-            tile("wv_bf0", [P, HALF * PACK], BF16, "last_max"),
-            front.tile([P, HALF * PACK], BF16, name="wv_bf1", offset=4 * RAW + ROUNDED // 2, align_bytes=64),
-        ]
-        wv_codes = [tile(f"wv_codes{s}", [P, HALF], U32) for s in range(2)]
-        wv_bytes = [tile(f"wv_bytes{s}", [P, HALF], U8) for s in range(2)]
-        h_bytes = [tile(f"h_bytes{g}", [P, N], U8) for g in range(PASSES)]
-        right_codes = [tile(f"right_codes{g}", [P, HALF], U32) for g in range(PASSES)]
-        right_bytes = [tile(f"right_bytes{g}", [P, HALF], U8) for g in range(PASSES)]
-        left_codes = [tile(f"left_codes{c}", [P, PASSES * CHUNK], U32) for c in range(2)]
-        left_bytes = [tile(f"left_bytes{c}", [P, PASSES * CHUNK], U8) for c in range(2)]
-
-        def round_wv(s):
-            nc.scalar.copy(weave_out(wv_bf[s][:]), weave_in(wv_raw[s][:]))
-
-        def quant(codes, scales, values):
-            nc.vector.quantize_mx(codes[:].bitcast(FP8X4), scales[:], values[:])
-
-        def h_product(out, g, t, s, cols):
-            nc.tensor.matmul_mx(
-                out=out, lhsT=x_codes[g][:, t, :].bitcast(FP8X4), lhsT_scale=x_bytes[g][:, t, :],
-                rhs=wv_codes[s][:, cols].bitcast(FP8X4), rhs_scale=wv_bytes[s][:, cols], start=True, stop=True,
-            )
-
-        def h_on_vector(g, s, first_bank):
-            for u in range(2):
-                hb = bank(first_bank + u, [P, PACK, CHUNK], f"h{g}{s}{u}")
-                for t in range(PACK):
-                    h_product(hb[:, t, :], g, t, s, slice(u * CHUNK, (u + 1) * CHUNK))
-                nc.vector.tensor_tensor(
-                    h_bf[g][:].rearrange("p (j c m t) -> p c j m t", j=PACK, c=CHUNKS, t=PACK)[:, 2 * s + u],
-                    hb[:].rearrange("p t (m j) -> p j m t", j=PACK),
-                    inv_t[:, g, :PACK].unsqueeze(1).unsqueeze(1).to_broadcast([P, PACK, CHUNK // PACK, PACK]),
-                    ALU.mult,
-                )
-
-        def h_on_scalar(g, s, first_bank):
-            h_planes = tile("h_planes", [P, PACK, HALF], BF16, "last_max")
-            for u in range(2):
-                hb = bank(first_bank + u, [P, 2, HALF], f"h{g}{s}{u}")
-                for t in range(2):
-                    h_product(hb[:, t, :], g, 2 * u + t, s, slice(0, HALF))
-                for t in range(2):
-                    nc.scalar.activation(h_planes[:, 2 * u + t, :].rearrange("p (j m) -> p j m", j=PACK), hb[:, t, :].rearrange("p (m j) -> p j m", j=PACK), ACT.Copy, scale=inv_t[:, g, 2 * u + t : 2 * u + t + 1])
-            nc.scalar.copy(
-                h_bf[g][:].rearrange("p (j s c i t) -> p s j c t i", j=PACK, s=2, i=2, t=PACK)[:, s],
-                h_planes[:].rearrange("p t (j c i) -> p j c t i", j=PACK, i=2),
-            )
-
-        def a_piece(g, c):
-            if c < 2:
-                return left_bf[c][:, g * CHUNK * PACK : (g + 1) * CHUNK * PACK]
-            return right_bf[g][:, (c - 2) * CHUNK * PACK : (c - 1) * CHUNK * PACK]
-
-        def a_on_scalar(g):
-            planes = tile("a_planes", [P, PACK, V - CHUNK], BF16, "last_max")
-            for j in range(PACK):
-                nc.scalar.activation(planes[:, j, :], ex[g][:, j, CHUNK:], ACT.Copy, scale=weight[:, g, j : j + 1])
-            nc.scalar.copy(weave_out(right_bf[g][:]), weave_in(planes[:, :, CHUNK:]))
-            nc.scalar.copy(weave_out(a_piece(g, 1)), weave_in(planes[:, :, :CHUNK]))
-
-        def a_on_vector(g, c):
-            weigh(nc.vector, g, c)
-
-        def weigh(engine, g, c):
-            cols = slice(c * CHUNK, (c + 1) * CHUNK)
-            engine.tensor_tensor(weave_out(a_piece(g, c)), weave_in(ex[g][:, :, cols]), spread(weight[:, g, :], CHUNK), ALU.mult)
-
-        round_wv(0)
-        x_codes = [tile("x_codes0", [P, PACK, P], U32)]
-        pick_words(0)
+        x_codes = [pick_words(0)]
         e_codes = tile("e_codes", [P, V], U32, "slots")
         nc.vector.tensor_copy(e_codes[:], ew[:].bitcast(U32).indirect(slot_t[:]))
-        x_codes.append(tile("x_codes1", [P, PACK, P], U32, "slot_words"))
-        pick_words(1)
-        ex = [front.tile([P, PACK, V], F32, name="ex0", offset=0, align_bytes=64)]
-        scores(0, (0, 1, 2, 3), None)
-        quant(wv_codes[0], wv_bytes[0], wv_bf[0])
-        round_wv(1)
-        quant(wv_codes[1], wv_bytes[1], wv_bf[1])
-        weights(0)
-        ex.append(front.tile([P, PACK, V], F32, name="ex1", offset=2 * RAW, align_bytes=64))
-        scores(1, (0, 1, 2, 3), "last_max")
-        weights(1)
-        right_bf = [
-            front.tile([P, HALF * PACK], BF16, name="right_bf0", offset=4 * RAW, align_bytes=64),
-            tile("right_bf1", [P, HALF * PACK], BF16),
-        ]
-        h_bf = [
-            front.tile([P, N * PACK], BF16, name="h_bf0", offset=4 * RAW + ROUNDED, align_bytes=64),
-            tile("h_bf1", [P, N * PACK], BF16),
-        ]
-        for c in (2, 3):
-            nc.gpsimd.tensor_tensor(
-                a_piece(0, c).rearrange("p (n j) -> p n j", j=PACK),
-                ex[0][:, :, c * CHUNK : (c + 1) * CHUNK].rearrange("p j n -> p n j"),
-                weight[:, 0, :].unsqueeze(1).to_broadcast([P, CHUNK, PACK]),
+        x_codes.append(pick_words(1, "ew"))
+
+        wv_bf = tile("wv_bf", [P, N * PACK], BF16)
+        for s in range(2):
+            nc.gpsimd.tensor_scalar(
+                wv_bf[:, s * HALF * PACK : (s + 1) * HALF * PACK].rearrange("p (n k) -> p n k", k=PACK),
+                wv_raw[s][:].rearrange("p k n -> p n k"), 1.0, 0.0, ALU.mult, ALU.add,
+            )
+        ex = [front.tile([P, PACK, V], F32, name=f"ex{g}", offset=(2 + 2 * g) * RAW, align_bytes=64) for g in range(PASSES)]
+
+        def score(g, j, neg_max=None):
+            if neg_max is None:
+                neg_max = tile(f"neg_max{g}{j}", [P, 1], F32)[:]
+            y = bank(PACK * g + j, [P, V], f"y{g}{j}")
+            product(y[:], x_codes[g][:, j, :], x_bytes[g][:, j, :], e_codes[:], e_bytes)
+            nc.vector.tensor_reduce(neg_max, y[:], AX.X, ALU.max, negate=True)
+            nc.scalar.activation(ex[g][:, j, :], y[:], ACT.Exp, bias=neg_max, accum_out=total[g][:, j : j + 1])
+
+        def weigh_rows(g, tag=None):
+            weight = tile(f"weight{g}", [P, PACK], F32, tag)
+            nc.vector.tensor_reduce(weight[:], factors[g][:, :, :2], AX.X, ALU.mult)
+            return weight
+
+        score(0, 0)
+        for j in range(1, PACK):
+            score(0, j)
+        wv_codes = tile("wv_codes", [P, N], U32)
+        wv_bytes = tile("wv_bytes", [P, N], U8)
+        quant(wv_codes[:], wv_bytes[:], wv_bf[:])
+        nc.vector.reciprocal(factors[0][:, :, 0], total[0][:])
+        weight = [weigh_rows(0, "wv_bf")]
+        score(1, 0)
+        late_max = front.tile([P, PACK], F32, name="late_max", offset=H_AT[0] - 64)
+        for j in range(1, PACK):
+            score(1, j, late_max[:, j : j + 1])
+        nc.vector.reciprocal(factors[1][:, :, 0], total[1][:])
+        weight.append(weigh_rows(1))
+
+        a_bf = [tile(f"a_bf{g}", [P, V * PACK], BF16) for g in range(PASSES)]
+        h_bf = [front.tile([P, N * PACK], BF16, name=f"h_bf{g}", offset=H_AT[g], align_bytes=64) for g in range(PASSES)]
+
+        def woven(values, cols):
+            return values[:, cols.start * PACK : cols.stop * PACK]
+
+        nc.gpsimd.tensor_tensor(
+            a_bf[0][:].rearrange("p (n j) -> p n j", j=PACK),
+            ex[0][:].rearrange("p j n -> p n j"),
+            weight[0][:].unsqueeze(1).to_broadcast([P, V, PACK]),
+            ALU.mult,
+        )
+
+        def h_product(g, c, b):
+            hb = bank(b, [P, PACK, CHUNK], f"h{g}{c}")
+            cols = slice(c * CHUNK, (c + 1) * CHUNK)
+            for t in range(PACK):
+                product(hb[:, t, :], x_codes[g][:, t, :], x_bytes[g][:, t, :], wv_codes[:, cols], wv_bytes[:, cols])
+            return hb
+
+        def h_on_vector(g, c, hb):
+            nc.vector.tensor_tensor(
+                h_bf[g][:].rearrange("p (j c m t) -> p c j m t", j=PACK, c=CHUNKS, t=PACK)[:, c],
+                hb[:].rearrange("p t (m j) -> p j m t", j=PACK),
+                inv_t[:, g, :PACK].unsqueeze(1).unsqueeze(1).to_broadcast([P, PACK, CHUNK // PACK, PACK]),
                 ALU.mult,
             )
-        h_on_vector(0, 0, 0)
-        h_on_scalar(1, 0, 2)
-        h_on_vector(0, 1, 4)
-        h_on_vector(1, 1, 6)
-        h_codes = [tile("h_codes0", [P, N], U32, "wv_codes1"), tile("h_codes1", [P, N], U32)]
-        left_bf = [tile(f"left_bf{c}", [P, PASSES * CHUNK * PACK], BF16, tag) for c, tag in enumerate(("wv_bytes1", "slot_words"))]
-        a_on_scalar(1)
 
-        def multiply(out, g, j, codes, scales):
-            rows = slice(j * P, (j + 1) * P)
-            nc.tensor.matmul_mx(
-                out=out, lhsT=h_codes[g][:, rows].bitcast(FP8X4), lhsT_scale=h_bytes[g][:, rows],
-                rhs=codes.bitcast(FP8X4), rhs_scale=scales, start=(g == 0), stop=(g == PASSES - 1),
+        def h_on_scalar(g, c, b):
+            hb = h_product(g, c, b)
+            h_planes = front.tile([P, PACK, CHUNK], BF16, name="h_planes", offset=H_AT[0] - 1024)
+            for t in range(PACK):
+                nc.scalar.activation(
+                    h_planes[:, t, :].rearrange("p (j m) -> p j m", j=PACK), hb[:, t, :].rearrange("p (m j) -> p j m", j=PACK),
+                    ACT.Copy, scale=inv_t[:, g, t : t + 1],
+                )
+            nc.scalar.copy(
+                h_bf[g][:].rearrange("p (j c m i t) -> p c j m t i", j=PACK, c=CHUNKS, i=2, t=PACK)[:, c],
+                h_planes[:].rearrange("p t (j m i) -> p j m t i", j=PACK, i=2),
             )
 
+        h_on_vector(0, 0, h_product(0, 0, 0))
+        h_on_vector(0, 1, h_product(0, 1, 1))
+        h_on_scalar(0, 3, 3)
+        planes = front.tile([P, PACK, V], BF16, name="planes", offset=6 * RAW)
+        for j in range(PACK):
+            nc.scalar.activation(planes[:, j, :], ex[1][:, j, :], ACT.Copy, scale=weight[1][:, j : j + 1])
+        for s in range(2):
+            cols = slice(s * HALF, (s + 1) * HALF)
+            nc.scalar.copy(weave_out(woven(a_bf[1], cols)), weave_in(planes[:, :, cols]))
+        for c, b in enumerate((2, 0, 1, 2)):
+            h_on_vector(1, c, h_product(1, c, b))
+        h_on_vector(0, 2, h_product(0, 2, 0))
+        spare = bank(1, [P, N], "spare")
+        for u in range(2):
+            product(spare[:], wv_codes[:, :P], wv_bytes[:, :P], wv_codes[:], wv_bytes[:])
+
+        h_codes = [front.tile([P, N], U32, name="h_codes0", offset=CODES_AT, align_bytes=64), tile("h_codes1", [P, N], U32)]
+        h_bytes = [tile(f"h_bytes{g}", [P, N], U8) for g in range(PASSES)]
+        a_codes = [front.tile([P, V], U32, name="a_codes0", offset=CODES_AT - V * 4, align_bytes=64), tile("a_codes1", [P, V], U32)]
+        a_bytes = [tile(f"a_bytes{g}", [P, V], U8) for g in range(PASSES)]
         out_codes = tile("out_codes", [P, V], U32)
         out_bytes = tile("out_bytes", [P, V], U8)
-        out_wide = tile("out_wide", [P, V * PACK], BF16)
-        right_f = tile("right_f", [P, PACK, HALF], F32)
-        left_f = [tile(f"left_f{c}", [P, PACK, CHUNK], F32) for c in range(2)]
+        out_bf = tile("out_bf", [P, V * PACK], BF16)
         out_rows = out_0.rearrange("(p j) v -> p j v", j=PACK)
-        right_acc = [bank(j, [P, HALF], f"right_acc{j}") for j in range(PACK)]
 
-        def right_pass(g):
-            quant(right_codes[g], right_bytes[g], right_bf[g])
+        pieces = [(slice(0, HALF), (4, 5)), (slice(HALF, 3 * CHUNK), (6,)), (slice(3 * CHUNK, V), (7, 3))]
+        accs = [
+            [bank(b, [P, PACK // len(banks), cols.stop - cols.start], f"acc{b}") for b in banks] for cols, banks in pieces
+        ]
+        out_f = [tile(f"out_f{i}", [P, PACK, cols.stop - cols.start], F32) for i, (cols, banks) in enumerate(pieces)]
+
+        def multiply(i, g):
+            cols, banks = pieces[i]
+            share = PACK // len(banks)
             for j in range(PACK):
-                multiply(right_acc[j][:], g, j, right_codes[g][:], right_bytes[g][:])
+                rows = slice(j * P, (j + 1) * P)
+                product(
+                    accs[i][j // share][:, j % share, :], h_codes[g][:, rows], h_bytes[g][:, rows], a_codes[g][:, cols], a_bytes[g][:, cols],
+                    start=(g == 0 and j % share == 0), stop=(g == PASSES - 1 and j % share == share - 1),
+                )
 
-        def left_product(c, banks):
-            quant(left_codes[c], left_bytes[c], left_bf[c])
-            accs = [bank(b, [P, PACK, CHUNK], f"left_acc{b}") for b in banks]
-            share = PACK // len(accs)
-            for j in range(PACK):
-                for g in range(PASSES):
-                    cols = slice(g * CHUNK, (g + 1) * CHUNK)
-                    multiply(accs[j // share][:, j, :], g, j, left_codes[c][:, cols], left_bytes[c][:, cols])
-            for acc, copy, first in zip(accs, (nc.scalar.copy, nc.vector.tensor_copy), (0, share)):
-                copy(left_f[c][:, first : first + share, :], acc[:, first : first + share, :])
-            nc.sync.dma_start(out_rows[:, :, c * CHUNK : (c + 1) * CHUNK], left_f[c][:])
+        def quant_a(g, cols):
+            quant(a_codes[g][:, cols], a_bytes[g][:, cols], woven(a_bf[g], cols))
 
-        def weave(c, copy):
-            planes = left_f[c][:] if c < 2 else right_f[:, :, (c - 2) * CHUNK : (c - 1) * CHUNK]
-            copy(weave_out(out_wide[:, c * CHUNK * PACK : (c + 1) * CHUNK * PACK]), weave_in(planes))
+        def copy_out(i, u, copy):
+            share = PACK // len(pieces[i][1])
+            copy(out_f[i][:, u * share : (u + 1) * share, :], accs[i][u][:])
 
-        def hand_on(s):
-            cols = slice(s * HALF, (s + 1) * HALF)
-            nc.vector.quantize_mx(out_codes[:, cols].bitcast(FP8X4), out_bytes[:, cols], out_wide[:, s * HALF * PACK : (s + 1) * HALF * PACK])
+        def store(i, hands):
+            nc.sync.dma_start(out_rows[:, hands, pieces[i][0]], out_f[i][:, hands, :])
+
+        def weave(i, copy):
+            copy(weave_out(woven(out_bf, pieces[i][0])), weave_in(out_f[i][:]))
+
+        def hand_on(cols):
+            quant(out_codes[:, cols], out_bytes[:, cols], woven(out_bf, cols))
             nc.sync.dma_start(out_1[0].rearrange("p n t -> p (n t)").bitcast(I32)[:, cols], out_codes[:, cols].bitcast(I32))
 
-        quant(h_codes[0], h_bytes[0], h_bf[0])
-        spare = bank(7, [P, N], "spare")
-        for u in range(2):
-            nc.tensor.matmul_mx(
-                out=spare[:], lhsT=h_codes[0][:, :P].bitcast(FP8X4), lhsT_scale=h_bytes[0][:, :P],
-                rhs=h_codes[0][:].bitcast(FP8X4), rhs_scale=h_bytes[0][:], start=True, stop=True,
-            )
-        a_on_vector(0, 0)
-        a_on_vector(1, 0)
-        right_pass(0)
-        quant(h_codes[1], h_bytes[1], h_bf[1])
-        left_product(0, (4,))
-        a_on_vector(0, 1)
-        right_pass(1)
-        for j in range(PACK):
-            nc.scalar.copy(right_f[:, j, :], right_acc[j][:])
-            if j % 2 == 1:
-                nc.sync.dma_start(out_rows[:, j - 1 : j + 1, HALF:], right_f[:, j - 1 : j + 1, :])
-        left_product(1, (5, 6))
+        left, right = slice(0, HALF), slice(HALF, V)
+        quant_a(0, left)
+        quant(h_codes[0][:], h_bytes[0][:], h_bf[0][:])
+        multiply(0, 0)
+        quant(h_codes[1][:], h_bytes[1][:], h_bf[1][:])
+        quant_a(1, left)
+        multiply(0, 1)
+        quant_a(0, right)
+        multiply(1, 0)
+        multiply(2, 0)
+        quant_a(1, right)
+        multiply(1, 1)
+        multiply(2, 1)
+        for u, copy in enumerate((nc.scalar.copy, nc.vector.tensor_copy)):
+            copy_out(0, u, copy)
+            store(0, slice(2 * u, 2 * u + 2))
+        copy_out(1, 0, nc.scalar.copy)
+        store(1, slice(0, PACK))
+        copy_out(2, 0, nc.scalar.copy)
+        copy_out(2, 1, nc.scalar.copy)
+        store(2, slice(0, PACK))
         weave(0, nc.vector.tensor_copy)
-        weave(2, nc.vector.tensor_copy)
-        weave(3, nc.scalar.copy)
+        hand_on(left)
         weave(1, nc.vector.tensor_copy)
-        hand_on(RIGHT)
-        hand_on(LEFT)
+        weave(2, nc.vector.tensor_copy)
+        hand_on(right)
         for q in range(QUADS):
             nc.scalar.dma_start(out_2[0, 4 * q : 4 * q + 4, :].bitcast(I32), out_bytes[32 * q : 32 * q + 4, :].bitcast(I32))

@@ -66,8 +66,7 @@ def tile_picked_yslot_soft_po_kernel(tc, x_words, x_scales, e_words, e_scales, m
         es = tile("es", [P, W], U8)
         placed = tile("placed", [P, S + V], U8)
         RAW = PACK * HALF * 4
-        CODES_AT = 10 * RAW
-        inv_t = front.tile([P, PASSES, 2 * PACK], F32, name="inv_t", offset=CODES_AT - 32)
+        inv_t = tile("inv_t", [P, PASSES, 2 * PACK], F32)
         mask_t = tile("mask_t", [P, PASSES, 2 * PACK], F32)
 
         nc.vector.memset(es[:ROW0, :].bitcast(I32), 0)
@@ -104,7 +103,7 @@ def tile_picked_yslot_soft_po_kernel(tc, x_words, x_scales, e_words, e_scales, m
                 placed[32 * q : 32 * q + 4, :].bitcast(I32),
                 staged[ROW0 + 4 * q : ROW0 + 4 * q + 4, :].bitcast(I32),
             )
-        wv_raw = [front.tile([P, PACK, HALF], F32, name=f"wv_raw{s}", offset=s * RAW, align_bytes=64) for s in range(2)]
+        wv_raw = [front.tile([P, PACK, HALF], F32, name=f"wv_raw{s}", offset=(1 - s) * RAW, align_bytes=64) for s in range(2)]
         for s in range(2):
             nc.sync.dma_start(wv_raw[s][:], wv.rearrange("(p k) m -> p k m", k=PACK)[:, :, s * HALF : (s + 1) * HALF])
         x_bytes = [placed[:, g * PASS : (g + 1) * PASS].rearrange("p (j n) -> p j n", j=PACK) for g in range(PASSES)]
@@ -122,12 +121,12 @@ def tile_picked_yslot_soft_po_kernel(tc, x_words, x_scales, e_words, e_scales, m
         x_codes.append(pick_words(1, "ew"))
 
         wv_bf = tile("wv_bf", [P, N * PACK], BF16)
-        for s in range(2):
-            nc.gpsimd.tensor_scalar(
-                wv_bf[:, s * HALF * PACK : (s + 1) * HALF * PACK].rearrange("p (n k) -> p n k", k=PACK),
-                wv_raw[s][:].rearrange("p k n -> p n k"), 1.0, 0.0, ALU.mult, ALU.add,
-            )
-        ex = [front.tile([P, PACK, V], F32, name=f"ex{g}", offset=(2 + 2 * g) * RAW, align_bytes=64) for g in range(PASSES)]
+        nc.scalar.copy(weave_out(wv_bf[:, : HALF * PACK]), weave_in(wv_raw[0][:]))
+        nc.gpsimd.tensor_scalar(
+            wv_bf[:, HALF * PACK :].rearrange("p (n k) -> p n k", k=PACK),
+            wv_raw[1][:].rearrange("p k n -> p n k"), 1.0, 0.0, ALU.mult, ALU.add,
+        )
+        ex = [front.tile([P, PACK, V], F32, name=f"ex{g}", offset=(1 + 2 * g) * RAW, align_bytes=64) for g in range(PASSES)]
 
         def score(g, j, neg_max=None):
             if neg_max is None:
@@ -145,14 +144,15 @@ def tile_picked_yslot_soft_po_kernel(tc, x_words, x_scales, e_words, e_scales, m
         score(0, 0)
         for j in range(1, PACK):
             score(0, j)
-        wv_codes = tile("wv_codes", [P, N], U32)
+        wv_codes = tile("wv_codes", [P, N], U32, "neg_max02")
         wv_bytes = tile("wv_bytes", [P, N], U8)
         quant(wv_codes[:], wv_bytes[:], wv_bf[:])
         nc.vector.reciprocal(factors[0][:, :, 0], total[0][:])
         weight = [weigh_rows(0, "wv_bf")]
         score(1, 0)
+        score(1, 1)
         late_max = front.tile([P, PACK], F32, name="late_max", offset=H_AT[0] - 64)
-        for j in range(1, PACK):
+        for j in range(2, PACK):
             score(1, j, late_max[:, j : j + 1])
         nc.vector.reciprocal(factors[1][:, :, 0], total[1][:])
         weight.append(weigh_rows(1))
@@ -163,10 +163,11 @@ def tile_picked_yslot_soft_po_kernel(tc, x_words, x_scales, e_words, e_scales, m
         def woven(values, cols):
             return values[:, cols.start * PACK : cols.stop * PACK]
 
+        left, right = slice(0, HALF), slice(HALF, V)
         nc.gpsimd.tensor_tensor(
-            a_bf[0][:].rearrange("p (n j) -> p n j", j=PACK),
-            ex[0][:].rearrange("p j n -> p n j"),
-            weight[0][:].unsqueeze(1).to_broadcast([P, V, PACK]),
+            woven(a_bf[0], left).rearrange("p (n j) -> p n j", j=PACK),
+            ex[0][:, :, left].rearrange("p j n -> p n j"),
+            weight[0][:].unsqueeze(1).to_broadcast([P, HALF, PACK]),
             ALU.mult,
         )
 
@@ -185,45 +186,38 @@ def tile_picked_yslot_soft_po_kernel(tc, x_words, x_scales, e_words, e_scales, m
                 ALU.mult,
             )
 
-        def h_on_scalar(g, c, b):
-            hb = h_product(g, c, b)
-            h_planes = front.tile([P, PACK, CHUNK], BF16, name="h_planes", offset=H_AT[0] - 1024)
-            for t in range(PACK):
-                nc.scalar.activation(
-                    h_planes[:, t, :].rearrange("p (j m) -> p j m", j=PACK), hb[:, t, :].rearrange("p (m j) -> p j m", j=PACK),
-                    ACT.Copy, scale=inv_t[:, g, t : t + 1],
-                )
-            nc.scalar.copy(
-                h_bf[g][:].rearrange("p (j c m i t) -> p c j m t i", j=PACK, c=CHUNKS, i=2, t=PACK)[:, c],
-                h_planes[:].rearrange("p t (j m i) -> p j m t i", j=PACK, i=2),
-            )
+        def scale_planes(planes, g, cols):
+            for j in range(PACK):
+                nc.scalar.activation(planes[:, j, :], ex[g][:, j, cols], ACT.Copy, scale=weight[g][:, j : j + 1])
 
         h_on_vector(0, 0, h_product(0, 0, 0))
-        h_on_vector(0, 1, h_product(0, 1, 1))
-        h_on_scalar(0, 3, 3)
-        planes = front.tile([P, PACK, V], BF16, name="planes", offset=6 * RAW)
-        for j in range(PACK):
-            nc.scalar.activation(planes[:, j, :], ex[1][:, j, :], ACT.Copy, scale=weight[1][:, j : j + 1])
-        for s in range(2):
-            cols = slice(s * HALF, (s + 1) * HALF)
-            nc.scalar.copy(weave_out(woven(a_bf[1], cols)), weave_in(planes[:, :, cols]))
-        for c, b in enumerate((2, 0, 1, 2)):
-            h_on_vector(1, c, h_product(1, c, b))
-        h_on_vector(0, 2, h_product(0, 2, 0))
-        spare = bank(1, [P, N], "spare")
-        for u in range(2):
-            product(spare[:], wv_codes[:, :P], wv_bytes[:, :P], wv_codes[:], wv_bytes[:])
+        h_on_vector(0, 1, h_product(0, 1, 6))
+        planes0 = front.tile([P, PACK, HALF], BF16, name="planes0", offset=H_AT[0] - HALF * PACK * 2)
+        scale_planes(planes0, 0, right)
+        nc.gpsimd.tensor_scalar(
+            woven(a_bf[0], right).rearrange("p (n j) -> p n j", j=PACK),
+            planes0[:].rearrange("p j n -> p n j"), 1.0, 0.0, ALU.mult, ALU.add,
+        )
+        planes1 = tile("planes1", [P, PACK, V], BF16)
+        scale_planes(planes1, 1, slice(0, V))
+        for cols in (left, right):
+            nc.scalar.copy(weave_out(woven(a_bf[1], cols)), weave_in(planes1[:, :, cols]))
+        h_on_vector(0, 2, h_product(0, 2, 7))
+        h_on_vector(0, 3, h_product(0, 3, 6))
+        h_on_vector(1, 0, h_product(1, 0, 1))
+        h_on_vector(1, 1, h_product(1, 1, 2))
+        late_h = [h_product(1, 2, 3), h_product(1, 3, 1)]
 
-        h_codes = [front.tile([P, N], U32, name="h_codes0", offset=CODES_AT, align_bytes=64), tile("h_codes1", [P, N], U32)]
+        h_codes = [tile("h_codes0", [P, N], U32, "wv_bytes"), tile("h_codes1", [P, N], U32)]
         h_bytes = [tile(f"h_bytes{g}", [P, N], U8) for g in range(PASSES)]
-        a_codes = [front.tile([P, V], U32, name="a_codes0", offset=CODES_AT - V * 4, align_bytes=64), tile("a_codes1", [P, V], U32)]
+        a_codes = [tile("a_codes0", [P, V], U32, "neg_max02"), tile("a_codes1", [P, V], U32)]
         a_bytes = [tile(f"a_bytes{g}", [P, V], U8) for g in range(PASSES)]
         out_codes = tile("out_codes", [P, V], U32)
         out_bytes = tile("out_bytes", [P, V], U8)
         out_bf = tile("out_bf", [P, V * PACK], BF16)
         out_rows = out_0.rearrange("(p j) v -> p j v", j=PACK)
 
-        pieces = [(slice(0, HALF), (4, 5)), (slice(HALF, 3 * CHUNK), (6,)), (slice(3 * CHUNK, V), (7, 3))]
+        pieces = [(slice(0, HALF), (4, 5)), (slice(HALF, 3 * CHUNK), (7,)), (slice(3 * CHUNK, V), (6,))]
         accs = [
             [bank(b, [P, PACK // len(banks), cols.stop - cols.start], f"acc{b}") for b in banks] for cols, banks in pieces
         ]
@@ -256,31 +250,32 @@ def tile_picked_yslot_soft_po_kernel(tc, x_words, x_scales, e_words, e_scales, m
             quant(out_codes[:, cols], out_bytes[:, cols], woven(out_bf, cols))
             nc.sync.dma_start(out_1[0].rearrange("p n t -> p (n t)").bitcast(I32)[:, cols], out_codes[:, cols].bitcast(I32))
 
-        left, right = slice(0, HALF), slice(HALF, V)
         quant_a(0, left)
         quant(h_codes[0][:], h_bytes[0][:], h_bf[0][:])
         multiply(0, 0)
+        h_on_vector(1, 2, late_h[0])
+        h_on_vector(1, 3, late_h[1])
         quant(h_codes[1][:], h_bytes[1][:], h_bf[1][:])
         quant_a(1, left)
         multiply(0, 1)
         quant_a(0, right)
         multiply(1, 0)
         multiply(2, 0)
+        copy_out(0, 0, nc.vector.tensor_copy)
+        store(0, slice(0, 2))
         quant_a(1, right)
         multiply(1, 1)
         multiply(2, 1)
-        for u, copy in enumerate((nc.scalar.copy, nc.vector.tensor_copy)):
-            copy_out(0, u, copy)
-            store(0, slice(2 * u, 2 * u + 2))
+        copy_out(0, 1, nc.scalar.copy)
+        store(0, slice(2, PACK))
         copy_out(1, 0, nc.scalar.copy)
         store(1, slice(0, PACK))
+        nc.vector.tensor_copy(woven(out_bf, pieces[2][0]).rearrange("p (n j) -> p n j", j=PACK), accs[2][0][:].rearrange("p j n -> p n j"))
         copy_out(2, 0, nc.scalar.copy)
-        copy_out(2, 1, nc.scalar.copy)
         store(2, slice(0, PACK))
         weave(0, nc.vector.tensor_copy)
         hand_on(left)
         weave(1, nc.vector.tensor_copy)
-        weave(2, nc.vector.tensor_copy)
         hand_on(right)
         for q in range(QUADS):
             nc.scalar.dma_start(out_2[0, 4 * q : 4 * q + 4, :].bitcast(I32), out_bytes[32 * q : 32 * q + 4, :].bitcast(I32))

@@ -66,8 +66,6 @@ def tile_picked_yslot_soft_po_kernel(tc, x_words, x_scales, e_words, e_scales, m
         es = tile("es", [P, W], U8)
         placed = tile("placed", [P, S + V], U8)
         RAW = PACK * HALF * 4
-        inv_t = tile("inv_t", [P, PASSES, 2 * PACK], F32)
-        mask_t = tile("mask_t", [P, PASSES, 2 * PACK], F32)
 
         nc.vector.memset(es[:ROW0, :].bitcast(I32), 0)
         nc.vector.memset(xs[:ROW0, :].bitcast(I32), 0)
@@ -77,20 +75,16 @@ def tile_picked_yslot_soft_po_kernel(tc, x_words, x_scales, e_words, e_scales, m
         nc.sync.dma_start(offs_t[:], offs)
         nc.sync.dma_start(xs[ROW0:, :].bitcast(I32), x_scales[0].bitcast(I32))
         nc.sync.dma_start(xw[:], x_words[0].rearrange("p n t -> p (n t)").bitcast(I32))
-        nc.scalar.dma_start(mask_t[:, :, :PACK], mask.rearrange("(g p j) o -> p g (j o)", p=P, j=PACK))
-        nc.scalar.dma_start(inv_t[:, :, :PACK], inv.rearrange("(g p j) o -> p g (j o)", p=P, j=PACK))
         nc.sync.dma_start(ew[:], e_words[0].rearrange("p n t -> p (n t)").bitcast(I32))
 
         WOVEN = N * PACK * 2
         H_AT = [7 * RAW + g * (WOVEN + 192) for g in range(PASSES)]
         total = [tile("total0", [P, PACK], F32), front.tile([P, PACK], F32, name="total1", offset=H_AT[1])]
         factors = [front.tile([P, PACK, 6], F32, name=f"factors{g}", offset=H_AT[g] - 64 - 64 * g) for g in range(PASSES)]
-        for g in range(PASSES):
-            nc.scalar.copy(factors[g][:, :, 1], mask_t[:, g, :PACK])
 
         e_picked = tile("e_picked", [P, V], U8, "slots")
-        x_picked = front.tile([P, S], U8, name="x_picked", offset=RAW - PASS, align_bytes=64)
-        staged = tile("staged", [P, S + V], U8, "tokens")
+        x_picked = front.tile([P, S], U8, name="x_picked", offset=RAW - PASS + 128, align_bytes=64)
+        staged = tile("staged", [P, S + V], U8)
         nc.vector.tensor_copy(e_picked[:], es[:].indirect(slot_t[:]))
         nc.vector.tensor_copy(x_picked[:], xs[:].indirect(offs_t[:]))
         nc.vector.tensor_copy(staged[:, S:].bitcast(I32), e_picked[:].bitcast(I32))
@@ -103,9 +97,13 @@ def tile_picked_yslot_soft_po_kernel(tc, x_words, x_scales, e_words, e_scales, m
                 placed[32 * q : 32 * q + 4, :].bitcast(I32),
                 staged[ROW0 + 4 * q : ROW0 + 4 * q + 4, :].bitcast(I32),
             )
-        wv_raw = [front.tile([P, PACK, HALF], F32, name=f"wv_raw{s}", offset=(1 - s) * RAW, align_bytes=64) for s in range(2)]
+        mask_t = front.tile([P, PASSES, 2 * PACK], F32, name="mask_t", offset=RAW)
+        nc.sync.dma_start(mask_t[:, :, :PACK], mask.rearrange("(g p j) o -> p g (j o)", p=P, j=PACK))
+        wv_raw = [front.tile([P, PACK, HALF], F32, name=f"wv_raw{s}", offset=(1 - s) * (RAW + 256), align_bytes=64) for s in range(2)]
         for s in range(2):
             nc.sync.dma_start(wv_raw[s][:], wv.rearrange("(p k) m -> p k m", k=PACK)[:, :, s * HALF : (s + 1) * HALF])
+        inv_t = front.tile([P, PASSES, 2 * PACK], F32, name="inv_t", offset=RAW + 64)
+        nc.sync.dma_start(inv_t[:, :, :PACK], inv.rearrange("(g p j) o -> p g (j o)", p=P, j=PACK))
         x_bytes = [placed[:, g * PASS : (g + 1) * PASS].rearrange("p (j n) -> p j n", j=PACK) for g in range(PASSES)]
         e_bytes = placed[:, S:]
 
@@ -121,12 +119,14 @@ def tile_picked_yslot_soft_po_kernel(tc, x_words, x_scales, e_words, e_scales, m
         x_codes.append(pick_words(1, "ew"))
 
         wv_bf = tile("wv_bf", [P, N * PACK], BF16)
+        for g in range(PASSES):
+            nc.scalar.copy(factors[g][:, :, 1], mask_t[:, g, :PACK])
         nc.scalar.copy(weave_out(wv_bf[:, : HALF * PACK]), weave_in(wv_raw[0][:]))
         nc.gpsimd.tensor_scalar(
             wv_bf[:, HALF * PACK :].rearrange("p (n k) -> p n k", k=PACK),
             wv_raw[1][:].rearrange("p k n -> p n k"), 1.0, 0.0, ALU.mult, ALU.add,
         )
-        ex = [front.tile([P, PACK, V], F32, name=f"ex{g}", offset=(1 + 2 * g) * RAW, align_bytes=64) for g in range(PASSES)]
+        ex = [front.tile([P, PACK, V], F32, name=f"ex{g}", offset=(1 + 2 * g) * RAW + 384, align_bytes=64) for g in range(PASSES)]
 
         def score(g, j, neg_max=None):
             if neg_max is None:
@@ -149,8 +149,8 @@ def tile_picked_yslot_soft_po_kernel(tc, x_words, x_scales, e_words, e_scales, m
         quant(wv_codes[:], wv_bytes[:], wv_bf[:])
         nc.vector.reciprocal(factors[0][:, :, 0], total[0][:])
         weight = [weigh_rows(0, "wv_bf")]
-        score(1, 0)
-        score(1, 1)
+        for j in range(2):
+            score(1, j, front.tile([P, 1], F32, name=f"neg_max1{j}", offset=RAW + 256 + 32 * j)[:])
         late_max = front.tile([P, PACK], F32, name="late_max", offset=H_AT[0] - 64)
         for j in range(2, PACK):
             score(1, j, late_max[:, j : j + 1])
@@ -254,13 +254,13 @@ def tile_picked_yslot_soft_po_kernel(tc, x_words, x_scales, e_words, e_scales, m
         quant(h_codes[0][:], h_bytes[0][:], h_bf[0][:])
         multiply(0, 0)
         h_on_vector(1, 2, late_h[0])
+        quant_a(0, right)
+        multiply(1, 0)
+        multiply(2, 0)
         h_on_vector(1, 3, late_h[1])
         quant(h_codes[1][:], h_bytes[1][:], h_bf[1][:])
         quant_a(1, left)
         multiply(0, 1)
-        quant_a(0, right)
-        multiply(1, 0)
-        multiply(2, 0)
         copy_out(0, 0, nc.vector.tensor_copy)
         store(0, slice(0, 2))
         quant_a(1, right)

@@ -148,14 +148,12 @@ def tile_picked_yslot_soft_po_kernel(tc, x_words, x_scales, e_words, e_scales, m
         wv_bytes = tile("wv_bytes", [P, N], U8)
         quant(wv_codes[:], wv_bytes[:], wv_bf[:])
         nc.vector.reciprocal(factors[0][:, :, 0], total[0][:])
-        weight = [weigh_rows(0, "wv_bf")]
         for j in range(2):
             score(1, j, front.tile([P, 1], F32, name=f"neg_max1{j}", offset=RAW + 256 + 32 * j)[:])
-        late_max = front.tile([P, PACK], F32, name="late_max", offset=H_AT[0] - 64)
-        for j in range(2, PACK):
-            score(1, j, late_max[:, j : j + 1])
+        score(1, 2, tile("neg_max12", [P, 1], F32, "total0")[:])
+        weight = [weigh_rows(0, "wv_bf")]
+        score(1, 3, front.tile([P, 1], F32, name="neg_max13", offset=H_AT[0] - 64)[:])
         nc.vector.reciprocal(factors[1][:, :, 0], total[1][:])
-        weight.append(weigh_rows(1))
 
         a_bf = [tile(f"a_bf{g}", [P, V * PACK], BF16) for g in range(PASSES)]
         h_bf = [front.tile([P, N * PACK], BF16, name=f"h_bf{g}", offset=H_AT[g], align_bytes=64) for g in range(PASSES)]
@@ -191,7 +189,9 @@ def tile_picked_yslot_soft_po_kernel(tc, x_words, x_scales, e_words, e_scales, m
                 nc.scalar.activation(planes[:, j, :], ex[g][:, j, cols], ACT.Copy, scale=weight[g][:, j : j + 1])
 
         h_on_vector(0, 0, h_product(0, 0, 0))
-        h_on_vector(0, 1, h_product(0, 1, 6))
+        h_on_vector(0, 1, h_product(0, 1, 1))
+        h_on_vector(1, 0, h_product(1, 0, 2))
+        weight.append(weigh_rows(1))
         planes0 = front.tile([P, PACK, HALF], BF16, name="planes0", offset=H_AT[0] - HALF * PACK * 2)
         scale_planes(planes0, 0, right)
         nc.gpsimd.tensor_scalar(
@@ -203,10 +203,9 @@ def tile_picked_yslot_soft_po_kernel(tc, x_words, x_scales, e_words, e_scales, m
         for cols in (left, right):
             nc.scalar.copy(weave_out(woven(a_bf[1], cols)), weave_in(planes1[:, :, cols]))
         h_on_vector(0, 2, h_product(0, 2, 7))
-        h_on_vector(0, 3, h_product(0, 3, 6))
-        h_on_vector(1, 0, h_product(1, 0, 1))
-        h_on_vector(1, 1, h_product(1, 1, 2))
-        late_h = [h_product(1, 2, 3), h_product(1, 3, 1)]
+        h_on_vector(1, 1, h_product(1, 1, 3))
+        h_on_vector(0, 3, h_product(0, 3, 7))
+        late_h = [h_product(1, 2, 0), h_product(1, 3, 3)]
 
         h_codes = [tile("h_codes0", [P, N], U32, "wv_bytes"), tile("h_codes1", [P, N], U32)]
         h_bytes = [tile(f"h_bytes{g}", [P, N], U8) for g in range(PASSES)]
@@ -217,7 +216,7 @@ def tile_picked_yslot_soft_po_kernel(tc, x_words, x_scales, e_words, e_scales, m
         out_bf = tile("out_bf", [P, V * PACK], BF16)
         out_rows = out_0.rearrange("(p j) v -> p j v", j=PACK)
 
-        pieces = [(slice(0, HALF), (4, 5)), (slice(HALF, 3 * CHUNK), (7,)), (slice(3 * CHUNK, V), (6,))]
+        pieces = [(slice(0, HALF), (4, 5, 7, 2)), (slice(HALF, 3 * CHUNK), (1,)), (slice(3 * CHUNK, V), (6,))]
         accs = [
             [bank(b, [P, PACK // len(banks), cols.stop - cols.start], f"acc{b}") for b in banks] for cols, banks in pieces
         ]
@@ -258,24 +257,23 @@ def tile_picked_yslot_soft_po_kernel(tc, x_words, x_scales, e_words, e_scales, m
         multiply(1, 0)
         multiply(2, 0)
         h_on_vector(1, 3, late_h[1])
-        quant(h_codes[1][:], h_bytes[1][:], h_bf[1][:])
         quant_a(1, left)
+        for rows in (slice(0, P), slice(P, HALF), right):
+            quant(h_codes[1][:, rows], h_bytes[1][:, rows], woven(h_bf[1], rows))
         multiply(0, 1)
-        copy_out(0, 0, nc.vector.tensor_copy)
-        store(0, slice(0, 2))
         quant_a(1, right)
         multiply(1, 1)
         multiply(2, 1)
-        copy_out(0, 1, nc.scalar.copy)
-        store(0, slice(2, PACK))
-        copy_out(1, 0, nc.scalar.copy)
-        store(1, slice(0, PACK))
-        nc.vector.tensor_copy(woven(out_bf, pieces[2][0]).rearrange("p (n j) -> p n j", j=PACK), accs[2][0][:].rearrange("p j n -> p n j"))
-        copy_out(2, 0, nc.scalar.copy)
-        store(2, slice(0, PACK))
+        for j in range(PACK):
+            copy_out(0, j, nc.scalar.copy)
+            store(0, slice(j, j + 1))
+        nc.vector.tensor_copy(woven(out_bf, pieces[1][0]).rearrange("p (n j) -> p n j", j=PACK), accs[1][0][:].rearrange("p j n -> p n j"))
+        for i in (2, 1):
+            copy_out(i, 0, nc.scalar.copy)
+            store(i, slice(0, PACK))
         weave(0, nc.vector.tensor_copy)
+        weave(2, nc.vector.tensor_copy)
         hand_on(left)
-        weave(1, nc.vector.tensor_copy)
         hand_on(right)
         for q in range(QUADS):
             nc.scalar.dma_start(out_2[0, 4 * q : 4 * q + 4, :].bitcast(I32), out_bytes[32 * q : 32 * q + 4, :].bitcast(I32))

@@ -23,6 +23,7 @@ PASSES = S // PASS
 QUADS = 4
 CHUNK = 128
 CHUNKS = V // CHUNK
+RUN = 8
 ROW0 = P - 16
 
 
@@ -74,59 +75,63 @@ def tile_picked_yslot_soft_po_kernel(tc, x_words, x_scales, e_words, e_scales, m
         nc.sync.dma_start(es[ROW0:, :].bitcast(I32), e_scales[0].bitcast(I32))
         nc.sync.dma_start(offs_t[:], offs)
         nc.sync.dma_start(xs[ROW0:, :].bitcast(I32), x_scales[0].bitcast(I32))
-        nc.sync.dma_start(xw[:], x_words[0].rearrange("p n t -> p (n t)").bitcast(I32))
         nc.sync.dma_start(ew[:], e_words[0].rearrange("p n t -> p (n t)").bitcast(I32))
+        nc.sync.dma_start(xw[:], x_words[0].rearrange("p n t -> p (n t)").bitcast(I32))
 
         WOVEN = N * PACK * 2
         H_AT = [7 * RAW + g * (WOVEN + 192) for g in range(PASSES)]
-        total = [tile("total0", [P, PACK], F32), front.tile([P, PACK], F32, name="total1", offset=H_AT[1])]
-        factors = [front.tile([P, PACK, 6], F32, name=f"factors{g}", offset=H_AT[g] - 64 - 64 * g) for g in range(PASSES)]
+        total = [front.tile([P, 24], F32, name="total0", offset=H_AT[0] - 64), front.tile([P, PACK], F32, name="total1", offset=H_AT[1])]
 
-        e_picked = tile("e_picked", [P, V], U8, "slots")
+        e_picked = front.tile([P, V], U8, name="e_picked", offset=10 * RAW, align_bytes=64)
         x_picked = front.tile([P, S], U8, name="x_picked", offset=RAW - PASS + 128, align_bytes=64)
         staged = tile("staged", [P, S + V], U8)
         nc.vector.tensor_copy(e_picked[:], es[:].indirect(slot_t[:]))
         nc.vector.tensor_copy(x_picked[:], xs[:].indirect(offs_t[:]))
+        for g in range(PASSES):
+            cols = slice(g * PASS, (g + 1) * PASS)
+            nc.vector.tensor_copy(
+                staged[:, cols].bitcast(I32).rearrange("p (j Q b q) -> p b Q j q", j=PACK, Q=QUADS, b=4),
+                x_picked[:, cols].bitcast(I32).rearrange("p (b Q j q) -> p b Q j q", j=PACK, Q=QUADS, b=4),
+            )
         nc.vector.tensor_copy(staged[:, S:].bitcast(I32), e_picked[:].bitcast(I32))
-        nc.vector.tensor_copy(
-            staged[:, :S].rearrange("p (g j n) -> p g j n", g=PASSES, j=PACK),
-            x_picked[:].rearrange("p (g n j) -> p g j n", g=PASSES, j=PACK),
-        )
         for q in (0, 2, 1, 3):
             nc.sync.dma_start(
                 placed[32 * q : 32 * q + 4, :].bitcast(I32),
                 staged[ROW0 + 4 * q : ROW0 + 4 * q + 4, :].bitcast(I32),
             )
-        mask_t = front.tile([P, PASSES, 2 * PACK], F32, name="mask_t", offset=RAW)
-        nc.sync.dma_start(mask_t[:, :, :PACK], mask.rearrange("(g p j) o -> p g (j o)", p=P, j=PACK))
-        wv_raw = [front.tile([P, PACK, HALF], F32, name=f"wv_raw{s}", offset=(1 - s) * (RAW + 256), align_bytes=64) for s in range(2)]
+        rows = front.tile([P, 2, PASSES * 32], F32, name="rows", offset=RAW, align_bytes=64)
+        nc.vector.memset(rows[:], 0.0)
+        for w, factor in enumerate((mask, inv)):
+            nc.sync.dma_start(
+                rows[0:P:RUN, w, :].rearrange("u (b q) -> u b q", q=RUN), factor.rearrange("(b u q) o -> u b (q o)", u=P // RUN, q=RUN)
+            )
+        wv_raw = [front.tile([P, PACK, HALF], F32, name=f"wv_raw{s}", offset=(1 - s) * (RAW + 576), align_bytes=64) for s in range(2)]
         for s in range(2):
             nc.sync.dma_start(wv_raw[s][:], wv.rearrange("(p k) m -> p k m", k=PACK)[:, :, s * HALF : (s + 1) * HALF])
-        inv_t = front.tile([P, PASSES, 2 * PACK], F32, name="inv_t", offset=RAW + 64)
-        nc.sync.dma_start(inv_t[:, :, :PACK], inv.rearrange("(g p j) o -> p g (j o)", p=P, j=PACK))
         x_bytes = [placed[:, g * PASS : (g + 1) * PASS].rearrange("p (j n) -> p j n", j=PACK) for g in range(PASSES)]
         e_bytes = placed[:, S:]
 
         def pick_words(g, tag=None):
             codes = tile(f"x_codes{g}", [P, PACK, P], U32, tag)
             entries = offs_t[:, g * PASS // 16 : (g + 1) * PASS // 16]
-            nc.vector.tensor_copy(codes[:].rearrange("p j n -> p n j"), xw[:].bitcast(U32).indirect(entries))
+            nc.vector.tensor_copy(codes[:].rearrange("p j (Q b q) -> p b Q j q", Q=QUADS, q=RUN), xw[:].bitcast(U32).indirect(entries))
             return codes
 
-        x_codes = [pick_words(0)]
-        e_codes = tile("e_codes", [P, V], U32, "slots")
+        e_codes = front.tile([P, V], U32, name="e_codes", offset=10 * RAW, align_bytes=64)
         nc.vector.tensor_copy(e_codes[:], ew[:].bitcast(U32).indirect(slot_t[:]))
-        x_codes.append(pick_words(1, "ew"))
+        x_codes = [pick_words(g) for g in range(PASSES)]
+        turned = tile("turned", [P, 2, PASSES, PACK, RUN], F32, "xw")
+        nc.vector.transpose(turned[:].rearrange("p w g j e -> p (w g j e)"), rows[:].rearrange("p w c -> p (w c)"))
+        inv_t = front.tile([P, PASSES, PACK], F32, name="inv_t", offset=0)
 
         wv_bf = tile("wv_bf", [P, N * PACK], BF16)
-        for g in range(PASSES):
-            nc.scalar.copy(factors[g][:, :, 1], mask_t[:, g, :PACK])
         nc.scalar.copy(weave_out(wv_bf[:, : HALF * PACK]), weave_in(wv_raw[0][:]))
         nc.gpsimd.tensor_scalar(
             wv_bf[:, HALF * PACK :].rearrange("p (n k) -> p n k", k=PACK),
             wv_raw[1][:].rearrange("p k n -> p n k"), 1.0, 0.0, ALU.mult, ALU.add,
         )
-        ex = [front.tile([P, PACK, V], F32, name=f"ex{g}", offset=(1 + 2 * g) * RAW + 384, align_bytes=64) for g in range(PASSES)]
+        nc.gpsimd.tensor_copy(inv_t[:], turned[:, 1, :, :, 0])
+        ex = [front.tile([P, PACK, V], F32, name=f"ex{g}", offset=(1 + 2 * g) * RAW + 704, align_bytes=64) for g in range(PASSES)]
 
         def score(g, j, neg_max=None):
             if neg_max is None:
@@ -138,7 +143,7 @@ def tile_picked_yslot_soft_po_kernel(tc, x_words, x_scales, e_words, e_scales, m
 
         def weigh_rows(g, tag=None):
             weight = tile(f"weight{g}", [P, PACK], F32, tag)
-            nc.vector.tensor_reduce(weight[:], factors[g][:, :, :2], AX.X, ALU.mult)
+            nc.vector.tensor_reduce(weight[:], turned[:, 0, g, :, :2], AX.X, ALU.mult)
             return weight
 
         score(0, 0)
@@ -147,13 +152,13 @@ def tile_picked_yslot_soft_po_kernel(tc, x_words, x_scales, e_words, e_scales, m
         wv_codes = tile("wv_codes", [P, N], U32, "neg_max02")
         wv_bytes = tile("wv_bytes", [P, N], U8)
         quant(wv_codes[:], wv_bytes[:], wv_bf[:])
-        nc.vector.reciprocal(factors[0][:, :, 0], total[0][:])
+        nc.vector.reciprocal(turned[:, 0, 0, :, 1], total[0][:, :PACK])
         for j in range(2):
-            score(1, j, front.tile([P, 1], F32, name=f"neg_max1{j}", offset=RAW + 256 + 32 * j)[:])
-        score(1, 2, tile("neg_max12", [P, 1], F32, "total0")[:])
+            score(1, j, front.tile([P, 1], F32, name=f"neg_max1{j}", offset=RAW + 576 + 32 * j)[:])
+        score(1, 2, front.tile([P, 1], F32, name="neg_max12", offset=H_AT[0] - 32)[:])
         weight = [weigh_rows(0, "wv_bf")]
         score(1, 3, front.tile([P, 1], F32, name="neg_max13", offset=H_AT[0] - 64)[:])
-        nc.vector.reciprocal(factors[1][:, :, 0], total[1][:])
+        nc.vector.reciprocal(turned[:, 0, 1, :, 1], total[1][:])
 
         a_bf = [tile(f"a_bf{g}", [P, V * PACK], BF16) for g in range(PASSES)]
         h_bf = [front.tile([P, N * PACK], BF16, name=f"h_bf{g}", offset=H_AT[g], align_bytes=64) for g in range(PASSES)]
@@ -180,7 +185,7 @@ def tile_picked_yslot_soft_po_kernel(tc, x_words, x_scales, e_words, e_scales, m
             nc.vector.tensor_tensor(
                 h_bf[g][:].rearrange("p (j c m t) -> p c j m t", j=PACK, c=CHUNKS, t=PACK)[:, c],
                 hb[:].rearrange("p t (m j) -> p j m t", j=PACK),
-                inv_t[:, g, :PACK].unsqueeze(1).unsqueeze(1).to_broadcast([P, PACK, CHUNK // PACK, PACK]),
+                inv_t[:, g, :].unsqueeze(1).unsqueeze(1).to_broadcast([P, PACK, CHUNK // PACK, PACK]),
                 ALU.mult,
             )
 

@@ -90,8 +90,8 @@ def tile_picked_yslot_soft_po_kernel(tc, x_words, x_scales, e_words, e_scales, m
         for g in range(PASSES):
             cols = slice(g * PASS, (g + 1) * PASS)
             nc.vector.tensor_copy(
-                staged[:, cols].bitcast(I32).rearrange("p (j Q b q) -> p b Q j q", j=PACK, Q=QUADS, b=4),
-                x_picked[:, cols].bitcast(I32).rearrange("p (b Q j q) -> p b Q j q", j=PACK, Q=QUADS, b=4),
+                staged[:, cols].bitcast(I32).rearrange("p (j Q b q) -> p j Q b q", j=PACK, Q=QUADS, b=4),
+                x_picked[:, cols].bitcast(I32).rearrange("p (b Q j q) -> p j Q b q", j=PACK, Q=QUADS, b=4),
             )
         nc.vector.tensor_copy(staged[:, S:].bitcast(I32), e_picked[:].bitcast(I32))
         for q in (0, 2, 1, 3):
@@ -153,10 +153,10 @@ def tile_picked_yslot_soft_po_kernel(tc, x_words, x_scales, e_words, e_scales, m
         wv_bytes = tile("wv_bytes", [P, N], U8)
         quant(wv_codes[:], wv_bytes[:], wv_bf[:])
         nc.vector.reciprocal(turned[:, 0, 0, :, 1], total[0][:, :PACK])
+        weight = [weigh_rows(0, "wv_bf")]
         for j in range(2):
             score(1, j, front.tile([P, 1], F32, name=f"neg_max1{j}", offset=RAW + 576 + 32 * j)[:])
         score(1, 2, front.tile([P, 1], F32, name="neg_max12", offset=H_AT[0] - 32)[:])
-        weight = [weigh_rows(0, "wv_bf")]
         score(1, 3, front.tile([P, 1], F32, name="neg_max13", offset=H_AT[0] - 64)[:])
         nc.vector.reciprocal(turned[:, 0, 1, :, 1], total[1][:])
 
@@ -195,8 +195,8 @@ def tile_picked_yslot_soft_po_kernel(tc, x_words, x_scales, e_words, e_scales, m
 
         h_on_vector(0, 0, h_product(0, 0, 0))
         h_on_vector(0, 1, h_product(0, 1, 1))
-        h_on_vector(1, 0, h_product(1, 0, 2))
         weight.append(weigh_rows(1))
+        h_on_vector(1, 0, h_product(1, 0, 2))
         planes0 = front.tile([P, PACK, HALF], BF16, name="planes0", offset=H_AT[0] - HALF * PACK * 2)
         scale_planes(planes0, 0, right)
         nc.gpsimd.tensor_scalar(
@@ -219,6 +219,7 @@ def tile_picked_yslot_soft_po_kernel(tc, x_words, x_scales, e_words, e_scales, m
         out_codes = tile("out_codes", [P, V], U32)
         out_bytes = tile("out_bytes", [P, V], U8)
         out_bf = tile("out_bf", [P, V * PACK], BF16)
+        out_words = out_1[0].rearrange("p n t -> p (n t)").bitcast(I32)
         out_rows = out_0.rearrange("(p j) v -> p j v", j=PACK)
 
         pieces = [(slice(0, HALF), (4, 5, 7, 2)), (slice(HALF, 3 * CHUNK), (1,)), (slice(3 * CHUNK, V), (6,))]
@@ -252,7 +253,7 @@ def tile_picked_yslot_soft_po_kernel(tc, x_words, x_scales, e_words, e_scales, m
 
         def hand_on(cols):
             quant(out_codes[:, cols], out_bytes[:, cols], woven(out_bf, cols))
-            nc.sync.dma_start(out_1[0].rearrange("p n t -> p (n t)").bitcast(I32)[:, cols], out_codes[:, cols].bitcast(I32))
+            nc.sync.dma_start(out_words[:, cols], out_codes[:, cols].bitcast(I32))
 
         quant_a(0, left)
         quant(h_codes[0][:], h_bytes[0][:], h_bf[0][:])
@@ -266,19 +267,23 @@ def tile_picked_yslot_soft_po_kernel(tc, x_words, x_scales, e_words, e_scales, m
         for rows in (slice(0, P), slice(P, HALF), right):
             quant(h_codes[1][:, rows], h_bytes[1][:, rows], woven(h_bf[1], rows))
         multiply(0, 1)
-        quant_a(1, right)
-        multiply(1, 1)
-        multiply(2, 1)
+        for i in (1, 2):
+            quant_a(1, pieces[i][0])
+            multiply(i, 1)
         for j in range(PACK):
-            copy_out(0, j, nc.scalar.copy)
+            copy_out(0, j, nc.scalar.copy if j < PACK - 1 else nc.vector.tensor_copy)
             store(0, slice(j, j + 1))
-        nc.vector.tensor_copy(woven(out_bf, pieces[1][0]).rearrange("p (n j) -> p n j", j=PACK), accs[1][0][:].rearrange("p j n -> p n j"))
-        for i in (2, 1):
+        for i in (1, 2):
             copy_out(i, 0, nc.scalar.copy)
             store(i, slice(0, PACK))
         weave(0, nc.vector.tensor_copy)
-        weave(2, nc.vector.tensor_copy)
+        weave(1, nc.vector.tensor_copy)
         hand_on(left)
-        hand_on(right)
+        weave(2, nc.vector.tensor_copy)
+        for i in (1, 2):
+            cols = pieces[i][0]
+            quant(out_codes[:, cols], out_bytes[:, cols], woven(out_bf, cols))
+        nc.sync.dma_start(out_words[:, right], out_codes[:, right].bitcast(I32))
         for q in range(QUADS):
-            nc.scalar.dma_start(out_2[0, 4 * q : 4 * q + 4, :].bitcast(I32), out_bytes[32 * q : 32 * q + 4, :].bitcast(I32))
+            queue = nc.sync if q == QUADS - 1 else nc.scalar
+            queue.dma_start(out_2[0, 4 * q : 4 * q + 4, :].bitcast(I32), out_bytes[32 * q : 32 * q + 4, :].bitcast(I32))

@@ -219,7 +219,6 @@ def tile_picked_yslot_soft_po_kernel(tc, x_words, x_scales, e_words, e_scales, m
         out_codes = tile("out_codes", [P, V], U32)
         out_bytes = tile("out_bytes", [P, V], U8)
         out_bf = tile("out_bf", [P, V * PACK], BF16)
-        out_words = out_1[0].rearrange("p n t -> p (n t)").bitcast(I32)
         out_rows = out_0.rearrange("(p j) v -> p j v", j=PACK)
 
         pieces = [(slice(0, HALF), (4, 5, 7, 2)), (slice(HALF, 3 * CHUNK), (1,)), (slice(3 * CHUNK, V), (6,))]
@@ -251,9 +250,9 @@ def tile_picked_yslot_soft_po_kernel(tc, x_words, x_scales, e_words, e_scales, m
         def weave(i, copy):
             copy(weave_out(woven(out_bf, pieces[i][0])), weave_in(out_f[i][:]))
 
-        def hand_on(cols):
+        def hand_on(i):
+            cols = pieces[i][0]
             quant(out_codes[:, cols], out_bytes[:, cols], woven(out_bf, cols))
-            nc.sync.dma_start(out_words[:, cols], out_codes[:, cols].bitcast(I32))
 
         quant_a(0, left)
         quant(h_codes[0][:], h_bytes[0][:], h_bf[0][:])
@@ -272,18 +271,18 @@ def tile_picked_yslot_soft_po_kernel(tc, x_words, x_scales, e_words, e_scales, m
             multiply(i, 1)
         for j in range(PACK):
             copy_out(0, j, nc.scalar.copy if j < PACK - 1 else nc.vector.tensor_copy)
-            store(0, slice(j, j + 1))
+            if j % 2 == 1:
+                store(0, slice(j - 1, j + 1))
         for i in (1, 2):
             copy_out(i, 0, nc.scalar.copy)
             store(i, slice(0, PACK))
         weave(0, nc.vector.tensor_copy)
         weave(1, nc.vector.tensor_copy)
-        hand_on(left)
+        hand_on(0)
         weave(2, nc.vector.tensor_copy)
-        for i in (1, 2):
-            cols = pieces[i][0]
-            quant(out_codes[:, cols], out_bytes[:, cols], woven(out_bf, cols))
-        nc.sync.dma_start(out_words[:, right], out_codes[:, right].bitcast(I32))
+        hand_on(1)
+        hand_on(2)
+        nc.sync.dma_start(out_1[0].rearrange("p n t -> p (n t)").bitcast(I32), out_codes[:].bitcast(I32))
         for q in range(QUADS):
             queue = nc.sync if q == QUADS - 1 else nc.scalar
             queue.dma_start(out_2[0, 4 * q : 4 * q + 4, :].bitcast(I32), out_bytes[32 * q : 32 * q + 4, :].bitcast(I32))

@@ -211,10 +211,13 @@ def tile_picked_yslot_soft_po_kernel(tc, x_words, x_scales, e_words, e_scales, m
         h_on_vector(1, 1, h_product(1, 1, 3))
         h_on_vector(0, 3, h_product(0, 3, 7))
         late_h = [h_product(1, 2, 0), h_product(1, 3, 3)]
+        spare = bank(7, [P, N], "spare")
+        for u in range(2):
+            product(spare[:], wv_codes[:, :P], wv_bytes[:, :P], wv_codes[:], wv_bytes[:])
 
-        h_codes = [tile("h_codes0", [P, N], U32, "wv_bytes"), tile("h_codes1", [P, N], U32)]
+        h_codes = [tile("h_codes0", [P, N], U32, "x_codes0"), tile("h_codes1", [P, N], U32)]
         h_bytes = [tile(f"h_bytes{g}", [P, N], U8) for g in range(PASSES)]
-        a_codes = [tile("a_codes0", [P, V], U32, "neg_max02"), tile("a_codes1", [P, V], U32)]
+        a_codes = [tile("a_codes0", [P, V], U32, "x_codes1"), tile("a_codes1", [P, V], U32)]
         a_bytes = [tile(f"a_bytes{g}", [P, V], U8) for g in range(PASSES)]
         out_codes = tile("out_codes", [P, V], U32)
         out_bytes = tile("out_bytes", [P, V], U8)

@@ -67,6 +67,9 @@ def tile_picked_yslot_soft_po_kernel(tc, x_words, x_scales, e_words, e_scales, m
         es = tile("es", [P, W], U8)
         placed = tile("placed", [P, S + V], U8)
         RAW = PACK * HALF * 4
+        FIRST = 192
+        wv_cols = [slice(0, FIRST), slice(FIRST, N)]
+        ROWS_AT = PACK * (N - FIRST) * 4
 
         nc.vector.memset(es[:ROW0, :].bitcast(I32), 0)
         nc.vector.memset(xs[:ROW0, :].bitcast(I32), 0)
@@ -83,7 +86,7 @@ def tile_picked_yslot_soft_po_kernel(tc, x_words, x_scales, e_words, e_scales, m
         total = [front.tile([P, 24], F32, name="total0", offset=H_AT[0] - 64), front.tile([P, PACK], F32, name="total1", offset=H_AT[1])]
 
         e_picked = front.tile([P, V], U8, name="e_picked", offset=10 * RAW, align_bytes=64)
-        x_picked = front.tile([P, S], U8, name="x_picked", offset=RAW - PASS + 128, align_bytes=64)
+        x_picked = front.tile([P, S], U8, name="x_picked", offset=ROWS_AT - 384, align_bytes=64)
         staged = tile("staged", [P, S + V], U8)
         nc.vector.tensor_copy(e_picked[:], es[:].indirect(slot_t[:]))
         nc.vector.tensor_copy(x_picked[:], xs[:].indirect(offs_t[:]))
@@ -99,15 +102,18 @@ def tile_picked_yslot_soft_po_kernel(tc, x_words, x_scales, e_words, e_scales, m
                 placed[32 * q : 32 * q + 4, :].bitcast(I32),
                 staged[ROW0 + 4 * q : ROW0 + 4 * q + 4, :].bitcast(I32),
             )
-        rows = front.tile([P, 2, PASSES * 32], F32, name="rows", offset=RAW, align_bytes=64)
+        rows = front.tile([P, 2, PASSES * 32], F32, name="rows", offset=ROWS_AT, align_bytes=64)
         nc.vector.memset(rows[:], 0.0)
+        wv_raw = [
+            front.tile([P, PACK, FIRST], F32, name="wv_raw0", offset=ROWS_AT + 576, align_bytes=64),
+            front.tile([P, PACK, N - FIRST], F32, name="wv_raw1", offset=0, align_bytes=64),
+        ]
+        for s in range(2):
+            nc.sync.dma_start(wv_raw[s][:], wv.rearrange("(p k) m -> p k m", k=PACK)[:, :, wv_cols[s]])
         for w, factor in enumerate((mask, inv)):
             nc.sync.dma_start(
                 rows[0:P:RUN, w, :].rearrange("u (b q) -> u b q", q=RUN), factor.rearrange("(b u q) o -> u b (q o)", u=P // RUN, q=RUN)
             )
-        wv_raw = [front.tile([P, PACK, HALF], F32, name=f"wv_raw{s}", offset=(1 - s) * (RAW + 576), align_bytes=64) for s in range(2)]
-        for s in range(2):
-            nc.sync.dma_start(wv_raw[s][:], wv.rearrange("(p k) m -> p k m", k=PACK)[:, :, s * HALF : (s + 1) * HALF])
         x_bytes = [placed[:, g * PASS : (g + 1) * PASS].rearrange("p (j n) -> p j n", j=PACK) for g in range(PASSES)]
         e_bytes = placed[:, S:]
 
@@ -120,18 +126,14 @@ def tile_picked_yslot_soft_po_kernel(tc, x_words, x_scales, e_words, e_scales, m
         e_codes = front.tile([P, V], U32, name="e_codes", offset=10 * RAW, align_bytes=64)
         nc.vector.tensor_copy(e_codes[:], ew[:].bitcast(U32).indirect(slot_t[:]))
         x_codes = [pick_words(g) for g in range(PASSES)]
-        turned = tile("turned", [P, 2, PASSES, PACK, RUN], F32, "xw")
-        nc.vector.transpose(turned[:].rearrange("p w g j e -> p (w g j e)"), rows[:].rearrange("p w c -> p (w c)"))
-        inv_t = front.tile([P, PASSES, PACK], F32, name="inv_t", offset=0)
 
         wv_bf = tile("wv_bf", [P, N * PACK], BF16)
-        nc.scalar.copy(weave_out(wv_bf[:, : HALF * PACK]), weave_in(wv_raw[0][:]))
+        nc.scalar.copy(weave_out(wv_bf[:, : FIRST * PACK]), weave_in(wv_raw[0][:]))
         nc.gpsimd.tensor_scalar(
-            wv_bf[:, HALF * PACK :].rearrange("p (n k) -> p n k", k=PACK),
+            wv_bf[:, FIRST * PACK :].rearrange("p (n k) -> p n k", k=PACK),
             wv_raw[1][:].rearrange("p k n -> p n k"), 1.0, 0.0, ALU.mult, ALU.add,
         )
-        nc.gpsimd.tensor_copy(inv_t[:], turned[:, 1, :, :, 0])
-        ex = [front.tile([P, PACK, V], F32, name=f"ex{g}", offset=(1 + 2 * g) * RAW + 704, align_bytes=64) for g in range(PASSES)]
+        ex = [front.tile([P, PACK, V], F32, name=f"ex{g}", offset=ROWS_AT + 704 + 2 * g * RAW, align_bytes=64) for g in range(PASSES)]
 
         def score(g, j, neg_max=None):
             if neg_max is None:
@@ -146,16 +148,19 @@ def tile_picked_yslot_soft_po_kernel(tc, x_words, x_scales, e_words, e_scales, m
             nc.vector.tensor_reduce(weight[:], turned[:, 0, g, :, :2], AX.X, ALU.mult)
             return weight
 
-        score(0, 0)
-        for j in range(1, PACK):
+        for j in range(PACK):
             score(0, j)
+        turned = tile("turned", [P, 2, PASSES, PACK, RUN], F32, "neg_max00")
+        nc.vector.transpose(turned[:].rearrange("p w g j e -> p (w g j e)"), rows[:].rearrange("p w c -> p (w c)"))
+        inv_t = front.tile([P, PASSES, PACK], F32, name="inv_t", offset=0)
+        nc.gpsimd.tensor_copy(inv_t[:], turned[:, 1, :, :, 0])
         wv_codes = tile("wv_codes", [P, N], U32, "neg_max02")
         wv_bytes = tile("wv_bytes", [P, N], U8)
         quant(wv_codes[:], wv_bytes[:], wv_bf[:])
         nc.vector.reciprocal(turned[:, 0, 0, :, 1], total[0][:, :PACK])
         weight = [weigh_rows(0, "wv_bf")]
         for j in range(2):
-            score(1, j, front.tile([P, 1], F32, name=f"neg_max1{j}", offset=RAW + 576 + 32 * j)[:])
+            score(1, j, front.tile([P, 1], F32, name=f"neg_max1{j}", offset=ROWS_AT + 576 + 32 * j)[:])
         score(1, 2, front.tile([P, 1], F32, name="neg_max12", offset=H_AT[0] - 32)[:])
         score(1, 3, front.tile([P, 1], F32, name="neg_max13", offset=H_AT[0] - 64)[:])
         nc.vector.reciprocal(turned[:, 0, 1, :, 1], total[1][:])
@@ -205,13 +210,13 @@ def tile_picked_yslot_soft_po_kernel(tc, x_words, x_scales, e_words, e_scales, m
         )
         planes1 = tile("planes1", [P, PACK, V], BF16)
         scale_planes(planes1, 1, slice(0, V))
-        for cols in (left, right):
+        for cols in (left, slice(HALF, 3 * CHUNK), slice(3 * CHUNK, V)):
             nc.scalar.copy(weave_out(woven(a_bf[1], cols)), weave_in(planes1[:, :, cols]))
         h_on_vector(0, 2, h_product(0, 2, 7))
         h_on_vector(1, 1, h_product(1, 1, 3))
-        h_on_vector(0, 3, h_product(0, 3, 7))
+        h_on_vector(0, 3, h_product(0, 3, 2))
         late_h = [h_product(1, 2, 0), h_product(1, 3, 3)]
-        spare = bank(7, [P, N], "spare")
+        spare = bank(2, [P, N], "spare")
         for u in range(2):
             product(spare[:], wv_codes[:, :P], wv_bytes[:, :P], wv_codes[:], wv_bytes[:])
 

@@ -161,6 +161,14 @@ def tile_picked_yslot_soft_po_kernel(tc, x_words, x_scales, e_words, e_scales, m
         weight = [weigh_rows(0, "wv_bf")]
         for j in range(2):
             score(1, j, front.tile([P, 1], F32, name=f"neg_max1{j}", offset=ROWS_AT + 576 + 32 * j)[:])
+        left, right = slice(0, HALF), slice(HALF, V)
+        planes0 = tile("planes0", [P, PACK, HALF], BF16)
+
+        def scale_planes(planes, g, cols, hands):
+            for j in hands:
+                nc.scalar.activation(planes[:, j, :], ex[g][:, j, cols], ACT.Copy, scale=weight[g][:, j : j + 1])
+
+        scale_planes(planes0, 0, right, (0, 1))
         score(1, 2, front.tile([P, 1], F32, name="neg_max12", offset=H_AT[0] - 32)[:])
         score(1, 3, front.tile([P, 1], F32, name="neg_max13", offset=H_AT[0] - 64)[:])
         nc.vector.reciprocal(turned[:, 0, 1, :, 1], total[1][:])
@@ -171,7 +179,6 @@ def tile_picked_yslot_soft_po_kernel(tc, x_words, x_scales, e_words, e_scales, m
         def woven(values, cols):
             return values[:, cols.start * PACK : cols.stop * PACK]
 
-        left, right = slice(0, HALF), slice(HALF, V)
         nc.gpsimd.tensor_tensor(
             woven(a_bf[0], left).rearrange("p (n j) -> p n j", j=PACK),
             ex[0][:, :, left].rearrange("p j n -> p n j"),
@@ -194,22 +201,17 @@ def tile_picked_yslot_soft_po_kernel(tc, x_words, x_scales, e_words, e_scales, m
                 ALU.mult,
             )
 
-        def scale_planes(planes, g, cols):
-            for j in range(PACK):
-                nc.scalar.activation(planes[:, j, :], ex[g][:, j, cols], ACT.Copy, scale=weight[g][:, j : j + 1])
-
         h_on_vector(0, 0, h_product(0, 0, 0))
         h_on_vector(0, 1, h_product(0, 1, 1))
         weight.append(weigh_rows(1))
         h_on_vector(1, 0, h_product(1, 0, 2))
-        planes0 = front.tile([P, PACK, HALF], BF16, name="planes0", offset=H_AT[0] - HALF * PACK * 2)
-        scale_planes(planes0, 0, right)
+        scale_planes(planes0, 0, right, (2, 3))
         nc.gpsimd.tensor_scalar(
             woven(a_bf[0], right).rearrange("p (n j) -> p n j", j=PACK),
             planes0[:].rearrange("p j n -> p n j"), 1.0, 0.0, ALU.mult, ALU.add,
         )
         planes1 = tile("planes1", [P, PACK, V], BF16)
-        scale_planes(planes1, 1, slice(0, V))
+        scale_planes(planes1, 1, slice(0, V), range(PACK))
         for cols in (left, slice(HALF, 3 * CHUNK), slice(3 * CHUNK, V)):
             nc.scalar.copy(weave_out(woven(a_bf[1], cols)), weave_in(planes1[:, :, cols]))
         h_on_vector(0, 2, h_product(0, 2, 7))
@@ -266,16 +268,15 @@ def tile_picked_yslot_soft_po_kernel(tc, x_words, x_scales, e_words, e_scales, m
         quant(h_codes[0][:], h_bytes[0][:], h_bf[0][:])
         multiply(0, 0)
         h_on_vector(1, 2, late_h[0])
-        quant_a(0, right)
-        multiply(1, 0)
-        multiply(2, 0)
         h_on_vector(1, 3, late_h[1])
         quant_a(1, left)
         for rows in (slice(0, P), slice(P, HALF), right):
             quant(h_codes[1][:, rows], h_bytes[1][:, rows], woven(h_bf[1], rows))
         multiply(0, 1)
+        quant_a(0, right)
         for i in (1, 2):
             quant_a(1, pieces[i][0])
+            multiply(i, 0)
             multiply(i, 1)
         for j in range(PACK):
             copy_out(0, j, nc.scalar.copy if j < PACK - 1 else nc.vector.tensor_copy)

@@ -71,6 +71,8 @@ def tile_picked_yslot_soft_po_kernel(tc, x_words, x_scales, e_words, e_scales, m
         wv_cols = [slice(0, FIRST), slice(FIRST, N)]
         ROWS_AT = PACK * (N - FIRST) * 4
 
+        rows = tile("rows", [P, 2, PASSES * 32], F32)
+        nc.vector.memset(rows[:], 0.0)
         nc.vector.memset(es[:ROW0, :].bitcast(I32), 0)
         nc.vector.memset(xs[:ROW0, :].bitcast(I32), 0)
         nc.vector.memset(placed[:].bitcast(I32), 0)
@@ -79,6 +81,10 @@ def tile_picked_yslot_soft_po_kernel(tc, x_words, x_scales, e_words, e_scales, m
         nc.sync.dma_start(offs_t[:], offs)
         nc.sync.dma_start(xs[ROW0:, :].bitcast(I32), x_scales[0].bitcast(I32))
         nc.sync.dma_start(ew[:], e_words[0].rearrange("p n t -> p (n t)").bitcast(I32))
+        for w, factor in enumerate((mask, inv)):
+            nc.sync.dma_start(
+                rows[0:P:RUN, w, :].rearrange("u (b q) -> u b q", q=RUN), factor.rearrange("(b u q) o -> u b (q o)", u=P // RUN, q=RUN)
+            )
         nc.sync.dma_start(xw[:], x_words[0].rearrange("p n t -> p (n t)").bitcast(I32))
 
         WOVEN = N * PACK * 2
@@ -102,18 +108,12 @@ def tile_picked_yslot_soft_po_kernel(tc, x_words, x_scales, e_words, e_scales, m
                 placed[32 * q : 32 * q + 4, :].bitcast(I32),
                 staged[ROW0 + 4 * q : ROW0 + 4 * q + 4, :].bitcast(I32),
             )
-        rows = front.tile([P, 2, PASSES * 32], F32, name="rows", offset=ROWS_AT, align_bytes=64)
-        nc.vector.memset(rows[:], 0.0)
         wv_raw = [
             front.tile([P, PACK, FIRST], F32, name="wv_raw0", offset=ROWS_AT + 576, align_bytes=64),
             front.tile([P, PACK, N - FIRST], F32, name="wv_raw1", offset=0, align_bytes=64),
         ]
         for s in range(2):
             nc.sync.dma_start(wv_raw[s][:], wv.rearrange("(p k) m -> p k m", k=PACK)[:, :, wv_cols[s]])
-        for w, factor in enumerate((mask, inv)):
-            nc.sync.dma_start(
-                rows[0:P:RUN, w, :].rearrange("u (b q) -> u b q", q=RUN), factor.rearrange("(b u q) o -> u b (q o)", u=P // RUN, q=RUN)
-            )
         x_bytes = [placed[:, g * PASS : (g + 1) * PASS].rearrange("p (j n) -> p j n", j=PACK) for g in range(PASSES)]
         e_bytes = placed[:, S:]
 
@@ -125,6 +125,8 @@ def tile_picked_yslot_soft_po_kernel(tc, x_words, x_scales, e_words, e_scales, m
 
         e_codes = front.tile([P, V], U32, name="e_codes", offset=10 * RAW, align_bytes=64)
         nc.vector.tensor_copy(e_codes[:], ew[:].bitcast(U32).indirect(slot_t[:]))
+        turned = front.tile([P, 2, PASSES, PACK, RUN], F32, name="turned", offset=ROWS_AT, align_bytes=64)
+        nc.vector.transpose(turned[:].rearrange("p w g j e -> p (w g j e)"), rows[:].rearrange("p w c -> p (w c)"))
         x_codes = [pick_words(g) for g in range(PASSES)]
 
         wv_bf = tile("wv_bf", [P, N * PACK], BF16)
@@ -143,22 +145,22 @@ def tile_picked_yslot_soft_po_kernel(tc, x_words, x_scales, e_words, e_scales, m
             nc.vector.tensor_reduce(neg_max, y[:], AX.X, ALU.max, negate=True)
             nc.scalar.activation(ex[g][:, j, :], y[:], ACT.Exp, bias=neg_max, accum_out=total[g][:, j : j + 1])
 
-        def weigh_rows(g, tag=None):
-            weight = tile(f"weight{g}", [P, PACK], F32, tag)
+        def weigh_rows(g):
+            weight = tile(f"weight{g}", [P, PACK], F32)
             nc.vector.tensor_reduce(weight[:], turned[:, 0, g, :, :2], AX.X, ALU.mult)
             return weight
 
         for j in range(PACK):
             score(0, j)
-        turned = tile("turned", [P, 2, PASSES, PACK, RUN], F32, "neg_max00")
-        nc.vector.transpose(turned[:].rearrange("p w g j e -> p (w g j e)"), rows[:].rearrange("p w c -> p (w c)"))
         inv_t = front.tile([P, PASSES, PACK], F32, name="inv_t", offset=0)
         nc.gpsimd.tensor_copy(inv_t[:], turned[:, 1, :, :, 0])
         wv_codes = tile("wv_codes", [P, N], U32, "neg_max02")
         wv_bytes = tile("wv_bytes", [P, N], U8)
         quant(wv_codes[:], wv_bytes[:], wv_bf[:])
-        nc.vector.reciprocal(turned[:, 0, 0, :, 1], total[0][:, :PACK])
-        weight = [weigh_rows(0, "wv_bf")]
+        share0 = tile("share0", [P, PACK], F32)
+        nc.vector.reciprocal(share0[:], total[0][:, :PACK])
+        weight = [tile("weight0", [P, PACK], F32)]
+        nc.gpsimd.tensor_tensor(weight[0][:], share0[:], turned[:, 0, 0, :, 0], ALU.mult)
         for j in range(2):
             score(1, j, front.tile([P, 1], F32, name=f"neg_max1{j}", offset=ROWS_AT + 576 + 32 * j)[:])
         left, right = slice(0, HALF), slice(HALF, V)
@@ -168,9 +170,10 @@ def tile_picked_yslot_soft_po_kernel(tc, x_words, x_scales, e_words, e_scales, m
             for j in hands:
                 nc.scalar.activation(planes[:, j, :], ex[g][:, j, cols], ACT.Copy, scale=weight[g][:, j : j + 1])
 
-        scale_planes(planes0, 0, right, (0, 1))
-        score(1, 2, front.tile([P, 1], F32, name="neg_max12", offset=H_AT[0] - 32)[:])
-        score(1, 3, front.tile([P, 1], F32, name="neg_max13", offset=H_AT[0] - 64)[:])
+        scale_planes(planes0, 0, right, (0,))
+        late_max = tile("late_max", [P, 2, RUN], F32, "neg_max03")
+        for j in (2, 3):
+            score(1, j, late_max[:, j - 2, :1])
         nc.vector.reciprocal(turned[:, 0, 1, :, 1], total[1][:])
 
         a_bf = [tile(f"a_bf{g}", [P, V * PACK], BF16) for g in range(PASSES)]
@@ -205,7 +208,7 @@ def tile_picked_yslot_soft_po_kernel(tc, x_words, x_scales, e_words, e_scales, m
         h_on_vector(0, 1, h_product(0, 1, 1))
         weight.append(weigh_rows(1))
         h_on_vector(1, 0, h_product(1, 0, 2))
-        scale_planes(planes0, 0, right, (2, 3))
+        scale_planes(planes0, 0, right, (1, 2, 3))
         nc.gpsimd.tensor_scalar(
             woven(a_bf[0], right).rearrange("p (n j) -> p n j", j=PACK),
             planes0[:].rearrange("p j n -> p n j"), 1.0, 0.0, ALU.mult, ALU.add,
@@ -288,10 +291,12 @@ def tile_picked_yslot_soft_po_kernel(tc, x_words, x_scales, e_words, e_scales, m
         weave(0, nc.vector.tensor_copy)
         weave(1, nc.vector.tensor_copy)
         hand_on(0)
+        out_words = out_1[0].rearrange("p n t -> p (n t)").bitcast(I32)
+        nc.sync.dma_start(out_words[:, left], out_codes[:, left].bitcast(I32))
         weave(2, nc.vector.tensor_copy)
         hand_on(1)
         hand_on(2)
-        nc.sync.dma_start(out_1[0].rearrange("p n t -> p (n t)").bitcast(I32), out_codes[:].bitcast(I32))
+        nc.sync.dma_start(out_words[:, right], out_codes[:, right].bitcast(I32))
         for q in range(QUADS):
             queue = nc.sync if q == QUADS - 1 else nc.scalar
             queue.dma_start(out_2[0, 4 * q : 4 * q + 4, :].bitcast(I32), out_bytes[32 * q : 32 * q + 4, :].bitcast(I32))

@@ -92,15 +92,19 @@ def tile_picked_yslot_soft_po_kernel(tc, x_words, x_scales, e_words, e_scales, m
         total = [front.tile([P, 24], F32, name="total0", offset=H_AT[0] - 64), front.tile([P, PACK], F32, name="total1", offset=H_AT[1])]
 
         e_picked = front.tile([P, V], U8, name="e_picked", offset=10 * RAW, align_bytes=64)
-        x_picked = front.tile([P, S], U8, name="x_picked", offset=ROWS_AT - 384, align_bytes=64)
+        x_picked = [
+            front.tile([P, PASS], U8, name="x_picked0", offset=10 * RAW + V, align_bytes=64),
+            front.tile([P, 2 * PASS], U8, name="x_picked1", offset=ROWS_AT - 384, align_bytes=64),
+        ]
         staged = tile("staged", [P, S + V], U8)
         nc.vector.tensor_copy(e_picked[:], es[:].indirect(slot_t[:]))
-        nc.vector.tensor_copy(x_picked[:], xs[:].indirect(offs_t[:]))
+        for g in range(PASSES):
+            nc.vector.tensor_copy(x_picked[g][:, :PASS], xs[:].indirect(offs_t[:, g * PASS // 16 : (g + 1) * PASS // 16]))
         for g in range(PASSES):
             cols = slice(g * PASS, (g + 1) * PASS)
             nc.vector.tensor_copy(
                 staged[:, cols].bitcast(I32).rearrange("p (j Q b q) -> p j Q b q", j=PACK, Q=QUADS, b=4),
-                x_picked[:, cols].bitcast(I32).rearrange("p (b Q j q) -> p j Q b q", j=PACK, Q=QUADS, b=4),
+                x_picked[g][:, :PASS].bitcast(I32).rearrange("p (b Q j q) -> p j Q b q", j=PACK, Q=QUADS, b=4),
             )
         nc.vector.tensor_copy(staged[:, S:].bitcast(I32), e_picked[:].bitcast(I32))
         for q in (0, 2, 1, 3):
@@ -123,9 +127,9 @@ def tile_picked_yslot_soft_po_kernel(tc, x_words, x_scales, e_words, e_scales, m
             nc.vector.tensor_copy(codes[:].rearrange("p j (Q b q) -> p b Q j q", Q=QUADS, q=RUN), xw[:].bitcast(U32).indirect(entries))
             return codes
 
-        e_codes = front.tile([P, V], U32, name="e_codes", offset=10 * RAW, align_bytes=64)
+        e_codes = front.tile([P, V], U32, name="e_codes", offset=10 * RAW + V + 64, align_bytes=64)
         nc.vector.tensor_copy(e_codes[:], ew[:].bitcast(U32).indirect(slot_t[:]))
-        turned = front.tile([P, 2, PASSES, PACK, RUN], F32, name="turned", offset=ROWS_AT, align_bytes=64)
+        turned = front.tile([P, 2, PASSES, PACK, RUN], F32, name="turned", offset=10 * RAW + 64, align_bytes=64)
         nc.vector.transpose(turned[:].rearrange("p w g j e -> p (w g j e)"), rows[:].rearrange("p w c -> p (w c)"))
         x_codes = [pick_words(g) for g in range(PASSES)]
 
@@ -267,10 +271,10 @@ def tile_picked_yslot_soft_po_kernel(tc, x_words, x_scales, e_words, e_scales, m
             cols = pieces[i][0]
             quant(out_codes[:, cols], out_bytes[:, cols], woven(out_bf, cols))
 
+        h_on_vector(1, 2, late_h[0])
         quant_a(0, left)
         quant(h_codes[0][:], h_bytes[0][:], h_bf[0][:])
         multiply(0, 0)
-        h_on_vector(1, 2, late_h[0])
         h_on_vector(1, 3, late_h[1])
         quant_a(1, left)
         for rows in (slice(0, P), slice(P, HALF), right):

@@ -24,6 +24,9 @@ QUADS = 4
 CHUNK = 128
 CHUNKS = V // CHUNK
 RUN = 8
+BANK = 2048
+BURST = 256
+PAIRS = 2
 ROW0 = P - 16
 
 
@@ -43,11 +46,11 @@ def tile_picked_yslot_soft_po_kernel(tc, x_words, x_scales, e_words, e_scales, m
         front = ctx.enter_context(tc.tile_pool(name="front", bufs=1))
         psum = ctx.enter_context(tc.psum_pool(name="psum", bufs=1))
 
-        def tile(name, shape, dtype, tag=None):
-            return sb.tile(shape, dtype, name=name, tag=tag or name, align_bytes=64)
+        def tile(name, shape, dtype, tag=None, align=64):
+            return sb.tile(shape, dtype, name=name, tag=tag or name, align_bytes=align)
 
         def bank(b, shape, name):
-            return psum.tile(shape, F32, name=name, tag=f"bank{b}")
+            return psum.tile(shape, F32, name=name, offset=BANK * b)
 
         def quant(codes, scales, values):
             nc.vector.quantize_mx(codes.bitcast(FP8X4), scales, values)
@@ -61,10 +64,10 @@ def tile_picked_yslot_soft_po_kernel(tc, x_words, x_scales, e_words, e_scales, m
         HALF = V // 2
         offs_t = lists.tile([P, S // 16], U16, name="offs_t")
         slot_t = lists.tile([P, V // 16], U16, name="slot_t")
-        xw = tile("xw", [P, T], I32)
-        ew = tile("ew", [P, W], I32)
-        xs = tile("xs", [P, T], U8)
-        es = tile("es", [P, W], U8)
+        xw = tile("xw", [P, T], I32, align=BURST)
+        ew = tile("ew", [P, W], I32, align=BURST)
+        xs = tile("xs", [P, T], U8, align=BURST)
+        es = tile("es", [P, W], U8, align=BURST)
         placed = tile("placed", [P, S + V], U8)
         RAW = PACK * HALF * 4
         FIRST = 192
@@ -87,9 +90,10 @@ def tile_picked_yslot_soft_po_kernel(tc, x_words, x_scales, e_words, e_scales, m
             )
         nc.sync.dma_start(xw[:], x_words[0].rearrange("p n t -> p (n t)").bitcast(I32))
 
-        WOVEN = N * PACK * 2
-        H_AT = [7 * RAW + g * (WOVEN + 192) for g in range(PASSES)]
-        total = [front.tile([P, 24], F32, name="total0", offset=H_AT[0] - 64), front.tile([P, PACK], F32, name="total1", offset=H_AT[1])]
+        WOVEN = HALF * PACK * 2
+        H_AT = {(0, 0): 6 * RAW, (1, 0): 7 * RAW, (0, 1): 7 * RAW + WOVEN, (1, 1): 8 * RAW}
+        total = [front.tile([P, 24], F32, name="total0", offset=H_AT[0, 0] - 64), front.tile([P, 16], F32, name="total1", offset=H_AT[0, 1] - 32)]
+        CODES_AT = 9 * RAW
 
         e_picked = front.tile([P, V], U8, name="e_picked", offset=10 * RAW, align_bytes=64)
         x_picked = [
@@ -113,16 +117,19 @@ def tile_picked_yslot_soft_po_kernel(tc, x_words, x_scales, e_words, e_scales, m
                 staged[ROW0 + 4 * q : ROW0 + 4 * q + 4, :].bitcast(I32),
             )
         wv_raw = [
-            front.tile([P, PACK, FIRST], F32, name="wv_raw0", offset=ROWS_AT + 576, align_bytes=64),
-            front.tile([P, PACK, N - FIRST], F32, name="wv_raw1", offset=0, align_bytes=64),
+            front.tile([P, PACK, FIRST], F32, name="wv_raw0", offset=ROWS_AT + 512, align_bytes=BURST),
+            front.tile([P, PACK, N - FIRST], F32, name="wv_raw1", offset=0, align_bytes=BURST),
         ]
         for s in range(2):
             nc.sync.dma_start(wv_raw[s][:], wv.rearrange("(p k) m -> p k m", k=PACK)[:, :, wv_cols[s]])
         x_bytes = [placed[:, g * PASS : (g + 1) * PASS].rearrange("p (j n) -> p j n", j=PACK) for g in range(PASSES)]
         e_bytes = placed[:, S:]
 
-        def pick_words(g, tag=None):
-            codes = tile(f"x_codes{g}", [P, PACK, P], U32, tag)
+        def pick_words(g):
+            if g == 0:
+                codes = tile("x_codes0", [P, PACK, P], U32)
+            else:
+                codes = front.tile([P, PACK, P], U32, name="x_codes1", offset=CODES_AT, align_bytes=64)
             entries = offs_t[:, g * PASS // 16 : (g + 1) * PASS // 16]
             nc.vector.tensor_copy(codes[:].rearrange("p j (Q b q) -> p b Q j q", Q=QUADS, q=RUN), xw[:].bitcast(U32).indirect(entries))
             return codes
@@ -134,10 +141,14 @@ def tile_picked_yslot_soft_po_kernel(tc, x_words, x_scales, e_words, e_scales, m
         x_codes = [pick_words(g) for g in range(PASSES)]
 
         wv_bf = tile("wv_bf", [P, N * PACK], BF16)
-        nc.scalar.copy(weave_out(wv_bf[:, : FIRST * PACK]), weave_in(wv_raw[0][:]))
+        dealt = wv_bf[:].rearrange("p (h m l k) -> p m h l k", h=PAIRS, l=2, k=PACK)
+        nc.scalar.copy(
+            dealt[:, : FIRST // PACK].rearrange("p m h l k -> p m h k l"),
+            wv_raw[0][:].rearrange("p k (m h l) -> p m h k l", h=PAIRS, l=2),
+        )
         nc.gpsimd.tensor_scalar(
-            wv_bf[:, FIRST * PACK :].rearrange("p (n k) -> p n k", k=PACK),
-            wv_raw[1][:].rearrange("p k n -> p n k"), 1.0, 0.0, ALU.mult, ALU.add,
+            dealt[:, FIRST // PACK :],
+            wv_raw[1][:].rearrange("p k (m h l) -> p m h l k", h=PAIRS, l=2), 1.0, 0.0, ALU.mult, ALU.add,
         )
         ex = [front.tile([P, PACK, V], F32, name=f"ex{g}", offset=ROWS_AT + 704 + 2 * g * RAW, align_bytes=64) for g in range(PASSES)]
 
@@ -178,10 +189,10 @@ def tile_picked_yslot_soft_po_kernel(tc, x_words, x_scales, e_words, e_scales, m
         late_max = tile("late_max", [P, 2, RUN], F32, "neg_max03")
         for j in (2, 3):
             score(1, j, late_max[:, j - 2, :1])
-        nc.vector.reciprocal(turned[:, 0, 1, :, 1], total[1][:])
+        nc.vector.reciprocal(turned[:, 0, 1, :, 1], total[1][:, :PACK])
 
         a_bf = [tile(f"a_bf{g}", [P, V * PACK], BF16) for g in range(PASSES)]
-        h_bf = [front.tile([P, N * PACK], BF16, name=f"h_bf{g}", offset=H_AT[g], align_bytes=64) for g in range(PASSES)]
+        h_bf = {at: front.tile([P, HALF * PACK], BF16, name=f"h_bf{at[0]}{at[1]}", offset=H_AT[at], align_bytes=64) for at in H_AT}
 
         def woven(values, cols):
             return values[:, cols.start * PACK : cols.stop * PACK]
@@ -193,25 +204,28 @@ def tile_picked_yslot_soft_po_kernel(tc, x_words, x_scales, e_words, e_scales, m
             ALU.mult,
         )
 
-        def h_product(g, c, b):
-            hb = bank(b, [P, PACK, CHUNK], f"h{g}{c}")
-            cols = slice(c * CHUNK, (c + 1) * CHUNK)
+        def h_product(g, u, w):
+            hb = bank(2 * g + w, [P, PACK, CHUNK], f"h{g}{u}{w}")
+            cols = slice(u * HALF + w * CHUNK, u * HALF + (w + 1) * CHUNK)
             for t in range(PACK):
                 product(hb[:, t, :], x_codes[g][:, t, :], x_bytes[g][:, t, :], wv_codes[:, cols], wv_bytes[:, cols])
             return hb
 
-        def h_on_vector(g, c, hb):
+        def h_on_vector(g, u, w, hb):
             nc.vector.tensor_tensor(
-                h_bf[g][:].rearrange("p (j c m t) -> p c j m t", j=PACK, c=CHUNKS, t=PACK)[:, c],
-                hb[:].rearrange("p t (m j) -> p j m t", j=PACK),
-                inv_t[:, g, :].unsqueeze(1).unsqueeze(1).to_broadcast([P, PACK, CHUNK // PACK, PACK]),
+                h_bf[g, u][:].rearrange("p (l w m t) -> p w m l t", l=2, w=2, t=PACK)[:, w],
+                hb[:].rearrange("p t (m l) -> p m l t", l=2),
+                inv_t[:, g, :].unsqueeze(1).unsqueeze(1).to_broadcast([P, CHUNK // 2, 2, PACK]),
                 ALU.mult,
             )
 
-        h_on_vector(0, 0, h_product(0, 0, 0))
-        h_on_vector(0, 1, h_product(0, 1, 1))
+        def make_h(g, u):
+            for w in range(2):
+                h_on_vector(g, u, w, h_product(g, u, w))
+
+        make_h(0, 0)
         weight.append(weigh_rows(1))
-        h_on_vector(1, 0, h_product(1, 0, 2))
+        make_h(1, 0)
         scale_planes(planes0, 0, right, (1, 2, 3))
         nc.gpsimd.tensor_scalar(
             woven(a_bf[0], right).rearrange("p (n j) -> p n j", j=PACK),
@@ -221,33 +235,33 @@ def tile_picked_yslot_soft_po_kernel(tc, x_words, x_scales, e_words, e_scales, m
         scale_planes(planes1, 1, slice(0, V), range(PACK))
         for cols in (left, slice(HALF, 3 * CHUNK), slice(3 * CHUNK, V)):
             nc.scalar.copy(weave_out(woven(a_bf[1], cols)), weave_in(planes1[:, :, cols]))
-        h_on_vector(0, 2, h_product(0, 2, 7))
-        h_on_vector(1, 1, h_product(1, 1, 3))
-        h_on_vector(0, 3, h_product(0, 3, 2))
-        late_h = [h_product(1, 2, 0), h_product(1, 3, 3)]
-        spare = bank(2, [P, N], "spare")
+        make_h(0, 1)
+        late_h = [h_product(1, 1, w) for w in range(2)]
+        h_on_vector(1, 1, 0, late_h[0])
+        spare = bank(1, [P, N], "spare")
         for u in range(2):
             product(spare[:], wv_codes[:, :P], wv_bytes[:, :P], wv_codes[:], wv_bytes[:])
+        h_on_vector(1, 1, 1, late_h[1])
 
-        h_codes = [tile("h_codes0", [P, N], U32, "x_codes0"), tile("h_codes1", [P, N], U32)]
+        h_codes = [front.tile([P, N], U32, name="h_codes0", offset=CODES_AT - 1024, align_bytes=64), tile("h_codes1", [P, N], U32)]
         h_bytes = [tile(f"h_bytes{g}", [P, N], U8) for g in range(PASSES)]
-        a_codes = [tile("a_codes0", [P, V], U32, "x_codes1"), tile("a_codes1", [P, V], U32)]
+        a_codes = [front.tile([P, V], U32, name="a_codes0", offset=CODES_AT + 1024, align_bytes=64), tile("a_codes1", [P, V], U32)]
         a_bytes = [tile(f"a_bytes{g}", [P, V], U8) for g in range(PASSES)]
-        out_codes = tile("out_codes", [P, V], U32)
+        out_codes = tile("out_codes", [P, V], U32, align=BURST)
         out_bytes = tile("out_bytes", [P, V], U8)
         out_bf = tile("out_bf", [P, V * PACK], BF16)
         out_rows = out_0.rearrange("(p j) v -> p j v", j=PACK)
 
-        pieces = [(slice(0, HALF), (4, 5, 7, 2)), (slice(HALF, 3 * CHUNK), (1,)), (slice(3 * CHUNK, V), (6,))]
+        pieces = [(slice(0, HALF), (4, 5, 6, 7)), (slice(HALF, 3 * CHUNK), (0,)), (slice(3 * CHUNK, V), (1,))]
         accs = [
             [bank(b, [P, PACK // len(banks), cols.stop - cols.start], f"acc{b}") for b in banks] for cols, banks in pieces
         ]
-        out_f = [tile(f"out_f{i}", [P, PACK, cols.stop - cols.start], F32) for i, (cols, banks) in enumerate(pieces)]
+        out_f = [tile(f"out_f{i}", [P, PACK, cols.stop - cols.start], F32, align=BURST) for i, (cols, banks) in enumerate(pieces)]
 
-        def multiply(i, g):
+        def multiply(i, g, hands=range(PACK)):
             cols, banks = pieces[i]
             share = PACK // len(banks)
-            for j in range(PACK):
+            for j in hands:
                 rows = slice(j * P, (j + 1) * P)
                 product(
                     accs[i][j // share][:, j % share, :], h_codes[g][:, rows], h_bytes[g][:, rows], a_codes[g][:, cols], a_bytes[g][:, cols],
@@ -271,15 +285,20 @@ def tile_picked_yslot_soft_po_kernel(tc, x_words, x_scales, e_words, e_scales, m
             cols = pieces[i][0]
             quant(out_codes[:, cols], out_bytes[:, cols], woven(out_bf, cols))
 
-        h_on_vector(1, 2, late_h[0])
+        def quant_h(g, u):
+            rows = slice(u * HALF, (u + 1) * HALF)
+            quant(h_codes[g][:, rows], h_bytes[g][:, rows], h_bf[g, u][:])
+
+        quant_h(0, 0)
         quant_a(0, left)
-        quant(h_codes[0][:], h_bytes[0][:], h_bf[0][:])
-        multiply(0, 0)
-        h_on_vector(1, 3, late_h[1])
+        multiply(0, 0, (0, 1))
+        quant_h(1, 0)
         quant_a(1, left)
-        for rows in (slice(0, P), slice(P, HALF), right):
-            quant(h_codes[1][:, rows], h_bytes[1][:, rows], woven(h_bf[1], rows))
-        multiply(0, 1)
+        multiply(0, 1, (0, 1))
+        quant_h(0, 1)
+        multiply(0, 0, (2, 3))
+        quant_h(1, 1)
+        multiply(0, 1, (2, 3))
         quant_a(0, right)
         for i in (1, 2):
             quant_a(1, pieces[i][0])

@@ -152,11 +152,16 @@ def tile_picked_yslot_soft_po_kernel(tc, x_words, x_scales, e_words, e_scales, m
         )
         ex = [front.tile([P, PACK, V], F32, name=f"ex{g}", offset=ROWS_AT + 704 + 2 * g * RAW, align_bytes=64) for g in range(PASSES)]
 
-        def score(g, j, neg_max=None):
-            if neg_max is None:
-                neg_max = tile(f"neg_max{g}{j}", [P, 1], F32)[:]
+        def scores(g, j):
             y = bank(PACK * g + j, [P, V], f"y{g}{j}")
             product(y[:], x_codes[g][:, j, :], x_bytes[g][:, j, :], e_codes[:], e_bytes)
+            return y
+
+        def score(g, j, neg_max=None, y=None):
+            if neg_max is None:
+                neg_max = tile(f"neg_max{g}{j}", [P, 1], F32)[:]
+            if y is None:
+                y = scores(g, j)
             nc.vector.tensor_reduce(neg_max, y[:], AX.X, ALU.max, negate=True)
             nc.scalar.activation(ex[g][:, j, :], y[:], ACT.Exp, bias=neg_max, accum_out=total[g][:, j : j + 1])
 
@@ -187,8 +192,9 @@ def tile_picked_yslot_soft_po_kernel(tc, x_words, x_scales, e_words, e_scales, m
 
         scale_planes(planes0, 0, right, (0,))
         late_max = tile("late_max", [P, 2, RUN], F32, "neg_max03")
+        late_y = {j: scores(1, j) for j in (3, 2)}
         for j in (2, 3):
-            score(1, j, late_max[:, j - 2, :1])
+            score(1, j, late_max[:, j - 2, :1], late_y[j])
         nc.vector.reciprocal(turned[:, 0, 1, :, 1], total[1][:, :PACK])
 
         a_bf = [tile(f"a_bf{g}", [P, V * PACK], BF16) for g in range(PASSES)]
@@ -205,7 +211,7 @@ def tile_picked_yslot_soft_po_kernel(tc, x_words, x_scales, e_words, e_scales, m
         )
 
         def h_product(g, u, w):
-            hb = bank(2 * g + w, [P, PACK, CHUNK], f"h{g}{u}{w}")
+            hb = bank(2 * g + (w + u) % 2, [P, PACK, CHUNK], f"h{g}{u}{w}")
             cols = slice(u * HALF + w * CHUNK, u * HALF + (w + 1) * CHUNK)
             for t in range(PACK):
                 product(hb[:, t, :], x_codes[g][:, t, :], x_bytes[g][:, t, :], wv_codes[:, cols], wv_bytes[:, cols])
@@ -220,8 +226,9 @@ def tile_picked_yslot_soft_po_kernel(tc, x_words, x_scales, e_words, e_scales, m
             )
 
         def make_h(g, u):
+            made = {w: h_product(g, u, w) for w in (1, 0)}
             for w in range(2):
-                h_on_vector(g, u, w, h_product(g, u, w))
+                h_on_vector(g, u, w, made[w])
 
         make_h(0, 0)
         weight.append(weigh_rows(1))
@@ -236,9 +243,9 @@ def tile_picked_yslot_soft_po_kernel(tc, x_words, x_scales, e_words, e_scales, m
         for cols in (left, slice(HALF, 3 * CHUNK), slice(3 * CHUNK, V)):
             nc.scalar.copy(weave_out(woven(a_bf[1], cols)), weave_in(planes1[:, :, cols]))
         make_h(0, 1)
-        late_h = [h_product(1, 1, w) for w in range(2)]
+        late_h = {w: h_product(1, 1, w) for w in (1, 0)}
         h_on_vector(1, 1, 0, late_h[0])
-        spare = bank(1, [P, N], "spare")
+        spare = bank(0, [P, N], "spare")
         for u in range(2):
             product(spare[:], wv_codes[:, :P], wv_bytes[:, :P], wv_codes[:], wv_bytes[:])
         h_on_vector(1, 1, 1, late_h[1])
@@ -252,7 +259,7 @@ def tile_picked_yslot_soft_po_kernel(tc, x_words, x_scales, e_words, e_scales, m
         out_bf = tile("out_bf", [P, V * PACK], BF16)
         out_rows = out_0.rearrange("(p j) v -> p j v", j=PACK)
 
-        pieces = [(slice(0, HALF), (4, 5, 6, 7)), (slice(HALF, 3 * CHUNK), (0,)), (slice(3 * CHUNK, V), (1,))]
+        pieces = [(slice(0, HALF), (4, 5, 6, 7)), (slice(HALF, 3 * CHUNK), (1,)), (slice(3 * CHUNK, V), (0,))]
         accs = [
             [bank(b, [P, PACK // len(banks), cols.stop - cols.start], f"acc{b}") for b in banks] for cols, banks in pieces
         ]
@@ -289,14 +296,13 @@ def tile_picked_yslot_soft_po_kernel(tc, x_words, x_scales, e_words, e_scales, m
             rows = slice(u * HALF, (u + 1) * HALF)
             quant(h_codes[g][:, rows], h_bytes[g][:, rows], h_bf[g, u][:])
 
+        quant_h(0, 1)
         quant_h(0, 0)
         quant_a(0, left)
-        multiply(0, 0, (0, 1))
+        multiply(0, 0)
         quant_h(1, 0)
         quant_a(1, left)
         multiply(0, 1, (0, 1))
-        quant_h(0, 1)
-        multiply(0, 0, (2, 3))
         quant_h(1, 1)
         multiply(0, 1, (2, 3))
         quant_a(0, right)

@@ -30,12 +30,12 @@ PAIRS = 2
 ROW0 = P - 16
 
 
-def weave_out(tile_ap):
-    return tile_ap.rearrange("p (c i j) -> p c j i", i=2, j=PACK)
+def weave_out(tile_ap, run=2):
+    return tile_ap.rearrange("p (c i j) -> p c j i", i=run, j=PACK)
 
 
-def weave_in(planes_ap):
-    return planes_ap.rearrange("p j (c i) -> p c j i", i=2)
+def weave_in(planes_ap, run=2):
+    return planes_ap.rearrange("p j (c i) -> p c j i", i=run)
 
 
 def tile_picked_yslot_soft_po_kernel(tc, x_words, x_scales, e_words, e_scales, mask, wv, inv, offs, slot, out_0, out_1, out_2):
@@ -184,29 +184,31 @@ def tile_picked_yslot_soft_po_kernel(tc, x_words, x_scales, e_words, e_scales, m
         for j in range(2):
             score(1, j, front.tile([P, 1], F32, name=f"neg_max1{j}", offset=ROWS_AT + 576 + 32 * j)[:])
         left, right = slice(0, HALF), slice(HALF, V)
-        planes0 = tile("planes0", [P, PACK, HALF], BF16)
+        WEIGHED = 3 * CHUNK
+        weighed, scaled = slice(0, WEIGHED), slice(WEIGHED, V)
+        planes0 = tile("planes0", [P, PACK, V - WEIGHED], BF16)
 
         def scale_planes(planes, g, cols, hands):
             for j in hands:
                 nc.scalar.activation(planes[:, j, :], ex[g][:, j, cols], ACT.Copy, scale=weight[g][:, j : j + 1])
 
-        scale_planes(planes0, 0, right, (0,))
+        scale_planes(planes0, 0, scaled, (0, 1))
         late_max = tile("late_max", [P, 2, RUN], F32, "neg_max03")
         late_y = {j: scores(1, j) for j in (3, 2)}
         for j in (2, 3):
             score(1, j, late_max[:, j - 2, :1], late_y[j])
         nc.vector.reciprocal(turned[:, 0, 1, :, 1], total[1][:, :PACK])
 
-        a_bf = [tile(f"a_bf{g}", [P, V * PACK], BF16) for g in range(PASSES)]
+        a_bf = [tile("a_bf0", [P, V * PACK], BF16), tile("a_bf1", [P, 3 * CHUNK * PACK], BF16)]
         h_bf = {at: front.tile([P, HALF * PACK], BF16, name=f"h_bf{at[0]}{at[1]}", offset=H_AT[at], align_bytes=64) for at in H_AT}
 
         def woven(values, cols):
             return values[:, cols.start * PACK : cols.stop * PACK]
 
         nc.gpsimd.tensor_tensor(
-            woven(a_bf[0], left).rearrange("p (n j) -> p n j", j=PACK),
-            ex[0][:, :, left].rearrange("p j n -> p n j"),
-            weight[0][:].unsqueeze(1).to_broadcast([P, HALF, PACK]),
+            woven(a_bf[0], weighed).rearrange("p (n j) -> p n j", j=PACK),
+            ex[0][:, :, weighed].rearrange("p j n -> p n j"),
+            weight[0][:].unsqueeze(1).to_broadcast([P, WEIGHED, PACK]),
             ALU.mult,
         )
 
@@ -233,15 +235,15 @@ def tile_picked_yslot_soft_po_kernel(tc, x_words, x_scales, e_words, e_scales, m
         make_h(0, 0)
         weight.append(weigh_rows(1))
         make_h(1, 0)
-        scale_planes(planes0, 0, right, (1, 2, 3))
+        scale_planes(planes0, 0, scaled, (2, 3))
         nc.gpsimd.tensor_scalar(
-            woven(a_bf[0], right).rearrange("p (n j) -> p n j", j=PACK),
+            woven(a_bf[0], scaled).rearrange("p (n j) -> p n j", j=PACK),
             planes0[:].rearrange("p j n -> p n j"), 1.0, 0.0, ALU.mult, ALU.add,
         )
         planes1 = tile("planes1", [P, PACK, V], BF16)
         scale_planes(planes1, 1, slice(0, V), range(PACK))
-        for cols in (left, slice(HALF, 3 * CHUNK), slice(3 * CHUNK, V)):
-            nc.scalar.copy(weave_out(woven(a_bf[1], cols)), weave_in(planes1[:, :, cols]))
+        for cols in (left, slice(HALF, 3 * CHUNK)):
+            nc.scalar.copy(weave_out(woven(a_bf[1], cols), 4), weave_in(planes1[:, :, cols], 4))
         make_h(0, 1)
         late_h = {w: h_product(1, 1, w) for w in (1, 0)}
         h_on_vector(1, 1, 0, late_h[0])
@@ -296,22 +298,30 @@ def tile_picked_yslot_soft_po_kernel(tc, x_words, x_scales, e_words, e_scales, m
             rows = slice(u * HALF, (u + 1) * HALF)
             quant(h_codes[g][:, rows], h_bytes[g][:, rows], h_bf[g, u][:])
 
-        quant_h(0, 1)
         quant_h(0, 0)
         quant_a(0, left)
-        multiply(0, 0)
+        multiply(0, 0, (0, 1))
         quant_h(1, 0)
         quant_a(1, left)
         multiply(0, 1, (0, 1))
-        quant_h(1, 1)
-        multiply(0, 1, (2, 3))
+        quant_h(0, 1)
+        multiply(0, 0, (2, 3))
+        for j in (2, 3):
+            rows = slice(j * P, (j + 1) * P)
+            quant(h_codes[1][:, rows], h_bytes[1][:, rows], h_bf[1, 1][:, (j - 2) * PASS : (j - 1) * PASS])
+            multiply(0, 1, (j,))
         quant_a(0, right)
-        for i in (1, 2):
-            quant_a(1, pieces[i][0])
-            multiply(i, 0)
-            multiply(i, 1)
+        quant_a(1, pieces[1][0])
+        multiply(1, 0)
+        multiply(1, 1)
+        last = pieces[2][0]
+        a_last = front.tile([P, CHUNK * PACK], BF16, name="a_last", offset=H_AT[1, 1], align_bytes=64)
+        nc.vector.tensor_copy(weave_out(a_last[:], 4), weave_in(planes1[:, :, last], 4))
+        quant(a_codes[1][:, last], a_bytes[1][:, last], a_last[:])
+        multiply(2, 0)
+        multiply(2, 1)
         for j in range(PACK):
-            copy_out(0, j, nc.scalar.copy if j < PACK - 1 else nc.vector.tensor_copy)
+            copy_out(0, j, nc.scalar.copy)
             if j % 2 == 1:
                 store(0, slice(j - 1, j + 1))
         for i in (1, 2):
@@ -322,7 +332,7 @@ def tile_picked_yslot_soft_po_kernel(tc, x_words, x_scales, e_words, e_scales, m
         hand_on(0)
         out_words = out_1[0].rearrange("p n t -> p (n t)").bitcast(I32)
         nc.sync.dma_start(out_words[:, left], out_codes[:, left].bitcast(I32))
-        weave(2, nc.vector.tensor_copy)
+        nc.scalar.copy(woven(out_bf, last).rearrange("p (n j) -> p n j", j=PACK), accs[2][0][:].rearrange("p j n -> p n j"))
         hand_on(1)
         hand_on(2)
         nc.sync.dma_start(out_words[:, right], out_codes[:, right].bitcast(I32))

@@ -194,9 +194,8 @@ def tile_picked_yslot_soft_po_kernel(tc, x_words, x_scales, e_words, e_scales, m
 
         scale_planes(planes0, 0, scaled, (0, 1))
         late_max = tile("late_max", [P, 2, RUN], F32, "neg_max03")
-        late_y = {j: scores(1, j) for j in (3, 2)}
         for j in (2, 3):
-            score(1, j, late_max[:, j - 2, :1], late_y[j])
+            score(1, j, late_max[:, j - 2, :1])
         nc.vector.reciprocal(turned[:, 0, 1, :, 1], total[1][:, :PACK])
 
         a_bf = [tile("a_bf0", [P, V * PACK], BF16), tile("a_bf1", [P, 3 * CHUNK * PACK], BF16)]
@@ -213,7 +212,7 @@ def tile_picked_yslot_soft_po_kernel(tc, x_words, x_scales, e_words, e_scales, m
         )
 
         def h_product(g, u, w):
-            hb = bank(2 * g + (w + u) % 2, [P, PACK, CHUNK], f"h{g}{u}{w}")
+            hb = bank(2 * g + w, [P, PACK, CHUNK], f"h{g}{u}{w}")
             cols = slice(u * HALF + w * CHUNK, u * HALF + (w + 1) * CHUNK)
             for t in range(PACK):
                 product(hb[:, t, :], x_codes[g][:, t, :], x_bytes[g][:, t, :], wv_codes[:, cols], wv_bytes[:, cols])
@@ -228,9 +227,8 @@ def tile_picked_yslot_soft_po_kernel(tc, x_words, x_scales, e_words, e_scales, m
             )
 
         def make_h(g, u):
-            made = {w: h_product(g, u, w) for w in (1, 0)}
             for w in range(2):
-                h_on_vector(g, u, w, made[w])
+                h_on_vector(g, u, w, h_product(g, u, w))
 
         make_h(0, 0)
         weight.append(weigh_rows(1))
@@ -245,12 +243,11 @@ def tile_picked_yslot_soft_po_kernel(tc, x_words, x_scales, e_words, e_scales, m
         for cols in (left, slice(HALF, 3 * CHUNK)):
             nc.scalar.copy(weave_out(woven(a_bf[1], cols), 4), weave_in(planes1[:, :, cols], 4))
         make_h(0, 1)
-        late_h = {w: h_product(1, 1, w) for w in (1, 0)}
-        h_on_vector(1, 1, 0, late_h[0])
-        spare = bank(0, [P, N], "spare")
-        for u in range(2):
+        for w in range(2):
+            h_on_vector(1, 1, w, h_product(1, 1, w))
+        for w in range(2):
+            spare = bank(2 + w, [P, N], f"spare{w}")
             product(spare[:], wv_codes[:, :P], wv_bytes[:, :P], wv_codes[:], wv_bytes[:])
-        h_on_vector(1, 1, 1, late_h[1])
 
         h_codes = [front.tile([P, N], U32, name="h_codes0", offset=CODES_AT - 1024, align_bytes=64), tile("h_codes1", [P, N], U32)]
         h_bytes = [tile(f"h_bytes{g}", [P, N], U8) for g in range(PASSES)]

@@ -184,7 +184,7 @@ def tile_picked_yslot_soft_po_kernel(tc, x_words, x_scales, e_words, e_scales, m
         for j in range(2):
             score(1, j, front.tile([P, 1], F32, name=f"neg_max1{j}", offset=ROWS_AT + 576 + 32 * j)[:])
         left, right = slice(0, HALF), slice(HALF, V)
-        WEIGHED = 3 * CHUNK
+        WEIGHED = HALF
         weighed, scaled = slice(0, WEIGHED), slice(WEIGHED, V)
         planes0 = tile("planes0", [P, PACK, V - WEIGHED], BF16)
 
@@ -192,7 +192,7 @@ def tile_picked_yslot_soft_po_kernel(tc, x_words, x_scales, e_words, e_scales, m
             for j in hands:
                 nc.scalar.activation(planes[:, j, :], ex[g][:, j, cols], ACT.Copy, scale=weight[g][:, j : j + 1])
 
-        scale_planes(planes0, 0, scaled, (0, 1))
+        scale_planes(planes0, 0, scaled, (0,))
         late_max = tile("late_max", [P, 2, RUN], F32, "neg_max03")
         for j in (2, 3):
             score(1, j, late_max[:, j - 2, :1])
@@ -233,7 +233,7 @@ def tile_picked_yslot_soft_po_kernel(tc, x_words, x_scales, e_words, e_scales, m
         make_h(0, 0)
         weight.append(weigh_rows(1))
         make_h(1, 0)
-        scale_planes(planes0, 0, scaled, (2, 3))
+        scale_planes(planes0, 0, scaled, (1, 2, 3))
         nc.gpsimd.tensor_scalar(
             woven(a_bf[0], scaled).rearrange("p (n j) -> p n j", j=PACK),
             planes0[:].rearrange("p j n -> p n j"), 1.0, 0.0, ALU.mult, ALU.add,

@@ -245,9 +245,6 @@ def tile_picked_yslot_soft_po_kernel(tc, x_words, x_scales, e_words, e_scales, m
         make_h(0, 1)
         for w in range(2):
             h_on_vector(1, 1, w, h_product(1, 1, w))
-        for w in range(2):
-            spare = bank(2 + w, [P, N], f"spare{w}")
-            product(spare[:], wv_codes[:, :P], wv_bytes[:, :P], wv_codes[:], wv_bytes[:])
 
         h_codes = [front.tile([P, N], U32, name="h_codes0", offset=CODES_AT - 1024, align_bytes=64), tile("h_codes1", [P, N], U32)]
         h_bytes = [tile(f"h_bytes{g}", [P, N], U8) for g in range(PASSES)]

@@ -212,7 +212,7 @@ def tile_picked_yslot_soft_po_kernel(tc, x_words, x_scales, e_words, e_scales, m
         )
 
         def h_product(g, u, w):
-            hb = bank(2 * g + w, [P, PACK, CHUNK], f"h{g}{u}{w}")
+            hb = bank(1 + w if u else 2 * g + w, [P, PACK, CHUNK], f"h{g}{u}{w}")
             cols = slice(u * HALF + w * CHUNK, u * HALF + (w + 1) * CHUNK)
             for t in range(PACK):
                 product(hb[:, t, :], x_codes[g][:, t, :], x_bytes[g][:, t, :], wv_codes[:, cols], wv_bytes[:, cols])
@@ -243,8 +243,8 @@ def tile_picked_yslot_soft_po_kernel(tc, x_words, x_scales, e_words, e_scales, m
         for cols in (left, slice(HALF, 3 * CHUNK)):
             nc.scalar.copy(weave_out(woven(a_bf[1], cols), 4), weave_in(planes1[:, :, cols], 4))
         make_h(0, 1)
-        for w in range(2):
-            h_on_vector(1, 1, w, h_product(1, 1, w))
+        h_on_vector(1, 1, 0, h_product(1, 1, 0))
+        late_h = h_product(1, 1, 1)
 
         h_codes = [front.tile([P, N], U32, name="h_codes0", offset=CODES_AT - 1024, align_bytes=64), tile("h_codes1", [P, N], U32)]
         h_bytes = [tile(f"h_bytes{g}", [P, N], U8) for g in range(PASSES)]
@@ -255,7 +255,7 @@ def tile_picked_yslot_soft_po_kernel(tc, x_words, x_scales, e_words, e_scales, m
         out_bf = tile("out_bf", [P, V * PACK], BF16)
         out_rows = out_0.rearrange("(p j) v -> p j v", j=PACK)
 
-        pieces = [(slice(0, HALF), (4, 5, 6, 7)), (slice(HALF, 3 * CHUNK), (1,)), (slice(3 * CHUNK, V), (0,))]
+        pieces = [(slice(0, HALF), (4, 5, 6, 7)), (slice(HALF, 3 * CHUNK), (0,)), (slice(3 * CHUNK, V), (3,))]
         accs = [
             [bank(b, [P, PACK // len(banks), cols.stop - cols.start], f"acc{b}") for b in banks] for cols, banks in pieces
         ]
@@ -295,18 +295,19 @@ def tile_picked_yslot_soft_po_kernel(tc, x_words, x_scales, e_words, e_scales, m
         quant_h(0, 0)
         quant_a(0, left)
         multiply(0, 0, (0, 1))
+        quant_h(0, 1)
+        multiply(0, 0, (2, 3))
         quant_h(1, 0)
         quant_a(1, left)
         multiply(0, 1, (0, 1))
-        quant_h(0, 1)
-        multiply(0, 0, (2, 3))
+        h_on_vector(1, 1, 1, late_h)
+        quant_a(0, right)
+        multiply(1, 0)
         for j in (2, 3):
             rows = slice(j * P, (j + 1) * P)
             quant(h_codes[1][:, rows], h_bytes[1][:, rows], h_bf[1, 1][:, (j - 2) * PASS : (j - 1) * PASS])
             multiply(0, 1, (j,))
-        quant_a(0, right)
         quant_a(1, pieces[1][0])
-        multiply(1, 0)
         multiply(1, 1)
         last = pieces[2][0]
         a_last = front.tile([P, CHUNK * PACK], BF16, name="a_last", offset=H_AT[1, 1], align_bytes=64)

@@ -212,7 +212,7 @@ def tile_picked_yslot_soft_po_kernel(tc, x_words, x_scales, e_words, e_scales, m
         )
 
         def h_product(g, u, w):
-            hb = bank(1 + w if u else 2 * g + w, [P, PACK, CHUNK], f"h{g}{u}{w}")
+            hb = bank(1 + w if u else (2 * g + w) % 3, [P, PACK, CHUNK], f"h{g}{u}{w}")
             cols = slice(u * HALF + w * CHUNK, u * HALF + (w + 1) * CHUNK)
             for t in range(PACK):
                 product(hb[:, t, :], x_codes[g][:, t, :], x_bytes[g][:, t, :], wv_codes[:, cols], wv_bytes[:, cols])
@@ -233,6 +233,12 @@ def tile_picked_yslot_soft_po_kernel(tc, x_words, x_scales, e_words, e_scales, m
         make_h(0, 0)
         weight.append(weigh_rows(1))
         make_h(1, 0)
+
+        def warm_up(b):
+            spare = bank(b, [P, N], f"spare{b}")
+            product(spare[:], wv_codes[:, :P], wv_bytes[:, :P], wv_codes[:], wv_bytes[:])
+
+        warm_up(0)
         scale_planes(planes0, 0, scaled, (1, 2, 3))
         nc.gpsimd.tensor_scalar(
             woven(a_bf[0], scaled).rearrange("p (n j) -> p n j", j=PACK),
@@ -245,6 +251,7 @@ def tile_picked_yslot_soft_po_kernel(tc, x_words, x_scales, e_words, e_scales, m
         make_h(0, 1)
         h_on_vector(1, 1, 0, h_product(1, 1, 0))
         late_h = h_product(1, 1, 1)
+        warm_up(1)
 
         h_codes = [front.tile([P, N], U32, name="h_codes0", offset=CODES_AT - 1024, align_bytes=64), tile("h_codes1", [P, N], U32)]
         h_bytes = [tile(f"h_bytes{g}", [P, N], U8) for g in range(PASSES)]
@@ -255,7 +262,7 @@ def tile_picked_yslot_soft_po_kernel(tc, x_words, x_scales, e_words, e_scales, m
         out_bf = tile("out_bf", [P, V * PACK], BF16)
         out_rows = out_0.rearrange("(p j) v -> p j v", j=PACK)
 
-        pieces = [(slice(0, HALF), (4, 5, 6, 7)), (slice(HALF, 3 * CHUNK), (0,)), (slice(3 * CHUNK, V), (3,))]
+        pieces = [(slice(0, HALF), (4, 5, 6, 7)), (slice(HALF, 3 * CHUNK), (3,)), (slice(3 * CHUNK, V), (0,))]
         accs = [
             [bank(b, [P, PACK // len(banks), cols.stop - cols.start], f"acc{b}") for b in banks] for cols, banks in pieces
         ]

from contextlib import ExitStack

import concourse.mybir as mybir

K, T, S, N, V, W = 512, 4096, 1024, 512, 512, 1024
FLOPS = 2 * (S * K * N + S * K * V + S * N * V)

F32 = mybir.dt.float32
BF16 = mybir.dt.bfloat16
I32 = mybir.dt.int32
U32 = mybir.dt.uint32
U16 = mybir.dt.uint16
U8 = mybir.dt.uint8
FP8X4 = mybir.dt.float8_e4m3fn_x4
ACT = mybir.ActivationFunctionType
ALU = mybir.AluOpType
AX = mybir.AxisListType

P = 128
PACK = 4
PASS = P * PACK
PASSES = S // PASS
QUADS = 4
CHUNK = 128
CHUNKS = V // CHUNK
RUN = 8
BANK = 2048
BURST = 256
PAIRS = 2
ROW0 = P - 16


def weave_out(tile_ap, run=2):
    return tile_ap.rearrange("p (c i j) -> p c j i", i=run, j=PACK)


def weave_in(planes_ap, run=2):
    return planes_ap.rearrange("p j (c i) -> p c j i", i=run)


def tile_picked_yslot_soft_po_kernel(tc, x_words, x_scales, e_words, e_scales, mask, wv, inv, offs, slot, out_0, out_1, out_2):
    nc = tc.nc
    with ExitStack() as ctx:
        lists = ctx.enter_context(tc.tile_pool(name="lists", bufs=1))
        sb = ctx.enter_context(tc.tile_pool(name="sb", bufs=1))
        front = ctx.enter_context(tc.tile_pool(name="front", bufs=1))
        psum = ctx.enter_context(tc.psum_pool(name="psum", bufs=1))

        def tile(name, shape, dtype, tag=None, align=64):
            return sb.tile(shape, dtype, name=name, tag=tag or name, align_bytes=align)

        def bank(b, shape, name):
            return psum.tile(shape, F32, name=name, offset=BANK * b)

        def quant(codes, scales, values):
            nc.vector.quantize_mx(codes.bitcast(FP8X4), scales, values)

        def product(out, left, left_bytes, right, right_bytes, start=True, stop=True):
            nc.tensor.matmul_mx(
                out=out, lhsT=left.bitcast(FP8X4), lhsT_scale=left_bytes,
                rhs=right.bitcast(FP8X4), rhs_scale=right_bytes, start=start, stop=stop,
            )

        HALF = V // 2
        offs_t = lists.tile([P, S // 16], U16, name="offs_t")
        slot_t = lists.tile([P, V // 16], U16, name="slot_t")
        xw = tile("xw", [P, T], I32, align=BURST)
        ew = tile("ew", [P, W], I32, align=BURST)
        xs = tile("xs", [P, T], U8, align=BURST)
        es = tile("es", [P, W], U8, align=BURST)
        placed = tile("placed", [P, S + V], U8)
        RAW = PACK * HALF * 4
        FIRST = 192
        wv_cols = [slice(0, FIRST), slice(FIRST, N)]
        ROWS_AT = PACK * (N - FIRST) * 4

        rows = tile("rows", [P, 2, PASSES * 32], F32)
        nc.vector.memset(rows[:], 0.0)
        nc.vector.memset(es[:ROW0, :].bitcast(I32), 0)
        nc.vector.memset(xs[:ROW0, :].bitcast(I32), 0)
        nc.vector.memset(placed[:].bitcast(I32), 0)
        nc.sync.dma_start(slot_t[:], slot)
        nc.sync.dma_start(es[ROW0:, :].bitcast(I32), e_scales[0].bitcast(I32))
        nc.sync.dma_start(offs_t[:], offs)
        nc.sync.dma_start(xs[ROW0:, :].bitcast(I32), x_scales[0].bitcast(I32))
        nc.sync.dma_start(ew[:], e_words[0].rearrange("p n t -> p (n t)").bitcast(I32))
        for w, factor in enumerate((mask, inv)):
            nc.sync.dma_start(
                rows[0:P:RUN, w, :].rearrange("u (b q) -> u b q", q=RUN), factor.rearrange("(b u q) o -> u b (q o)", u=P // RUN, q=RUN)
            )
        nc.sync.dma_start(xw[:], x_words[0].rearrange("p n t -> p (n t)").bitcast(I32))

        WOVEN = HALF * PACK * 2
        H_AT = {(0, 0): 6 * RAW, (1, 0): 7 * RAW, (0, 1): 7 * RAW + WOVEN, (1, 1): 8 * RAW}
        total = [front.tile([P, 24], F32, name="total0", offset=H_AT[0, 0] - 64), front.tile([P, 16], F32, name="total1", offset=H_AT[0, 1] - 32)]
        CODES_AT = 9 * RAW

        e_picked = front.tile([P, V], U8, name="e_picked", offset=10 * RAW, align_bytes=64)
        x_picked = [
            front.tile([P, PASS], U8, name="x_picked0", offset=10 * RAW + V, align_bytes=64),
            front.tile([P, 2 * PASS], U8, name="x_picked1", offset=ROWS_AT - 384, align_bytes=64),
        ]
        staged = tile("staged", [P, S + V], U8)
        nc.vector.tensor_copy(e_picked[:], es[:].indirect(slot_t[:]))
        for g in range(PASSES):
            nc.vector.tensor_copy(x_picked[g][:, :PASS], xs[:].indirect(offs_t[:, g * PASS // 16 : (g + 1) * PASS // 16]))
        for g in range(PASSES):
            cols = slice(g * PASS, (g + 1) * PASS)
            nc.vector.tensor_copy(
                staged[:, cols].bitcast(I32).rearrange("p (j Q b q) -> p j Q b q", j=PACK, Q=QUADS, b=4),
                x_picked[g][:, :PASS].bitcast(I32).rearrange("p (b Q j q) -> p j Q b q", j=PACK, Q=QUADS, b=4),
            )
        nc.vector.tensor_copy(staged[:, S:].bitcast(I32), e_picked[:].bitcast(I32))
        for q in (0, 2, 1, 3):
            nc.sync.dma_start(
                placed[32 * q : 32 * q + 4, :].bitcast(I32),
                staged[ROW0 + 4 * q : ROW0 + 4 * q + 4, :].bitcast(I32),
            )
        wv_raw = [
            front.tile([P, PACK, FIRST], F32, name="wv_raw0", offset=ROWS_AT + 512, align_bytes=BURST),
            front.tile([P, PACK, N - FIRST], F32, name="wv_raw1", offset=0, align_bytes=BURST),
        ]
        for s in range(2):
            nc.sync.dma_start(wv_raw[s][:], wv.rearrange("(p k) m -> p k m", k=PACK)[:, :, wv_cols[s]])
        x_bytes = [placed[:, g * PASS : (g + 1) * PASS].rearrange("p (j n) -> p j n", j=PACK) for g in range(PASSES)]
        e_bytes = placed[:, S:]

        def pick_words(g):
            if g == 0:
                codes = tile("x_codes0", [P, PACK, P], U32)
            else:
                codes = front.tile([P, PACK, P], U32, name="x_codes1", offset=CODES_AT, align_bytes=64)
            entries = offs_t[:, g * PASS // 16 : (g + 1) * PASS // 16]
            nc.vector.tensor_copy(codes[:].rearrange("p j (Q b q) -> p b Q j q", Q=QUADS, q=RUN), xw[:].bitcast(U32).indirect(entries))
            return codes

        e_codes = front.tile([P, V], U32, name="e_codes", offset=10 * RAW + V + 64, align_bytes=64)
        nc.vector.tensor_copy(e_codes[:], ew[:].bitcast(U32).indirect(slot_t[:]))
        turned = front.tile([P, 2, PASSES, PACK, RUN], F32, name="turned", offset=10 * RAW + 64, align_bytes=64)
        nc.vector.transpose(turned[:].rearrange("p w g j e -> p (w g j e)"), rows[:].rearrange("p w c -> p (w c)"))
        x_codes = [pick_words(g) for g in range(PASSES)]

        wv_bf = tile("wv_bf", [P, N * PACK], BF16)
        dealt = wv_bf[:].rearrange("p (h m l k) -> p m h l k", h=PAIRS, l=2, k=PACK)
        nc.scalar.copy(
            dealt[:, : FIRST // PACK].rearrange("p m h l k -> p m h k l"),
            wv_raw[0][:].rearrange("p k (m h l) -> p m h k l", h=PAIRS, l=2),
        )
        nc.gpsimd.tensor_scalar(
            dealt[:, FIRST // PACK :],
            wv_raw[1][:].rearrange("p k (m h l) -> p m h l k", h=PAIRS, l=2), 1.0, 0.0, ALU.mult, ALU.add,
        )
        ex = [front.tile([P, PACK, V], F32, name=f"ex{g}", offset=ROWS_AT + 704 + 2 * g * RAW, align_bytes=64) for g in range(PASSES)]

        def scores(g, j):
            y = bank(PACK * g + j, [P, V], f"y{g}{j}")
            product(y[:], x_codes[g][:, j, :], x_bytes[g][:, j, :], e_codes[:], e_bytes)
            return y

        def score(g, j, neg_max=None, y=None):
            if neg_max is None:
                neg_max = tile(f"neg_max{g}{j}", [P, 1], F32)[:]
            if y is None:
                y = scores(g, j)
            nc.vector.tensor_reduce(neg_max, y[:], AX.X, ALU.max, negate=True)
            nc.scalar.activation(ex[g][:, j, :], y[:], ACT.Exp, bias=neg_max, accum_out=total[g][:, j : j + 1])

        def weigh_rows(g):
            weight = tile(f"weight{g}", [P, PACK], F32)
            nc.vector.tensor_reduce(weight[:], turned[:, 0, g, :, :2], AX.X, ALU.mult)
            return weight

        for j in range(PACK):
            score(0, j)
        inv_t = front.tile([P, PASSES, PACK], F32, name="inv_t", offset=0)
        nc.gpsimd.tensor_copy(inv_t[:], turned[:, 1, :, :, 0])
        wv_codes = tile("wv_codes", [P, N], U32, "neg_max02")
        wv_bytes = tile("wv_bytes", [P, N], U8)
        quant(wv_codes[:], wv_bytes[:], wv_bf[:])
        share0 = tile("share0", [P, PACK], F32)
        nc.vector.reciprocal(share0[:], total[0][:, :PACK])
        weight = [tile("weight0", [P, PACK], F32)]
        nc.gpsimd.tensor_tensor(weight[0][:], share0[:], turned[:, 0, 0, :, 0], ALU.mult)
        for j in range(2):
            score(1, j, front.tile([P, 1], F32, name=f"neg_max1{j}", offset=ROWS_AT + 576 + 32 * j)[:])
        left, right = slice(0, HALF), slice(HALF, V)
        WEIGHED = HALF
        weighed, scaled = slice(0, WEIGHED), slice(WEIGHED, V)
        planes0 = tile("planes0", [P, PACK, V - WEIGHED], BF16)

        def scale_planes(planes, g, cols, hands):
            for j in hands:
                nc.scalar.activation(planes[:, j, :], ex[g][:, j, cols], ACT.Copy, scale=weight[g][:, j : j + 1])

        scale_planes(planes0, 0, scaled, (0,))
        late_max = tile("late_max", [P, 2, RUN], F32, "neg_max03")
        for j in (2, 3):
            score(1, j, late_max[:, j - 2, :1])
        nc.vector.reciprocal(turned[:, 0, 1, :, 1], total[1][:, :PACK])

        a_bf = [tile("a_bf0", [P, V * PACK], BF16), tile("a_bf1", [P, 3 * CHUNK * PACK], BF16)]
        h_bf = {at: front.tile([P, HALF * PACK], BF16, name=f"h_bf{at[0]}{at[1]}", offset=H_AT[at], align_bytes=64) for at in H_AT}

        def woven(values, cols):
            return values[:, cols.start * PACK : cols.stop * PACK]

        nc.gpsimd.tensor_tensor(
            woven(a_bf[0], weighed).rearrange("p (n j) -> p n j", j=PACK),
            ex[0][:, :, weighed].rearrange("p j n -> p n j"),
            weight[0][:].unsqueeze(1).to_broadcast([P, WEIGHED, PACK]),
            ALU.mult,
        )

        def h_product(g, u, w):
            hb = bank(1 + w if u else (2 * g + w) % 3, [P, PACK, CHUNK], f"h{g}{u}{w}")
            cols = slice(u * HALF + w * CHUNK, u * HALF + (w + 1) * CHUNK)
            for t in range(PACK):
                product(hb[:, t, :], x_codes[g][:, t, :], x_bytes[g][:, t, :], wv_codes[:, cols], wv_bytes[:, cols])
            return hb

        def h_on_vector(g, u, w, hb):
            nc.vector.tensor_tensor(
                h_bf[g, u][:].rearrange("p (l w m t) -> p w m l t", l=2, w=2, t=PACK)[:, w],
                hb[:].rearrange("p t (m l) -> p m l t", l=2),
                inv_t[:, g, :].unsqueeze(1).unsqueeze(1).to_broadcast([P, CHUNK // 2, 2, PACK]),
                ALU.mult,
            )

        def make_h(g, u):
            for w in range(2):
                h_on_vector(g, u, w, h_product(g, u, w))

        make_h(0, 0)
        weight.append(weigh_rows(1))
        make_h(1, 0)

        def warm_up(b):
            spare = bank(b, [P, N], f"spare{b}")
            product(spare[:], wv_codes[:, :P], wv_bytes[:, :P], wv_codes[:], wv_bytes[:])

        warm_up(0)
        scale_planes(planes0, 0, scaled, (1, 2, 3))
        nc.gpsimd.tensor_scalar(
            woven(a_bf[0], scaled).rearrange("p (n j) -> p n j", j=PACK),
            planes0[:].rearrange("p j n -> p n j"), 1.0, 0.0, ALU.mult, ALU.add,
        )
        planes1 = tile("planes1", [P, PACK, V], BF16)
        scale_planes(planes1, 1, slice(0, V), range(PACK))
        for cols in (left, slice(HALF, 3 * CHUNK)):
            nc.scalar.copy(weave_out(woven(a_bf[1], cols), 4), weave_in(planes1[:, :, cols], 4))
        make_h(0, 1)
        h_on_vector(1, 1, 0, h_product(1, 1, 0))
        late_h = h_product(1, 1, 1)
        warm_up(1)

        h_codes = [front.tile([P, N], U32, name="h_codes0", offset=CODES_AT - 1024, align_bytes=64), tile("h_codes1", [P, N], U32)]
        h_bytes = [tile(f"h_bytes{g}", [P, N], U8) for g in range(PASSES)]
        a_codes = [front.tile([P, V], U32, name="a_codes0", offset=CODES_AT + 1024, align_bytes=64), tile("a_codes1", [P, V], U32)]
        a_bytes = [tile(f"a_bytes{g}", [P, V], U8) for g in range(PASSES)]
        out_codes = tile("out_codes", [P, V], U32, align=BURST)
        out_bytes = tile("out_bytes", [P, V], U8)
        out_bf = tile("out_bf", [P, V * PACK], BF16)
        out_rows = out_0.rearrange("(p j) v -> p j v", j=PACK)

        pieces = [(slice(0, HALF), (4, 5, 6, 7)), (slice(HALF, 3 * CHUNK), (3,)), (slice(3 * CHUNK, V), (0,))]
        accs = [
            [bank(b, [P, PACK // len(banks), cols.stop - cols.start], f"acc{b}") for b in banks] for cols, banks in pieces
        ]
        out_f = [tile(f"out_f{i}", [P, PACK, cols.stop - cols.start], F32, align=BURST) for i, (cols, banks) in enumerate(pieces)]

        def multiply(i, g, hands=range(PACK)):
            cols, banks = pieces[i]
            share = PACK // len(banks)
            for j in hands:
                rows = slice(j * P, (j + 1) * P)
                product(
                    accs[i][j // share][:, j % share, :], h_codes[g][:, rows], h_bytes[g][:, rows], a_codes[g][:, cols], a_bytes[g][:, cols],
                    start=(g == 0 and j % share == 0), stop=(g == PASSES - 1 and j % share == share - 1),
                )

        def quant_a(g, cols):
            quant(a_codes[g][:, cols], a_bytes[g][:, cols], woven(a_bf[g], cols))

        def copy_out(i, u, copy):
            share = PACK // len(pieces[i][1])
            copy(out_f[i][:, u * share : (u + 1) * share, :], accs[i][u][:])

        def store(i, hands):
            nc.sync.dma_start(out_rows[:, hands, pieces[i][0]], out_f[i][:, hands, :])

        def weave(i, copy):
            copy(weave_out(woven(out_bf, pieces[i][0])), weave_in(out_f[i][:]))

        def hand_on(i):
            cols = pieces[i][0]
            quant(out_codes[:, cols], out_bytes[:, cols], woven(out_bf, cols))

        def quant_h(g, u):
            rows = slice(u * HALF, (u + 1) * HALF)
            quant(h_codes[g][:, rows], h_bytes[g][:, rows], h_bf[g, u][:])

        quant_h(0, 0)
        quant_a(0, left)
        multiply(0, 0, (0, 1))
        quant_h(0, 1)
        multiply(0, 0, (2, 3))
        quant_h(1, 0)
        quant_a(1, left)
        multiply(0, 1, (0, 1))
        h_on_vector(1, 1, 1, late_h)
        quant_a(0, right)
        multiply(1, 0)
        for j in (2, 3):
            rows = slice(j * P, (j + 1) * P)
            quant(h_codes[1][:, rows], h_bytes[1][:, rows], h_bf[1, 1][:, (j - 2) * PASS : (j - 1) * PASS])
            multiply(0, 1, (j,))
        quant_a(1, pieces[1][0])
        multiply(1, 1)
        last = pieces[2][0]
        a_last = front.tile([P, CHUNK * PACK], BF16, name="a_last", offset=H_AT[1, 1], align_bytes=64)
        nc.vector.tensor_copy(weave_out(a_last[:], 4), weave_in(planes1[:, :, last], 4))
        quant(a_codes[1][:, last], a_bytes[1][:, last], a_last[:])
        multiply(2, 0)
        multiply(2, 1)
        for j in range(PACK):
            copy_out(0, j, nc.scalar.copy)
            if j % 2 == 1:
                store(0, slice(j - 1, j + 1))
        for i in (1, 2):
            copy_out(i, 0, nc.scalar.copy)
            store(i, slice(0, PACK))
        weave(0, nc.vector.tensor_copy)
        weave(1, nc.vector.tensor_copy)
        hand_on(0)
        out_words = out_1[0].rearrange("p n t -> p (n t)").bitcast(I32)
        nc.sync.dma_start(out_words[:, left], out_codes[:, left].bitcast(I32))
        nc.scalar.copy(woven(out_bf, last).rearrange("p (n j) -> p n j", j=PACK), accs[2][0][:].rearrange("p j n -> p n j"))
        hand_on(1)
        hand_on(2)
        nc.sync.dma_start(out_words[:, right], out_codes[:, right].bitcast(I32))
        for q in range(QUADS):
            queue = nc.sync if q == QUADS - 1 else nc.scalar
            queue.dma_start(out_2[0, 4 * q : 4 * q + 4, :].bitcast(I32), out_bytes[32 * q : 32 * q + 4, :].bitcast(I32))
